import numpy as np, ml_dtypes
CORES = [9,25,41,57]
N = 4
import mx_ref
BF = ml_dtypes.bfloat16
def gentries(a):
    return np.ascontiguousarray(a.reshape(8, 16, -1).transpose(0, 2, 1)).reshape(8, -1)
def gtable(e):
    e = np.asarray(e); return np.ascontiguousarray(e.reshape(8, -1, 16).transpose(0, 2, 1)).reshape(128, -1).astype(np.int32)
def gcols(t, e):
    v = np.concatenate([t.reshape(8, 16, -1, 4), np.zeros((8, 16, 1, 4), BF)], axis=2)
    return np.ascontiguousarray(np.stack([v[g][:, e[g]] for g in range(8)])).reshape(128, -1)
def tile(rs):
    return np.stack(rs, axis=2).reshape(128, -1).astype(BF)
def pick(q, e):
    c = np.concatenate([q[0].reshape(128, -1, 4), np.zeros((128, 1, 4), np.uint8)], axis=1); s = np.concatenate([q[1], np.ones((16, 1), np.uint8)], axis=1)
    return (np.ascontiguousarray(c[:, e].reshape(128, -1)), np.ascontiguousarray(s[:, e]))
def join(*qs):
    return (np.concatenate([q[0] for q in qs], axis=1), np.concatenate([q[1] for q in qs], axis=1))
def put(q, e, v):
    c, s = q[0].reshape(128, -1, 4).copy(), q[1].copy(); c[:, e] = v[0].reshape(128, -1, 4); s[:, e] = v[1]
    return (c.reshape(128, -1), s)
def pk(c, s):
    return (np.ascontiguousarray(c), mx_ref.live(s))
def emit(q):
    return q[0], q[1]
def packed(v, rng):
    q = [mx_ref.quantize(np.ascontiguousarray(v[r])) for r in range(N)]
    return np.stack([a for a, b in q]), np.stack([mx_ref.plane(b, rng) for a, b in q])
def values_of_codes():
    e, c = np.zeros((128, 128, 4), np.float32), np.zeros((128, 2, 4), np.uint8)
    e[np.arange(128), np.arange(128), 0] = 1
    c[:127, :, 0] = np.arange(256).reshape(2, 128).T[:127]
    return mx_ref.matmul(mx_ref.quantize(e.reshape(128, 512).astype(BF)), (c.reshape(128, 8), np.full((16, 2), 127, np.uint8))).T.reshape(-1).astype(np.float64)
CODE_VALUE, SCALE_VALUE = values_of_codes(), 2.0 ** (np.arange(256) - 127.0)
def decode(q):
    return (CODE_VALUE[q[0]].reshape(16, 8, -1, 4) * SCALE_VALUE[q[1]][:, None, :, None] + 0.0).reshape(128, -1).astype(np.float32)
def f(rng, *shape):
    return mx_ref.flush((rng.standard_normal(shape, dtype=np.float32) * np.exp2(rng.integers(-2, 3, shape[:-1] + (1,)))).astype(BF))
def wide(rng, *shape, cols=0):
    v = rng.standard_normal(shape, dtype=np.float32) * np.exp2(rng.integers(-12, 13, shape)).astype(np.float32)
    if cols: v *= np.repeat(np.exp2(rng.integers(-cols, cols + 1, shape[:-2] + (1, shape[-1] // 4))) * (rng.random(shape[:-2] + (1, shape[-1] // 4)) > 0.0625), 4, axis=-1).astype(np.float32)
    return mx_ref.flush(v.astype(BF))
L, R = 192, 2
STEP = [1, 2]
def contract(a, b, turn):
    turn = turn & (b >= 0)
    a, b = np.where(turn, b, a), np.where(turn, a, b)
    go, o = [int(a[L - 1])], []
    while go:
        n = go.pop()
        if n < L: o.append(n)
        else: go += [int(b[n - L]), int(a[n - L])]
    leaf = np.array(o)[1::2]
    up = np.zeros(2 * L, np.int64)
    up[b] = L + np.arange(L)
    up[a] = L + np.arange(L)
    parent = up[leaf]
    left = a[parent - L] == leaf
    add = np.full((2, 2 * L), -1)
    for i, now in enumerate((left, ~left)):
        l, p = leaf[now], parent[now]
        s = a[p - L] + b[p - L] - l
        add[i, s] = np.flatnonzero(now)
        top = up[p]
        w = a[top - L] == p
        a[top[w] - L] = s[w]
        b[top[~w] - L] = s[~w]
        up[s] = top
        a[p - L] = -1
        b[p - L] = -1
    return a, b, leaf, parent, add
def numbers_of(rng):
    return {"x": np.array(f(rng, N, 128, 8 * L)), "u": np.array(f(rng, N, 128, 512)), "v": np.array(f(rng, N, 128, 512))}
def weights(rng, w):
    c, p = packed(w, rng)
    return {"wc": c, "ws": p}
def trees(rng, kind, q=None):
    e = np.full((2, N, 8, L), -1)
    for r in range(N):
        for g in range(8):
            pool, k = rng.permutation(L).tolist(), int(kind[r, g])
            w, c = rng.random(L), rng.integers(0, 2, L)
            for i, n in enumerate(rng.permutation(L - 1).tolist()):
                j = int(w[i] * (len(pool) - 1)) if k == 0 or k == 5 and i >= L // 2 else i // 2 * 2 + 1 if k == 5 else 0
                two = pool[j:j + 2]
                if k == 4 or k == 1 and c[i] or k == 5 and q[r, g, L + n] > 0: two = two[::-1]
                pool[j:j + 2] = []
                pool.insert(len(pool) if k == 2 else j, L + n)
                e[:, r, g, n] = two
            e[0, r, g, L - 1] = pool[0]
    return {"ka": np.stack([gtable(a) for a in e[0]]), "kb": np.stack([gtable(a) for a in e[1]])}
def planted(rng, kind, q, size, unit):
    d = numbers_of(rng)
    x = d["x"].astype(np.float32).reshape(N, 8, 16, 2 * L, 4)
    x[:, :, :8] = 0
    x[:, :, 0, :, 0] = (10 - q) * 0.125 * size
    x[:, :, 1, :, 0] = (9 - q) * 0.125 * size
    u = d["u"].reshape(N, 128, 128, 4)
    u[:, :, ::16] = 0
    for h in range(0, 128, 16):
        u[:, h, h, 0] = (1.125 * unit).astype(np.float32).astype(BF)
        u[:, h + 1, h, 0] = (-1.25 * unit).astype(np.float32).astype(BF)
    w = np.array(f(rng, N, 128, 2048)).reshape(N, 128, 4, 8, 16, 4)
    w[:, :, :, :, :8] = 0
    return {"x": x.reshape(N, 128, 8 * L).astype(BF), "u": u.reshape(N, 128, 512), "v": d["v"], **trees(rng, kind, q), **weights(rng, w.reshape(N, 128, 2048))}
def setup_inputs(rng):
    return {**numbers_of(rng), **trees(rng, rng.integers(0, 3, (N, 8))), **weights(rng, f(rng, N, 128, 2048))}
def setup_inputs_near(rng):
    q = rng.integers(-1, 2, (N, 8, 2 * L))
    size = np.exp2(-1.0 * rng.integers(0, 21, (N, 8, 2 * L)))
    small = rng.permutation(N) % 2 == 0
    size[small] = 2.0 ** -30
    kind = rng.integers(0, 3, (N, 8))
    g = np.stack([rng.permutation(8) for r in range(N)])
    kind[np.arange(N), g[:, 0]] = 5
    d = planted(rng, kind, q, size, np.where(small, 2.0 ** -30, 1.0))
    x = d["x"].reshape(N, 8, 16, 2 * L, 4)
    for r in range(N):
        e = int(g[r, 1])
        x[r, e, :8] = 0
        x[r, e, 0, :, 0] = np.exp2(-12.0 - np.arange(2 * L) % 8).astype(np.float32).astype(BF)
        x[r, e, 2, :, 0] = 1.9921875
    return {**d, "x": x.reshape(N, 128, 8 * L)}
def setup_inputs_deep(rng):
    k = np.stack([rng.permutation(8) for r in range(N)])
    m = (k // 2)[:, :, None]
    q = np.where(m < 3, m - 1, rng.integers(0, 2, (N, 8, 2 * L)) * 2 - 1)
    return planted(rng, 3 + k % 2, q, np.ones((N, 8, 2 * L)), np.ones(N))
def setup_inputs_huge(rng):
    d = numbers_of(rng)
    o = rng.permutation(N)
    c = np.stack([rng.permutation(2 * L) % 2 * 2.0 - 1.0 for r in range(N)])
    c[o == 0] = 1
    c[o == 1] = -1
    x = 2.0 ** 28 * (1 + rng.random((N, 128, 2 * L, 4))) * c[:, None, :, None]
    g = np.stack([rng.permutation(8) % 2 * 2.0 - 1.0 for r in range(N)])
    u = d["u"].reshape(N, 128, 128, 4)
    u[:, :, ::16] = (2.0 ** 30 * (0.75 + 0.25 * rng.random((N, 128, 8, 4))) * g[:, None, :, None]).astype(np.float32).astype(BF)
    w = np.zeros((N, 128, 4, 128, 4), np.float32)
    i = np.arange(128)
    for b in range(4): w[:, i, b, i, b] = 2
    return {"x": x.astype(np.float32).reshape(N, 128, 8 * L).astype(BF), "u": u.reshape(N, 128, 512), "v": d["v"], **trees(rng, rng.integers(0, 3, (N, 8))), **weights(rng, w.reshape(N, 128, 2048).astype(BF))}
def setup_inputs_spread(rng):
    d = setup_inputs(rng)
    d["x"] = wide(rng, N, 128, 8 * L, cols=6)
    return d
def check_inputs(d):
    bad = []
    for k in ("x", "u", "v"):
        a = np.abs(d[k].astype(np.float32))
        if not (np.isfinite(a).all() and ((a == 0) | (a >= 2.0 ** -30) & (a <= 2.0 ** 30)).all()): bad.append("a value of " + k)
    top = 2 * L - 1
    for r in range(N):
        a, b = gentries(d["ka"][r]).astype(np.int64), gentries(d["kb"][r]).astype(np.int64)
        if (b[:, L - 1] != -1).any(): bad.append("kb: the last entry of a group isn't -1")
        k = np.concatenate([a, b[:, :L - 1]], axis=1)
        if (np.sort(k, axis=1) != np.arange(top)).any():
            bad.append("ka, kb: a node isn't a child exactly once")
            continue
        up = np.full((8, 2 * L), top)
        np.put_along_axis(up, k, np.tile(np.concatenate([L + np.arange(L), L + np.arange(L - 1)]), (8, 1)), axis=1)
        for i in range(10): up = np.take_along_axis(up, up, axis=1)
        if (up != top).any(): bad.append("ka, kb: a node isn't under the head")
    return bad
def reference(x, u, v, ka, kb, wc, ws):
    qu = [mx_ref.quantize(u[r]) for r in range(N)]
    lay = [pk(wc[r], ws[r]) for r in range(N)]
    state = [x[r] for r in range(N)]
    own = [[(gentries(ka[r])[g], gentries(kb[r])[g]) for g in range(8)] for r in range(N)]
    for t in range(R):
        sent, add = [], []
        for r in range(N):
            q = mx_ref.quantize(state[r])
            state[r] = decode(q).astype(BF)
            p = mx_ref.matmul(qu[r], q)[::16, L:]
            done = [contract(own[r][g][0], own[r][g][1], p[g] > 0) for g in range(8)]
            own[r] = [e[:2] for e in done]
            one = gcols(state[r], np.stack([e[2] for e in done])).astype(np.float32)
            two = gcols(state[r], np.stack([e[3] for e in done])).astype(np.float32)
            sent.append(mx_ref.quantize(((one + two) * np.float32(0.5)).astype(BF)))
            add.append(np.stack([e[4] for e in done]))
        for r in range(N):
            q = sent[r ^ STEP[t]]
            h = tile([np.maximum(mx_ref.matmul(pick(lay[r], np.arange(128 * b, 128 * b + 128)), q), np.float32(0.0)) * np.float32(0.03125) for b in range(4)])
            for i in range(2):
                state[r] = (state[r].astype(np.float32) + gcols(h, add[r][:, i]).astype(np.float32)).astype(BF)
    y, kid = np.zeros((N, 128, 2 * L), np.float32), np.zeros((N, 8, 2 * L), np.float32)
    oc, osc = np.zeros((N, 128, 8 * L), np.uint8), np.zeros((N, 16, 2 * L), np.uint8)
    for r in range(N):
        q = mx_ref.quantize(state[r])
        y[r] = mx_ref.matmul(mx_ref.quantize(v[r]), q)
        for g in range(8): kid[r, g] = np.concatenate(own[r][g])
        oc[r], osc[r] = emit(q)
    return {"y": y, "kid": kid, "oc": oc, "osc": osc}

@@ -1,0 +1,623 @@
+from concourse.mybir import dt, AluOpType as A, ActivationFunctionType as AF
+
+F32, BF, I32, U16, C4X, U8 = "float32", "bfloat16", "int32", "uint16", "float8_e4m3fn_x4", "uint8"
+NL = 192
+NN = 384
+NT = 392
+PB = 1024
+M0 = 6291456.0
+M1 = 12582912.0
+SIB, HOLE, JUNK = 392, 840, 848
+WOFF = [200]
+for _k in range(8):
+    WOFF.append(WOFF[-1] + NN + max(8, 2 ** _k))
+WEND = WOFF[8] + NN + 128
+ORDER = [int(_k) for _k in """
+0 1 42 86 3 2 9 5 4 84 8 6 7 87 43 11 10 12 56 85 72 13 46 16 55 83 14 19 58 36 18 57 15 63 17 20 53 37 78 21 27 28 45 40 111 22
+112 60 39 61 29 47 23 41 30 24 59 93 62 113 94 95 97 51 88 31 114 98 25 115 64 116 67 70 52 44 117 65 99 54 69 118 92 101 119 81
+120 109 32 121 89 122 110 103 90 76 123 130 105 125 131 49 106 66 100 124 50 102 104 71 140 74 34 141 142 73 145 91 77 143 96 107
+144 75 38 148 48 33 149 68 126 151 80 146 108 79 154 147 155 127 150 82 152 157 153 128 156 160 158 161 159 35 162 129 163 164 133
+165 166 168 26 167 138 169 170 139 171 172 174 173 175 176 132 177 178 180 179 135 181 182 136 183 184 186 185 137 187 206 134 210
+188 208 189 204 192 195 190 193 207 191 196 198 211 205 209 197 199 270 200 194 264 271 201 272 265 202 203 263 266 220 212 221 273
+213 222 223 224 225 215 226 214 274 217 228 216 227 218 275 277 219 230 276 231 279 232 229 282 248 247 233 278 249 234 252 235 236
+268 237 256 250 253 238 287 283 280 241 289 239 257 288 251 290 240 258 242 291 254 244 296 259 298 284 245 297 294 243 292 299 295
+267 293 300 269 260 281 246 301 261 302 255 303 262 304 314 285 305 337 315 306 338 312 374 308 307 286 310 316 309 317 311 318 319
+313 320 321 322 339 323 340 324 325 326 341 327 328 342 343 344 330 329 345 331 347 332 333 375 335 346 334 377 348 336 349 376 350
+370 366 353 351 367 355 352 378 368 354 369 379 356 371 380 372 381 382 357 383 360 358 361 359 362 373 363 386 364 388 387 365 390
+392 389 391 393 384 394 395 385 396 397 402 398 401 403 406 410 399 409 407 404 408 400 405
+""".split()]
+
+
+def _sb(n, d=F32):
+    return ("sbuf", [128, n], d)
+
+
+SCRATCH = {
+    "xin": _sb(1536, BF), "uin": _sb(512, BF), "vin": _sb(512, BF), "kw": _sb(24, I32),
+    "wq": _sb(512, C4X), "wsc": _sb(512, U8), "eq": _sb(512, C4X), "es": _sb(512, U8),
+    "uq": _sb(128, C4X), "us": _sb(128, U8), "uq2": _sb(128, C4X), "us2": _sb(128, U8),
+    "vq": _sb(128, C4X), "vs": _sb(128, U8),
+    "q0": _sb(NN, C4X), "s0": _sb(NN, U8), "q1": _sb(NN, C4X), "s1": _sb(NN, U8), "q2": _sb(NN, C4X), "s2": _sb(NN, U8),
+    "lq": _sb(NN, C4X), "ls": _sb(NN, U8), "ll": _sb(48, U16), "gq": _sb(176, C4X), "gs": _sb(176, U8),
+    "fq0": _sb(128, C4X), "fs0": _sb(128, U8), "fq1": _sb(128, C4X), "fs1": _sb(128, U8),
+    "z": _sb(520, BF), "one": _sb(128, BF), "zero": _sb(512, BF),
+    "th": _sb(1536, BF), "xa": _sb(3072, BF), "xb": _sb(3072, BF),
+    "f0": _sb(512, BF), "f1": _sb(512, BF), "fp0": _sb(384, BF), "fp1": _sb(192, BF), "fsum": _sb(192, BF),
+    "h0": _sb(400, BF), "h1": _sb(208, BF), "ts0": _sb(384, BF), "ts1": _sb(192, BF),
+    "va0": _sb(384, BF), "va1": _sb(192, BF), "vb0": _sb(384, BF), "vb1": _sb(192, BF),
+    "c16": _sb(NN, BF), "c4": _sb(NL, BF), "m2": _sb(NN, BF), "cst": _sb(256), "csi": _sb(32, I32),
+    "hv": _sb(NT), "hn": _sb(NT), "leaf": _sb(NT), "sk": _sb(2 * NT), "kf": _sb(96), "fz": _sb(HOLE),
+    "w": _sb(WEND), "val": _sb(NN), "slot": _sb(NN), "pre": _sb(NL), "fr": _sb(NL), "tb": _sb(1248), "pos": _sb(648),
+    "so": _sb(8192), "sm": _sb(1024), "si": _sb(1024, I32), "off": _sb(1024, U16),
+    "sop": _sb(NN), "paye": _sb(NN), "scat": _sb(NN), "cnt": _sb(NT), "lqr": _sb(NL), "num": _sb(NL),
+    "pay0": _sb(NL), "pays": _sb(NL), "sort0": _sb(NL), "sort1": _sb(96), "ulo": _sb(NT), "um": _sb(NL), "uh": _sb(NL),
+    "bt": _sb(960), "b1": _sb(480), "g1": _sb(480), "ss": _sb(NN), "ft": _sb(456), "lpr": _sb(96), "num1": _sb(96),
+    "pay1": _sb(96), "pay1s": _sb(96), "ab0": _sb(672), "ab1": _sb(336), "dc0": _sb(192), "dc1": _sb(96),
+    "fb": _sb(NL), "kido": _sb(NN), "yo": _sb(NN), "lst0": _sb(48, U16),
+    "ps": ("psum", [128, 4096], F32),
+}
+SEMAPHORES = ["e%d" % i for i in range(140)] + ["ax", "al", "ag", "sent"]
+CY = 1.04
+
+
+def V(n, a, b, s=1):
+    return (n, a, b, s)
+
+
+def IT(a, b):
+    return ("sk", NT + a, NT + b, 1)
+
+
+def _len(v):
+    return (v[2] - v[1] + v[3] - 1) // v[3]
+
+
+def _span(v):
+    if v[0] == "ps":
+        return ("ps", v[1] // 512 * 512, (v[2] + 511) // 512 * 512, 1)
+    return v
+
+
+def _meet(x, y):
+    if x[0] != y[0] or x[2] <= y[1] or y[2] <= x[1]:
+        return False
+    return not (x[3] == y[3] and x[3] > 1 and (x[1] - y[1]) % x[3] != 0)
+
+
+def build(T, topo, core, rank):
+    ops = []
+    used = {"sm": 0, "si": 0, "off": 0, "so": 0}
+
+    def new(n, k):
+        a = used[n]
+        used[n] = a + (k + 7) // 8 * 8
+        assert used[n] <= SCRATCH[n][1][1]
+        return V(n, a, a + k)
+
+    def sub(v, a, b):
+        return V(v[0], v[1] + a * v[3], min(v[2], v[1] + b * v[3]), v[3])
+
+    def ap(v):
+        if len(v) == 2:
+            return ap(v[0]).indirect(ap(v[1]))
+        if v[3] == 1:
+            return T[v[0]][:, v[1]:v[2]]
+        return T[v[0]][:, v[1]:v[2]:v[3]]
+
+    def two(*vs):
+        return all(SCRATCH[v[0]][2] in (BF, U16) for v in vs)
+
+    def add(eng, fn, outs, ins, cost, lat=0.0, kind="c", after=()):
+        r, w = [], []
+        for v in ins:
+            if isinstance(v, tuple):
+                r += list(v) if len(v) == 2 else [v]
+        for v in outs:
+            if len(v) == 2:
+                w.append(v[0])
+                r.append(v[1])
+            else:
+                w.append(v)
+        w += [v for v in r if v[0] == "ps"]
+        r = [_span(v) for v in r if v[0] != "ps"]
+        w = [_span(v) for v in w]
+        deps = set(after)
+        for i, o in enumerate(ops):
+            if any(_meet(x, y) for x in w for y in o["r"] + o["w"]) or any(_meet(x, y) for x in r for y in o["w"]):
+                deps.add(i)
+        ops.append({"e": eng, "f": fn, "r": r, "w": w, "c": cost, "l": lat, "k": kind, "d": deps})
+        return len(ops) - 1
+
+    def sc(x):
+        return ap(x) if isinstance(x, tuple) else x
+
+    def vcost(out, in0, n, plain):
+        if len(in0) == 2:
+            return 50 + 1.56 * CY * n
+        if len(out) == 2:
+            return 50 + 3.8 * CY * n
+        return max(64, plain) * CY
+
+    def ts(out, in0, s1, o1, s2=None, o2=None):
+        n = _len(out)
+        c = vcost(out, in0, n, n / 2 if len(in0) > 2 and two(out, in0) else n)
+        if o2 is None:
+            return add("v", lambda q: q.tensor_scalar(ap(out), ap(in0), sc(s1), None, o1), [out], [in0, s1], c)
+        return add("v", lambda q: q.tensor_scalar(ap(out), ap(in0), sc(s1), sc(s2), o1, o2), [out], [in0, s1, s2], c)
+
+    def lin(out, in0, m, c):
+        return ts(out, in0, m, A.mult, c, A.add)
+
+    def tt(out, a, b, o):
+        n = _len(out)
+        return add("v", lambda q: q.tensor_tensor(ap(out), ap(a), ap(b), o), [out], [a, b], vcost(out, a, n, 2 * n))
+
+    def cp(out, in0):
+        n = _len(in0) if len(out) == 2 else _len(out)
+        return add("v", lambda q: q.tensor_copy(ap(out), ap(in0)), [out], [in0], vcost(out, in0, n, n))
+
+    def ms(out, c):
+        n = _len(out)
+        return add("v", lambda q: q.memset(ap(out), c), [out], [], max(64, n / 2 if two(out) else n) * CY)
+
+    def act(out, in0, scale=1.0, bias=0.0, fn=AF.Identity):
+        n = _len(out)
+        c = 65 + (1.56 if len(in0) == 2 else 1.0) * CY * n
+        if fn == AF.Identity and scale == 1.0 and bias == 0.0:
+            return add("s", lambda q: q.activation(ap(out), ap(in0), AF.Copy), [out], [in0], c)
+        return add("s", lambda q: q.activation(ap(out), ap(in0), fn, bias=bias, scale=scale), [out], [in0], c)
+
+    def scan(out, d0, d1, init, o0, o1):
+        return add("v", lambda q: q.tensor_tensor_scan(ap(out), ap(d0), ap(d1), init, o0, o1), [out], [d0, d1],
+                   max(64, _len(out)) * CY)
+
+    def deal(src, blk=16):
+        n = _len(src)
+        o = new("so", n)
+        scan(o, src, V("c16" if blk == 16 else "c4", 0, n), 0.0, A.max, A.mult)
+        return V("so", o[1] + blk - 1, o[2], blk)
+
+    def iota(out, pat, base, ch=0):
+        if SCRATCH[out[0]][2] == I32:
+            return add("g", lambda q: q.iota(ap(out), pat, base, ch), [out], [], 130 + 2 * CY * _len(out))
+        return add("g", lambda q: q.iota(ap(out), pat, base, ch, allow_small_or_imprecise_dtypes=True), [out], [],
+                   130 + 2 * CY * _len(out))
+
+    def fill(out, c):
+        return iota(out, [[0, _len(out)]], c)
+
+    def ramp(out, base, step=1.0):
+        return act(out, IT(0, _len(out)), step, base - 504.0 * step)
+
+    def quant(q, s, a, b, src):
+        o, p = V(q, a, b), V(s, a, b)
+        return add("v", lambda e: e.quantize_mx(ap(o), ap(p), ap(src)), [o, p], [src], 12 + 0.22 * 4 * (b - a))
+
+    def mm(bank, lq, ls, la, rq, rs, a, b):
+        o, i = V("ps", 512 * bank, 512 * bank + b - a), [V(lq, la, la + 128), V(ls, la, la + 128), V(rq, a, b), V(rs, a, b)]
+        add("t", lambda e: e.matmul_mx(ap(o), ap(i[0]), ap(i[1]), ap(i[2]), ap(i[3]), True, True), [o], i, (b - a + 16) * 0.7)
+        return o
+
+    def dma(eng, out, in_, outs, ins, nbytes):
+        return add(eng, lambda e: e.dma_start(out, in_), outs, ins, 60, 1700 + nbytes / 150.0, "d")
+
+    def u8(v):
+        return ap(v).bitcast(dt.uint8) if SCRATCH[v[0]][2] == C4X else ap(v)
+
+    count = {}
+
+    def send(dst, out, in_, sem):
+        assert topo.may_write(core, dst)
+        rid, pid = topo.addr(dst)[:2]
+        n = len(topo.engines(core, dst))
+        count[sem] = count.get(sem, 0) + n
+        count["sent"] = count.get("sent", 0) + n
+        return add("g", lambda e: e.remote_dma(u8(out), u8(in_), T.sem[sem], T.sem["sent"], pid, rid, topo.mask(core, dst)),
+                   [], [in_], 150, 0.0, "r")
+
+    def arrive(sem, outs, sends, lat):
+        i = add("a", None, outs, [], 0.0, lat, "a", sends)
+        ops[i]["sem"] = (sem, count[sem])
+
+    peer = [T.cores[rank ^ 1], T.cores[rank ^ 2]]
+
+    dma("y", T.xin[:, 768:1536], T.x[:, 768:1536], [V("xin", 768, 1536)], [], 196608)
+    dma("s", T.uin[:], T.u[:], [V("uin", 0, 512)], [], 131072)
+    dma("y", T.kw[:, 0:12], T.ka[:], [V("kw", 0, 12)], [], 6144)
+    dma("y", T.kw[:, 12:24], T.kb[:], [V("kw", 12, 24)], [], 6144)
+    dma("y", T.xin[:, 0:768], T.x[:, 0:768], [V("xin", 0, 768)], [], 196608)
+    dma("y", T.wq[:].bitcast(dt.uint8), T.wc[:], [V("wq", 0, 512)], [], 262144)
+    dma("y", T.wsc[:], T.ws[:], [V("wsc", 0, 512)], [], 65536)
+    dma("y", T.vin[:], T.v[:], [V("vin", 0, 512)], [], 131072)
+
+    iota(IT(0, NT), [[1, NT]], 504)
+    pi, pc = V("csi", 0, 1), V("cst", 0, 5)
+    iota(pi, [[1, 1]], 0, 1)
+    ts(V("csi", 2, 3), pi, 15, A.bitwise_and)
+    ts(V("csi", 3, 4), pi, 2, A.logical_shift_right, 3, A.bitwise_and)
+    ts(V("csi", 4, 5), pi, 3, A.bitwise_and)
+    cp(V("cst", 0, 3), V("csi", 2, 5))
+    p16, p4, pt, pt768, ptm = [sub(pc, i, i + 1) for i in range(5)]
+    ts(pt768, pt, 768.0, A.add)
+    ts(ptm, pt, -2048.0, A.add)
+    j16, j4 = V("cst", 8, 24), V("cst", 24, 40)
+    iota(j16, [[1, 16]], 0)
+    iota(j4, [[0, 4], [1, 4]], 0)
+    for c, j, p, blk, t0, top in (("c16", j16, p16, 16, 40, NN), ("c4", j4, p4, 4, 72, NL)):
+        ge, eq = V("cst", t0, t0 + 16), V("cst", t0 + 16, t0 + 32)
+        ts(ge, j, p, A.is_ge)
+        ts(eq, j, p, A.is_equal)
+        tt(V(c, 0, 16), ge, eq, A.add)
+        ts(V(c, blk - 1, 16, blk), V(c, blk - 1, 16, blk), 0.25, A.mult)
+        n = 16
+        while n < top:
+            k = min(n, top - n)
+            cp(V(c, n, n + k), V(c, 0, k))
+            n += k
+    ms(V("m2", 0, NN), -2.0)
+    k16, awr, kwh, nodeh, awl = V("cst", 104, 116), V("cst", 116, 128), V("cst", 128, 134), V("cst", 136, 148), V("cst", 148, 160)
+    iota(k16, [[16, 12]], 0)
+    ts(k16, k16, p16, A.add, 0.5, A.mult)
+    ts(awr, k16, (SIB - 512) / 2.0, A.add)
+    ts(awl, k16, (SIB + 768) / 2.0, A.add)
+    ts(kwh, sub(k16, 0, 6), -256.0, A.add)
+    ts(nodeh, k16, (NL + 512) / 2.0, A.add)
+    iota(V("csi", 8, 16), [[16, 8]], 0)
+    ou = new("off", 8)
+    cp(ou, V("csi", 8, 16))
+    ms(V("hv", 0, 200), 0.0)
+    ramp(V("hv", 200, NT), PB + NL)
+    ms(V("hn", 0, 200), 4096.0)
+    ramp(V("hn", 200, NT), -(PB + NL), -1.0)
+    fill(V("leaf", 0, 8), 2)
+    fill(V("leaf", 8, 200), 3)
+    fill(V("leaf", 200, NT), 2)
+    act(V("sk", 0, NT), IT(0, NT))
+    ramp(V("val", NL, NN), PB)
+    ramp(V("slot", 0, NL), 512)
+    ramp(V("slot", NL, NN), 768)
+    act(V("kf", 0, 96), IT(9, 105), 1.0 / 1024, -0.5)
+    ms(V("w", WOFF[0] + NL - 1, WOFF[0] + NL), float(PB + NN))
+    for k in range(9):
+        n = min(128, max(8, 2 ** k))
+        ramp(V("w", WOFF[k] + NN, WOFF[k] + NN + n), PB + NN + 2 ** k)
+    fill(V("tb", 0, 8), 512)
+    fill(V("tb", 391, NT), 767)
+    fill(V("tb", SIB + NL, SIB + 256), 512)
+    fill(V("tb", HOLE, JUNK), 511)
+    fill(V("pos", 0, 200), 1408)
+    fill(V("pos", 200 + NL, 456), 1408)
+    ms(V("cnt", 0, 1), M0 + 0.5)
+    fill(V("ulo", 0, 8), int(M1))
+    fill(V("bt", NL, 256), 0)
+    fill(V("bt", 448, 512), 0)
+    fill(V("ft", 0, 200), 0)
+    fill(V("ft", 391, 456), 0)
+    fill(V("fz", 0, SIB + 256), 512)
+    fill(V("fz", SIB + 256, HOLE), 512 + NT)
+    fill(V("f0", 384, 512), 0)
+    fill(V("f1", NL, 512), 0)
+    fill(V("h0", 0, 4), 0)
+    fill(V("h1", 0, 4), 0)
+    ms(V("zero", 0, 512), 0.0)
+    quant("gq", "gs", 48, 176, V("zero", 0, 512))
+    ms(V("z", 0, 520), 0.0)
+    ms(V("one", 0, 128), 1.0)
+    add("g", lambda q: q.affine_select(T.z[:, 4:516:4], T.one[:], [[-1, 128]], A.is_equal, 0.0, 0, 1),
+        [V("z", 4, 516, 4)], [V("one", 0, 128)], 170 + 256 * CY)
+    for b in range(4):
+        quant("eq", "es", 128 * b, 128 * b + 128, V("z", 4 - b, 516 - b))
+
+    quant("uq", "us", 0, 128, V("uin", 0, 512))
+    add("v", lambda q: q.tensor_copy(T.uq2[:].bitcast(dt.uint32), T.uq[:].bitcast(dt.uint32).indirect(ap(ou))),
+        [V("uq2", 0, 128)], [V("uq", 0, 128), ou], 50 + 200 * CY)
+    add("s", lambda q: q.activation(T.us2[:], T.us[:].indirect(ap(ou)), AF.Copy),
+        [V("us2", 0, 128)], [V("us", 0, 128), ou], 65 + 200 * CY)
+    quant("vq", "vs", 0, 128, V("vin", 0, 512))
+
+    def unpack(q, s, dst, scale, b0=0):
+        for b in range(4):
+            o = mm(b0 + b, "eq", "es", 128 * b, q, s, 0, NN)
+            act(V(dst, b, 1536, 4), o, scale)
+
+    quant("q0", "s0", NL, NN, V("xin", 768, 1536))
+    p0 = mm(4, "uq2", "us2", 0, "q0", "s0", NL, NN)
+    quant("q0", "s0", 0, NL, V("xin", 0, 768))
+    sx = [send(peer[0], V("lq", 0, NN), V("q0", 0, NN), "ax"), send(peer[0], V("ls", 0, NN), V("s0", 0, NN), "ax")]
+    arrive("ax", [V("lq", 0, NN), V("ls", 0, NN)], sx, 9000)
+    unpack("q0", "s0", "xa", 1.0)
+    ka, kb = V("kw", 0, 12), V("kw", 12, 24)
+    d, gz, d2, ca, cb = [new("sm", 12) for _ in range(5)]
+    tt(d, kb, ka, A.subtract)
+    ts(gz, kb, 0.0, A.is_ge, 2.0, A.mult)
+    tt(d2, d, gz, A.mult)
+    tt(ca, ka, d2, A.subtract)
+    tt(cb, kb, d2, A.add)
+    ts(V("fr", 0, NL), p0, 0.0, A.is_gt, 2.0, A.add)
+    fw = deal(V("fr", 0, NL))
+    t, kn = new("sm", 12), new("sm", 24)
+    tt(t, fw, d2, A.mult)
+    tt(sub(kn, 12, 24), cb, t, A.subtract)
+    tt(sub(kn, 0, 12), ca, t, A.add)
+    oc = new("off", 24)
+    ts(oc, kn, 8.0, A.add)
+    ocl, ocr = sub(oc, 0, 12), sub(oc, 12, 24)
+    tt(V("val", 0, NL), (V("hv", 0, NT), ocr), V("val", NL, NN), A.max)
+    tt(V("pre", 0, NL), (V("hn", 0, NT), ocl), V("val", 0, NL), A.min)
+    act(V("w", WOFF[0] + NL, WOFF[0] + NN), V("pre", 0, NL), fn=AF.Abs)
+    cp((V("w", 0, WOFF[0] + NL - 1), oc), V("val", 0, NN))
+    for h in range(4):
+        cp((V("tb", 0, 391), sub(oc, 6 * h, 6 * h + 6)), V("slot", 96 * h, 96 * h + 96))
+    act(V("tb", SIB, SIB + NL), (IT(0, NT), ocr))
+    act(V("tb", SIB + 256, SIB + 256 + NL), (IT(0, NT), ocl))
+    act(V("sop", 0, NL), V("tb", 200, NT), 1.0 / 4096, -0.125)
+    act(V("sop", NL, NN), V("tb", 200, NT), 1.0 / 4096)
+    tt(V("paye", 0, NL), (V("leaf", 0, NT), ocl), V("sop", 0, NL), A.add)
+    tt(V("paye", NL, NN), (V("leaf", 0, NT), ocr), V("sop", NL, NN), A.add)
+    act(V("pays", 0, NL), V("tb", 8, 200), 256.0, -512.0)
+    tt(V("pay0", 0, NL), V("pays", 0, NL), IT(8, 200), A.add)
+    oev = new("off", 12)
+    lin(oev, deal(V("tb", 8, 200)), 2.0, -312.0)
+    op = None
+    for k in range(9):
+        win = V("w", WOFF[k], WOFF[k] + NN + min(128, max(8, 2 ** k)))
+        if k < 8:
+            op = new("off", 24)
+            for h in (1, 0) if k == 0 else (0, 1):
+                lin(sub(op, 12 * h, 12 * h + 12), deal(V("w", WOFF[k] + NL * h, WOFF[k] + NL * h + NL)), 2.0, float(-PB))
+        for h in (0, 1):
+            if k < 8:
+                o = V("w", WOFF[k + 1] + NL * h, WOFF[k + 1] + NL * h + NL)
+            else:
+                o = V("pos", 456 - 256 * h, 456 - 256 * h + NL)
+            src = (win, sub(op, 12 * h, 12 * h + 12))
+            if k >= 8 and h == 1:
+                cp(o, src)
+            else:
+                act(o, src)
+    pw = V("pos", 0, 648)
+    opos = new("off", 24)
+    lin(sub(opos, 0, 12), deal(V("pos", 200, NT)), 2.0, -1408.0)
+    dpost = deal(V("pos", 456, 648))
+    lin(sub(opos, 12, 24), dpost, 2.0, -1408.0)
+    ohi = new("off", 12)
+    lin(ohi, dpost, 2.0, -1407.0)
+    act(V("lqr", 0, NL), (pw, oev))
+    olq = new("off", 12)
+    lin(olq, deal(V("lqr", 0, NL)), 2.0, -1408.0)
+    cp((V("scat", 0, NN), opos), V("paye", 0, NN))
+    scan(V("cnt", 1, 385), V("scat", 0, NN), V("m2", 0, NN), M0 + 0.5, A.add, A.add)
+    cw = V("cnt", 0, 385)
+    act(V("num", 0, NL), (cw, olq))
+    onum = new("off", 12)
+    lin(onum, deal(V("num", 0, NL)), 2.0, -(M0 + 0.5))
+    cp((V("sort0", 0, NL), onum), V("pay0", 0, NL))
+    unpack("lq", "ls", "th", 0.5, 4)
+
+    def fold_lists(sort, m, lst):
+        e = m // 8
+        i4, l4, q4 = new("si", e), new("si", e), new("si", e)
+        lin(i4, deal(V(sort, 1, m, 2), 4), 2.0, -131072.0)
+        ts(q4, i4, 8, A.logical_shift_right, 255, A.bitwise_and)
+        ts(l4, i4, 255, A.bitwise_and)
+        lin(sub(lst, e, 2 * e), q4, 4.0, pt768)
+        lin(sub(lst, 0, e), l4, 4.0, pt)
+
+    def fold(win, lst, e, tmp, out):
+        h = e // 2
+        for i in range(2):
+            act(V(tmp, 16 * h * i, 16 * h * (i + 1)), (win, sub(lst, e + h * i, e + h * (i + 1))))
+            tt(V(out, 16 * h * i, 16 * h * (i + 1)), (win, sub(lst, h * i, h * (i + 1))), V(tmp, 16 * h * i, 16 * h * (i + 1)), A.add)
+
+    def rake(r, sort, m, x):
+        n, c, e = m // 2, m // 32, m // 8
+        c2 = c + c % 2
+        ab = "ab%d" % r
+        i16, s16, par = new("si", c), new("si", c), new("si", c)
+        lin(i16, deal(V(sort, 1, m, 2)), 2.0, -131072.0)
+        ts(par, i16, 8, A.logical_shift_right, 255, A.bitwise_and)
+        ts(s16, i16, 8, A.logical_shift_right)
+        opar, osib = new("off", c), new("off", c)
+        ts(opar, par, 200.0, A.add)
+        ts(osib, s16, float(SIB), A.add)
+        act(V(ab, 0, n), (V("tb", 0, NT), opar))
+        tt(V(ab, n, 2 * n), (V("tb", 0, HOLE), osib), V("kf", 0, n), A.add)
+        act(V(ab, 2 * n, 3 * n), (V("fz", 0, HOLE), osib))
+        cp((V("sk", 0, NT), opar), V(ab, n, 2 * n))
+        oa = deal(V(ab, 0, 3 * n))
+        ia, gp, t1, t2 = new("si", 3 * c), new("si", c), new("sm", c), new("sm", c)
+        lin(ia, oa, 2.0, -512.0)
+        ts(gp, sub(ia, 0, c), 255, A.bitwise_and)
+        sib, zz = sub(ia, c, 2 * c), sub(ia, 2 * c, 3 * c)
+        tt(t1, gp, zz, A.add)
+        tt(t2, sib, zz, A.subtract)
+        og, ob = new("off", 2 * c), new("off", 2 * c)
+        ts(sub(og, 0, c), t1, 200.0, A.add)
+        ts(sub(og, c, 2 * c), t2, 8.0 + NT, A.add)
+        act(V(ab, 5 * n, 7 * n), (V("sk", 0, 2 * NT), og))
+        o = deal(V(ab, 5 * n, 7 * n), 4)
+        os_, opre, otg = new("off", e), new("off", e), new("off", e)
+        lin(os_, sub(o, e, 2 * e), 8.0, ptm)
+        act(V("ts%d" % r, 0, 4 * n), (V(x, 0, 1536), os_))
+        ii, jj, cc, tg = new("si", 2 * e), new("si", 2 * e), new("sm", e), new("sm", e)
+        ts(ii, o, 2048.0, A.mult)
+        ts(jj, ii, 1023, A.bitwise_and)
+        lin(opre, sub(jj, e, 2 * e), 4.0, pt)
+        ts(cc, sub(jj, 0, e), 0.0, A.is_gt, float(NL), A.mult)
+        tt(tg, sub(o, e, 2 * e), cc, A.add)
+        lin(otg, tg, 8.0, ptm)
+        if r == 0:
+            ts(sub(ob, 0, c), gp, 200.0, A.add)
+            ts(sub(ob, c, 2 * c), sib, 8.0, A.add)
+            act(V(ab, 3 * n, 5 * n), (V("sk", 0, NT), ob))
+        else:
+            ts(sub(ob, 0, c), sib, 8.0, A.add)
+            act(V(ab, 4 * n, 5 * n), (V("sk", 0, NT), sub(ob, 0, c)))
+        dc = "dc%d" % r
+        act(V(dc, n, 2 * n), V(ab, 4 * n, 5 * n), 1.0, M1)
+        act(V(dc, 0, n), V(dc, n, 2 * n), 1.0, -M1)
+        i2, i3, oct_ = new("si", c2), new("si", c2), new("off", c2)
+        lin(sub(i2, 0, c), sub(oa, 0, c), 2.0, -256.0)
+        ts(sub(i3, 0, c), sub(i2, 0, c), 511, A.bitwise_and)
+        ts(sub(oct_, 0, c), sub(i3, 0, c), float(SIB), A.add)
+        cp((V("tb", 0, HOLE), sub(oct_, 0, c)), V(dc, 0, n))
+        if r == 0:
+            rb, ee, nt, st, ost = new("si", 2 * c), new("sm", c), new("sm", c), new("sm", c), new("off", c)
+            lin(rb, deal(V(ab, 3 * n, 5 * n)), 2.0, -512.0)
+            tt(ee, sub(rb, 0, c), gp, A.subtract)
+            ts(nt, ee, float(NL), A.not_equal, float(JUNK), A.mult)
+            tt(st, sub(rb, c, 2 * c), nt, A.add)
+            ts(ost, st, 8.0, A.add)
+            cp((V("tb", 0, 1248), ost), V(ab, 0, n))
+        return opre, otg
+
+    def layer(r, gq, gs, n, lists, x):
+        h = "h%d" % r
+        for b in range(4):
+            o = mm(4 + b, "wq", "wsc", 128 * b, gq, gs, 0, 128)
+            o, dst = V("ps", o[1], o[1] + n), V(h, 4 + b, 4 + 4 * n, 4)
+            if b == 3:
+                ts(dst, o, 0.0, A.max, 0.03125, A.mult)
+            else:
+                act(dst, o, 0.03125, fn=AF.Relu)
+        va, vb = V("va%d" % r, 0, 4 * n), V("vb%d" % r, 0, 4 * n)
+        tt(va, (V(h, 0, 4 + 4 * n), lists[0]), V("ts%d" % r, 0, 4 * n), A.add)
+        tt(vb, va, V(h, 4, 4 + 4 * n), A.add)
+        cp((V(x, 0, 3072), lists[1]), vb)
+
+    lst0 = V("lst0", 0, 48)
+    fold_lists("sort0", NL, lst0)
+    arrive("al", [V("ll", 0, 48)], [send(peer[0], V("ll", 0, 48), lst0, "al")], 2200)
+    lists0 = rake(0, "sort0", NL, "xa")
+    ub = M1 - M0 / 2
+    act(V("ulo", 8, 200), V("num", 0, NL), 0.5, ub)
+    act(V("ulo", 200, NT), (cw, sub(opos, 0, 12)), 0.5, ub)
+    act(V("uh", 0, NL), (cw, ohi), 0.5, ub)
+    act(V("um", 0, NL), (V("ulo", 0, NT), ocr))
+    tt(V("bt", 0, NL), V("uh", 0, NL), V("um", 0, NL), A.subtract)
+    tt(V("bt", 256, 448), V("ulo", 200, NT), V("um", 0, NL), A.subtract)
+    act(V("bt", 512, 960), V("bt", 0, 448), -1.0)
+    isl, cs, cpar = new("si", 24), new("si", 30), new("si", 30)
+    ts(isl, deal(V("scat", 0, NN)), 8192.0, A.mult)
+    ts(sub(cs, 0, 24), isl, 1023, A.bitwise_and)
+    ie, lf = new("si", 6), new("si", 6)
+    lin(ie, deal(V("sort0", 0, NL, 2)), 2.0, -131072.0)
+    ts(sub(cs, 24, 30), ie, 8, A.logical_shift_right)
+    ts(cpar, cs, 255, A.bitwise_and)
+    ts(lf, ie, 255, A.bitwise_and)
+    osl, opl, olf, olp = new("off", 30), new("off", 30), new("off", 6), new("off", 6)
+    cp(osl, cs)
+    ts(opl, cpar, 200.0, A.add)
+    ts(olf, lf, 8.0, A.add)
+    act(V("b1", 0, 480), (V("bt", 0, 960), osl))
+    act(V("lpr", 0, 96), (pw, sub(opl, 24, 30)))
+    lin(olp, deal(V("lpr", 0, 96)), 2.0, -1408.0)
+    act(V("pay1s", 0, 96), (V("tb", 0, NT), olf), 256.0, -512.0)
+    tt(V("pay1", 0, 96), (IT(0, NT), olf), V("pay1s", 0, 96), A.add)
+    fold(V("th", 0, 1536), V("ll", 0, 48), 24, "fp0", "f0")
+    quant("fq0", "fs0", 0, 128, V("f0", 0, 512))
+    layer(0, "fq0", "fs0", 96, lists0, "xa")
+
+    quant("q1", "s1", NL, NN, V("xa", 768, 1536))
+    p1 = mm(4, "uq2", "us2", 0, "q1", "s1", NL, NN)
+    quant("q1", "s1", 0, NL, V("xa", 0, 768))
+    unpack("q1", "s1", "xb", 1.0)
+    ts(V("ft", 200, 391), V("ps", p1[1], p1[1] + NL - 1), 0.0, A.is_gt)
+    tt(V("g1", 0, 480), (V("ft", 0, 456), opl), V("b1", 0, 480), A.mult)
+    scan(V("ss", 0, NN), V("g1", 0, NN), V("m2", 0, NN), 512.0, A.add, A.max)
+    tt(V("num1", 0, 96), (V("ss", 0, NN), olp), V("g1", NN, 480), A.add)
+    nh, on1 = new("sm", 6), new("off", 6)
+    tt(nh, deal(V("num1", 0, 96)), kwh, A.add)
+    ts(on1, nh, 2.0, A.mult)
+    cp((V("sort1", 0, 96), on1), V("pay1", 0, 96))
+    lst1 = new("off", 24)
+    fold_lists("sort1", 96, lst1)
+    fold(V("xb", 0, 1536), lst1, 12, "fp1", "fsum")
+    ts(V("f1", 0, NL), V("fsum", 0, NL), 0.5, A.mult)
+    quant("fq1", "fs1", 0, 128, V("f1", 0, 512))
+    sg = [send(peer[1], V("gq", 0, 48), V("fq1", 0, 48), "ag"), send(peer[1], V("gs", 0, 48), V("fs1", 0, 48), "ag")]
+    arrive("ag", [V("gq", 0, 48), V("gs", 0, 48)], sg, 2500)
+    act(V("fz", SIB, SIB + NL), V("ft", 200, NT), float(NT), 512.0)
+    act(V("fz", SIB + 256, HOLE), V("ft", 200, NT), float(-NT), 512.0 + NT)
+    lists1 = rake(1, "sort1", 96, "xb")
+    act(V("fb", 0, NL), V("ft", 200, NT), 256.0, 512.0)
+    fh, dead, dz, ik, ik2, ok = deal(V("fb", 0, NL)), new("sm", 12), new("sm", 12), new("sm", 24), new("sm", 24), new("off", 24)
+    tt(sub(ik, 0, 12), awl, fh, A.subtract)
+    tt(sub(ik, 12, 24), awr, fh, A.add)
+    tt(dead, deal(V("sk", 200, NT)), nodeh, A.not_equal)
+    ts(dz, dead, HOLE / 2.0, A.mult)
+    tt(sub(ik2, 0, 12), sub(ik, 0, 12), dz, A.max)
+    tt(sub(ik2, 12, 24), sub(ik, 12, 24), dz, A.max)
+    ts(ok, ik2, 2.0, A.mult)
+    act(V("kido", 0, NN), (V("tb", 0, JUNK), ok), 1.0, -512.0)
+    dma("y", T.kid[:], T.kido[0:128:16, :], [], [V("kido", 0, NN)], 12288)
+    layer(1, "gq", "gs", 48, lists1, "xb")
+
+    for h in range(2):
+        a, b = NL * h, NL * h + NL
+        quant("q2", "s2", a, b, V("xb", 4 * a, 4 * b))
+        o = mm(h, "vq", "vs", 0, "q2", "s2", a, b)
+        if h:
+            cp(V("yo", a, b), o)
+        else:
+            act(V("yo", a, b), o)
+        dma("y" if h else "s", T.y[:, a:b], T.yo[:, a:b], [], [V("yo", a, b)], 98304)
+        dma("y", T.oc[:, 4 * a:4 * b], T.q2[:, a:b].bitcast(dt.uint8), [], [V("q2", a, b)], 98304)
+    for k in range(4):
+        dma("s" if k % 2 else "y", T.osc[4 * k:4 * k + 4, :], T.s2[32 * k:32 * k + 4, :], [], [V("s2", 0, NN)], 1536)
+    return ops, count
+
+
+def rank_program(g, core, T, topo):
+    rank = T.rank_of(core)
+    if rank is None:
+        return
+    ops, count = build(T, topo, core, rank)
+    order = ORDER
+    place = {i: k for k, i in enumerate(order)}
+    assert len(place) == len(ops) and all(place[j] < place[i] for i, o in enumerate(ops) for j in o["d"])
+    queue = {"v": g.vector, "s": g.scalar, "t": g.tensor, "y": g.sync, "g": g}
+    known = {e: set() for e in queue}
+    saw, waits, needed = {}, {}, set()
+    for i in order:
+        o = ops[i]
+        if o["k"] == "a":
+            saw[i] = set()
+            continue
+        k, ws = known[o["e"]], []
+        for j in sorted(o["d"], key=lambda q: -place[q]):
+            if j not in k and ops[j]["k"] != "r":
+                ws.append(j)
+                k.add(j)
+                k |= saw[j]
+        waits[i] = ws
+        needed |= set(ws)
+        saw[i] = set(k)
+    tail = [i for i in order if ops[i]["k"] == "d" and i not in needed]
+    needed |= set(tail)
+    last, total, sem = [], [], {}
+    for i in order:
+        o = ops[i]
+        if o["k"] == "a":
+            sem[i] = o["sem"]
+            continue
+        q = queue[o["e"]]
+        for j in waits[i]:
+            q.wait_ge(T.sem[sem[j][0]], sem[j][1])
+        call = o["f"](q)
+        if i in needed:
+            step = 16 if o["k"] == "d" else 1
+            free = [s for s in range(len(last)) if step == 1 and last[s] in saw[i] and ops[last[s]]["e"] == o["e"] and ops[last[s]]["k"] == "c"]
+            if free:
+                s = free[0]
+            else:
+                s = len(last)
+                last.append(i)
+                total.append(0)
+            last[s] = i
+            total[s] += step
+            sem[i] = ("e%d" % s, total[s])
+            call.then_inc(T.sem[sem[i][0]], step)
+    for i in tail:
+        g.wait_ge(T.sem[sem[i][0]], sem[i][1])
+    g.wait_ge(T.sem["sent"], count["sent"])

@@ -1,31 +1,17 @@
 from concourse.mybir import dt, AluOpType as A, ActivationFunctionType as AF
 
-F32, BF, I32, U16, C4X, U8 = "float32", "bfloat16", "int32", "uint16", "float8_e4m3fn_x4", "uint8"
+F32, BF, F16, I32, U16, C4X, U8 = "float32", "bfloat16", "float16", "int32", "uint16", "float8_e4m3fn_x4", "uint8"
 NL = 192
 NN = 384
-NT = 392
-PB = 1024
-M0 = 6291456.0
-M1 = 12582912.0
-SIB, HOLE, JUNK = 392, 840, 848
-WOFF = [200]
-for _k in range(8):
-    WOFF.append(WOFF[-1] + NN + max(8, 2 ** _k))
-WEND = WOFF[8] + NN + 128
-ORDER = [int(_k) for _k in """
-0 1 42 86 3 2 9 5 4 84 8 6 7 87 43 11 10 12 56 85 72 13 46 16 55 83 14 19 58 36 18 57 15 63 17 20 53 37 78 21 27 28 45 40 111 22
-112 60 39 61 29 47 23 41 30 24 59 93 62 113 94 95 97 51 88 31 114 98 25 115 64 116 67 70 52 44 117 65 99 54 69 118 92 101 119 81
-120 109 32 121 89 122 110 103 90 76 123 130 105 125 131 49 106 66 100 124 50 102 104 71 140 74 34 141 142 73 145 91 77 143 96 107
-144 75 38 148 48 33 149 68 126 151 80 146 108 79 154 147 155 127 150 82 152 157 153 128 156 160 158 161 159 35 162 129 163 164 133
-165 166 168 26 167 138 169 170 139 171 172 174 173 175 176 132 177 178 180 179 135 181 182 136 183 184 186 185 137 187 206 134 210
-188 208 189 204 192 195 190 193 207 191 196 198 211 205 209 197 199 270 200 194 264 271 201 272 265 202 203 263 266 220 212 221 273
-213 222 223 224 225 215 226 214 274 217 228 216 227 218 275 277 219 230 276 231 279 232 229 282 248 247 233 278 249 234 252 235 236
-268 237 256 250 253 238 287 283 280 241 289 239 257 288 251 290 240 258 242 291 254 244 296 259 298 284 245 297 294 243 292 299 295
-267 293 300 269 260 281 246 301 261 302 255 303 262 304 314 285 305 337 315 306 338 312 374 308 307 286 310 316 309 317 311 318 319
-313 320 321 322 339 323 340 324 325 326 341 327 328 342 343 344 330 329 345 331 347 332 333 375 335 346 334 377 348 336 349 376 350
-370 366 353 351 367 355 352 378 368 354 369 379 356 371 380 372 381 382 357 383 360 358 361 359 362 373 363 386 364 388 387 365 390
-392 389 391 393 384 394 395 385 396 397 402 398 401 403 406 410 399 409 407 404 408 400 405
-""".split()]
+NB = 16
+NT = NN + NB
+NI = NL + NB
+SB = 256
+K = 1024.0
+M = 8388864.0
+CY, WAKE = 1.04, 100
+TRIES = 6000
+ON = {"sx": "s", "sz": "vss", "ch": "ss", "pay": "sv", "y": "ss", "relu": "ssss", "jv": [0] * 7, "gw": 2, "xh": 0, "fb": "s"}
 
 
 def _sb(n, d=F32):
@@ -38,34 +24,29 @@ SCRATCH = {
     "uq": _sb(128, C4X), "us": _sb(128, U8), "uq2": _sb(128, C4X), "us2": _sb(128, U8),
     "vq": _sb(128, C4X), "vs": _sb(128, U8),
     "q0": _sb(NN, C4X), "s0": _sb(NN, U8), "q1": _sb(NN, C4X), "s1": _sb(NN, U8), "q2": _sb(NN, C4X), "s2": _sb(NN, U8),
-    "lq": _sb(NN, C4X), "ls": _sb(NN, U8), "ll": _sb(48, U16), "gq": _sb(176, C4X), "gs": _sb(176, U8),
+    "lq": _sb(NN + 48, C4X), "ls": _sb(NN + 48, U8), "ll": _sb(48, U16), "lst0": _sb(48, U16),
     "fq0": _sb(128, C4X), "fs0": _sb(128, U8), "fq1": _sb(128, C4X), "fs1": _sb(128, U8),
-    "z": _sb(520, BF), "one": _sb(128, BF), "zero": _sb(512, BF),
-    "th": _sb(1536, BF), "xa": _sb(3072, BF), "xb": _sb(3072, BF),
+    "z": _sb(520, BF), "one": _sb(128, BF), "zero": _sb(NN, BF),
+    "th": _sb(1536, BF), "xa": _sb(3072, BF), "xb": _sb(3072, BF), "xh": _sb(1536, BF),
     "f0": _sb(512, BF), "f1": _sb(512, BF), "fp0": _sb(384, BF), "fp1": _sb(192, BF), "fsum": _sb(192, BF),
-    "h0": _sb(400, BF), "h1": _sb(208, BF), "ts0": _sb(384, BF), "ts1": _sb(192, BF),
-    "va0": _sb(384, BF), "va1": _sb(192, BF), "vb0": _sb(384, BF), "vb1": _sb(192, BF),
-    "c16": _sb(NN, BF), "c4": _sb(NL, BF), "m2": _sb(NN, BF), "cst": _sb(256), "csi": _sb(32, I32),
-    "hv": _sb(NT), "hn": _sb(NT), "leaf": _sb(NT), "sk": _sb(2 * NT), "kf": _sb(96), "fz": _sb(HOLE),
-    "w": _sb(WEND), "val": _sb(NN), "slot": _sb(NN), "pre": _sb(NL), "fr": _sb(NL), "tb": _sb(1248), "pos": _sb(648),
-    "so": _sb(8192), "sm": _sb(1024), "si": _sb(1024, I32), "off": _sb(1024, U16),
-    "sop": _sb(NN), "paye": _sb(NN), "scat": _sb(NN), "cnt": _sb(NT), "lqr": _sb(NL), "num": _sb(NL),
-    "pay0": _sb(NL), "pays": _sb(NL), "sort0": _sb(NL), "sort1": _sb(96), "ulo": _sb(NT), "um": _sb(NL), "uh": _sb(NL),
-    "bt": _sb(960), "b1": _sb(480), "g1": _sb(480), "ss": _sb(NN), "ft": _sb(456), "lpr": _sb(96), "num1": _sb(96),
-    "pay1": _sb(96), "pay1s": _sb(96), "ab0": _sb(672), "ab1": _sb(336), "dc0": _sb(192), "dc1": _sb(96),
-    "fb": _sb(NL), "kido": _sb(NN), "yo": _sb(NN), "lst0": _sb(48, U16),
+    "ih0": _sb(1536, BF), "ih1": _sb(768, BF), "vb0": _sb(384, BF), "vb1": _sb(192, BF), "alt": _sb(768, BF),
+    "c16": _sb(NN, BF), "c4": _sb(NL, BF), "cj": _sb(96, BF), "cst": _sb(192), "csi": _sb(32, I32),
+    "rp": _sb(448), "id4": _sb(NL), "slot": _sb(NN, BF), "zz": _sb(640, BF), "w": _sb(9 * 512, BF), "pos": _sb(448, BF),
+    "tb": _sb(2 * NT, BF), "ch": _sb(976), "ix": _sb(448), "sx": _sb(NN), "sz": _sb(2 * NT), "een": _sb(NL),
+    "pay": _sb(NN), "sc": _sb(NN), "ss": _sb(NN), "ol": _sb(NL), "lqr": _sb(NL, BF), "num": _sb(NL, BF), "pay0": _sb(NL),
+    "sort0": _sb(NL), "sort1": _sb(96), "rm": _sb(2 * NT), "kf": _sb(96), "fa": _sb(NL, BF), "fb": _sb(NL, BF),
+    "ft0": _sb(NI + NB, BF), "ft1": _sb(NI + NB, BF), "gone": _sb(NL, BF), "lo": _sb(NL, BF), "ta": _sb(NT, BF),
+    "par": _sb(NL, BF), "asz": _sb(NT, BF), "bt": _sb(1024, BF), "b1": _sb(480, BF), "g1": _sb(480, BF), "ss1": _sb(NN, BF),
+    "lp1": _sb(96, BF), "num1": _sb(96, BF), "p1s": _sb(96), "pay1": _sb(96), "ab0": _sb(1248), "ab1": _sb(832),
+    "so": _sb(4096), "sh": _sb(6144, F16), "sm": _sb(768), "si": _sb(768, I32), "off": _sb(1024, U16),
+    "kido": _sb(NN), "yo": _sb(NN),
     "ps": ("psum", [128, 4096], F32),
 }
 SEMAPHORES = ["e%d" % i for i in range(140)] + ["ax", "al", "ag", "sent"]
-CY = 1.04
 
 
 def V(n, a, b, s=1):
     return (n, a, b, s)
-
-
-def IT(a, b):
-    return ("sk", NT + a, NT + b, 1)
 
 
 def _len(v):
@@ -86,7 +67,7 @@ def _meet(x, y):
 
 def build(T, topo, core, rank):
     ops = []
-    used = {"sm": 0, "si": 0, "off": 0, "so": 0}
+    used = {"sm": 0, "si": 16, "off": 0, "so": 0, "sh": 0}
 
     def new(n, k):
         a = used[n]
@@ -105,7 +86,7 @@ def build(T, topo, core, rank):
         return T[v[0]][:, v[1]:v[2]:v[3]]
 
     def two(*vs):
-        return all(SCRATCH[v[0]][2] in (BF, U16) for v in vs)
+        return all(SCRATCH[v[0]][2] in (BF, U16, F16) for v in vs)
 
     def add(eng, fn, outs, ins, cost, lat=0.0, kind="c", after=()):
         r, w = [], []
@@ -148,13 +129,25 @@ def build(T, topo, core, rank):
     def lin(out, in0, m, c):
         return ts(out, in0, m, A.mult, c, A.add)
 
+    def plus(out, in0, c):
+        return ts(out, in0, c, A.add)
+
+    def whole(out, d, m):
+        return ts(out, d, K, A.add, float(m), A.mult)
+
+    def bits(out, in0, shift, mask):
+        if shift:
+            return ts(out, in0, shift, A.logical_shift_right, mask, A.bitwise_and)
+        return ts(out, in0, mask, A.bitwise_and)
+
     def tt(out, a, b, o):
         n = _len(out)
         return add("v", lambda q: q.tensor_tensor(ap(out), ap(a), ap(b), o), [out], [a, b], vcost(out, a, n, 2 * n))
 
     def cp(out, in0):
         n = _len(in0) if len(out) == 2 else _len(out)
-        return add("v", lambda q: q.tensor_copy(ap(out), ap(in0)), [out], [in0], vcost(out, in0, n, n))
+        c = vcost(out, in0, n, n / 2 if len(in0) > 2 and len(out) > 2 and two(out, in0) else n)
+        return add("v", lambda q: q.tensor_copy(ap(out), ap(in0)), [out], [in0], c)
 
     def ms(out, c):
         n = _len(out)
@@ -162,20 +155,28 @@ def build(T, topo, core, rank):
 
     def act(out, in0, scale=1.0, bias=0.0, fn=AF.Identity):
         n = _len(out)
-        c = 65 + (1.56 if len(in0) == 2 else 1.0) * CY * n
+        c = 65 + 1.56 * CY * n if len(in0) == 2 else max(64, n) * CY + 30
         if fn == AF.Identity and scale == 1.0 and bias == 0.0:
             return add("s", lambda q: q.activation(ap(out), ap(in0), AF.Copy), [out], [in0], c)
-        return add("s", lambda q: q.activation(ap(out), ap(in0), fn, bias=bias, scale=scale), [out], [in0], c)
+        return add("s", lambda q: q.activation(ap(out), ap(in0), fn, bias=sc(bias), scale=scale), [out], [in0, bias], c)
+
+    def get(eng, out, src, scale=1.0, bias=0.0):
+        if eng == "s":
+            return act(out, src, scale, bias)
+        if scale == 1.0 and bias == 0.0:
+            return cp(out, src)
+        return lin(out, src, scale, bias)
 
     def scan(out, d0, d1, init, o0, o1):
+        n = _len(out)
         return add("v", lambda q: q.tensor_tensor_scan(ap(out), ap(d0), ap(d1), init, o0, o1), [out], [d0, d1],
-                   max(64, _len(out)) * CY)
+                   max(64, n / 2 if two(out, d0, d1) else n) * CY)
 
-    def deal(src, blk=16):
+    def deal(src, blk=16, pat=None):
         n = _len(src)
-        o = new("so", n)
-        scan(o, src, V("c16" if blk == 16 else "c4", 0, n), 0.0, A.max, A.mult)
-        return V("so", o[1] + blk - 1, o[2], blk)
+        o = new("sh" if two(src) else "so", n)
+        scan(o, src, pat or V("c16" if blk == 16 else "c4", 0, n), -2 * K, A.max, A.add)
+        return V(o[0], o[1] + blk - 1, o[2], blk)
 
     def iota(out, pat, base, ch=0):
         if SCRATCH[out[0]][2] == I32:
@@ -187,19 +188,19 @@ def build(T, topo, core, rank):
         return iota(out, [[0, _len(out)]], c)
 
     def ramp(out, base, step=1.0):
-        return act(out, IT(0, _len(out)), step, base - 504.0 * step)
+        return act(out, V("rp", 0, _len(out)), float(step), float(base))
 
     def quant(q, s, a, b, src):
         o, p = V(q, a, b), V(s, a, b)
-        return add("v", lambda e: e.quantize_mx(ap(o), ap(p), ap(src)), [o, p], [src], 12 + 0.22 * 4 * (b - a))
+        return add("v", lambda e: e.quantize_mx(ap(o), ap(p), ap(src)), [o, p], [src], 1.25 * (12 + 0.22 * 4 * (b - a)))
 
     def mm(bank, lq, ls, la, rq, rs, a, b):
         o, i = V("ps", 512 * bank, 512 * bank + b - a), [V(lq, la, la + 128), V(ls, la, la + 128), V(rq, a, b), V(rs, a, b)]
-        add("t", lambda e: e.matmul_mx(ap(o), ap(i[0]), ap(i[1]), ap(i[2]), ap(i[3]), True, True), [o], i, (b - a + 16) * 0.7)
+        add("t", lambda e: e.matmul_mx(ap(o), ap(i[0]), ap(i[1]), ap(i[2]), ap(i[3]), True, True), [o], i, (b - a + 16) * 0.6)
         return o
 
-    def dma(eng, out, in_, outs, ins, nbytes):
-        return add(eng, lambda e: e.dma_start(out, in_), outs, ins, 60, 1700 + nbytes / 150.0, "d")
+    def dma(eng, out, in_, outs, ins, lat, after=()):
+        return add(eng, lambda e: e.dma_start(out, in_), outs, ins, 60, lat, "d", after)
 
     def u8(v):
         return ap(v).bitcast(dt.uint8) if SCRATCH[v[0]][2] == C4X else ap(v)
@@ -213,94 +214,82 @@ def build(T, topo, core, rank):
         count[sem] = count.get(sem, 0) + n
         count["sent"] = count.get("sent", 0) + n
         return add("g", lambda e: e.remote_dma(u8(out), u8(in_), T.sem[sem], T.sem["sent"], pid, rid, topo.mask(core, dst)),
-                   [], [in_], 150, 0.0, "r")
+                   [], [in_], 300, 0.0, "r")
 
     def arrive(sem, outs, sends, lat):
         i = add("a", None, outs, [], 0.0, lat, "a", sends)
         ops[i]["sem"] = (sem, count[sem])
+        return i
 
     peer = [T.cores[rank ^ 1], T.cores[rank ^ 2]]
 
-    dma("y", T.xin[:, 768:1536], T.x[:, 768:1536], [V("xin", 768, 1536)], [], 196608)
-    dma("s", T.uin[:], T.u[:], [V("uin", 0, 512)], [], 131072)
-    dma("y", T.kw[:, 0:12], T.ka[:], [V("kw", 0, 12)], [], 6144)
-    dma("y", T.kw[:, 12:24], T.kb[:], [V("kw", 12, 24)], [], 6144)
-    dma("y", T.xin[:, 0:768], T.x[:, 0:768], [V("xin", 0, 768)], [], 196608)
-    dma("y", T.wq[:].bitcast(dt.uint8), T.wc[:], [V("wq", 0, 512)], [], 262144)
-    dma("y", T.wsc[:], T.ws[:], [V("wsc", 0, 512)], [], 65536)
-    dma("y", T.vin[:], T.v[:], [V("vin", 0, 512)], [], 131072)
+    dma("y", T.kw[:, 0:12], T.ka[:], [V("kw", 0, 12)], [], 1900)
+    dma("s", T.kw[:, 12:24], T.kb[:], [V("kw", 12, 24)], [], 2100)
+    dma("y", T.uin[:], T.u[:], [V("uin", 0, 512)], [], 2700)
+    dma("y", T.xin[:, 768:1536], T.x[:, 768:1536], [V("xin", 768, 1536)], [], 3400)
+    xl = dma("y", T.xin[:, 0:768], T.x[:, 0:768], [V("xin", 0, 768)], [], 4100)
+    dma("y", T.wq[:].bitcast(dt.uint8), T.wc[:], [V("wq", 0, 512)], [], 3000, [xl])
+    dma("y", T.wsc[:], T.ws[:], [V("wsc", 0, 512)], [], 3300, [xl])
+    dma("y", T.vin[:], T.v[:], [V("vin", 0, 512)], [], 3800, [xl])
 
-    iota(IT(0, NT), [[1, NT]], 504)
-    pi, pc = V("csi", 0, 1), V("cst", 0, 5)
+    pi, pc = V("csi", 0, 1), V("cst", 0, 8)
     iota(pi, [[1, 1]], 0, 1)
-    ts(V("csi", 2, 3), pi, 15, A.bitwise_and)
-    ts(V("csi", 3, 4), pi, 2, A.logical_shift_right, 3, A.bitwise_and)
-    ts(V("csi", 4, 5), pi, 3, A.bitwise_and)
+    bits(V("csi", 2, 3), pi, 0, 15)
+    bits(V("csi", 3, 4), pi, 2, 3)
+    bits(V("csi", 4, 5), pi, 0, 3)
     cp(V("cst", 0, 3), V("csi", 2, 5))
-    p16, p4, pt, pt768, ptm = [sub(pc, i, i + 1) for i in range(5)]
-    ts(pt768, pt, 768.0, A.add)
-    ts(ptm, pt, -2048.0, A.add)
-    j16, j4 = V("cst", 8, 24), V("cst", 24, 40)
-    iota(j16, [[1, 16]], 0)
-    iota(j4, [[0, 4], [1, 4]], 0)
-    for c, j, p, blk, t0, top in (("c16", j16, p16, 16, 40, NN), ("c4", j4, p4, 4, 72, NL)):
-        ge, eq = V("cst", t0, t0 + 16), V("cst", t0 + 16, t0 + 32)
-        ts(ge, j, p, A.is_ge)
-        ts(eq, j, p, A.is_equal)
-        tt(V(c, 0, 16), ge, eq, A.add)
-        ts(V(c, blk - 1, 16, blk), V(c, blk - 1, 16, blk), 0.25, A.mult)
+    p16, p4, pt, ptp, ptk, ptj, pb, p32 = [sub(pc, i, i + 1) for i in range(8)]
+    pk = V("cst", 176, 177)
+    for out, src, m, c in ((ptp, pt, 1, 4 * (NL - NB)), (ptk, pt, 1, 4 * K), (ptj, pt, 1, 8 * K - 4 * NB), (pb, pt, 2, 1025),
+                           (p32, p16, 2, 0), (pk, p16, 1, K)):
+        act(out, src, float(m), float(c))
+    j16, j4 = V("cst", 8, 40), V("cst", 40, 72)
+    iota(j16, [[1, 2], [1, 16]], 0)
+    iota(j4, [[1, 2], [0, 4], [1, 4]], 0)
+    for c, j, p, blk, top in (("c16", j16, p16, 16, NN), ("c4", j4, p4, 4, NL)):
+        ts(j, j, p, A.is_equal, K, A.mult)
+        tt(V(c, 0, 16), sub(j, 0, 16), sub(j, 16, 32), A.subtract)
+        plus(V(c, blk - 1, 16, blk), V(c, blk - 1, 16, blk), -2 * K)
         n = 16
         while n < top:
             k = min(n, top - n)
-            cp(V(c, n, n + k), V(c, 0, k))
+            act(V(c, n, n + k), V(c, 0, k))
             n += k
-    ms(V("m2", 0, NN), -2.0)
-    k16, awr, kwh, nodeh, awl = V("cst", 104, 116), V("cst", 116, 128), V("cst", 128, 134), V("cst", 136, 148), V("cst", 148, 160)
-    iota(k16, [[16, 12]], 0)
-    ts(k16, k16, p16, A.add, 0.5, A.mult)
-    ts(awr, k16, (SIB - 512) / 2.0, A.add)
-    ts(awl, k16, (SIB + 768) / 2.0, A.add)
-    ts(kwh, sub(k16, 0, 6), -256.0, A.add)
-    ts(nodeh, k16, (NL + 512) / 2.0, A.add)
+    own, kidc, tsp = V("cst", 104, 128), V("cst", 128, 140), V("cst", 152, 176)
+    for out, pat, base, p in ((own, [[SB, 2], [16, 12]], NL, p16), (kidc, [[16, 12]], NB, p16), (tsp, [[32, 24]], 0, p32)):
+        iota(out, pat, base)
+        act(out, out, 1.0, p)
+    iota(V("rp", 0, 112), [[1, 112]], 0)
+    for a in (112, 224):
+        ramp(V("rp", a, 2 * a), a)
+    ramp(V("slot", 0, NL), -NL)
+    ramp(V("slot", NL, NN), SB - NL)
+    ramp(V("zz", NL + 1, 640), NL + 1 - NN)
+    ms(V("zz", NL, NL + 1), -256.0)
+    ms(V("tb", 0, NB), 0.0)
+    ms(V("tb", NT - 1, NT), 0.0)
+    for k in range(9):
+        if k < ON["gw"]:
+            ramp(V("w", 512 * k, 512 * k + 128), 2 ** k - 256)
+        else:
+            iota(V("w", 512 * k, 512 * k + 128), [[1, 128]], 2 ** k - 256)
     iota(V("csi", 8, 16), [[16, 8]], 0)
     ou = new("off", 8)
     cp(ou, V("csi", 8, 16))
-    ms(V("hv", 0, 200), 0.0)
-    ramp(V("hv", 200, NT), PB + NL)
-    ms(V("hn", 0, 200), 4096.0)
-    ramp(V("hn", 200, NT), -(PB + NL), -1.0)
-    fill(V("leaf", 0, 8), 2)
-    fill(V("leaf", 8, 200), 3)
-    fill(V("leaf", 200, NT), 2)
-    act(V("sk", 0, NT), IT(0, NT))
-    ramp(V("val", NL, NN), PB)
-    ramp(V("slot", 0, NL), 512)
-    ramp(V("slot", NL, NN), 768)
-    act(V("kf", 0, 96), IT(9, 105), 1.0 / 1024, -0.5)
-    ms(V("w", WOFF[0] + NL - 1, WOFF[0] + NL), float(PB + NN))
-    for k in range(9):
-        n = min(128, max(8, 2 ** k))
-        ramp(V("w", WOFF[k] + NN, WOFF[k] + NN + n), PB + NN + 2 ** k)
-    fill(V("tb", 0, 8), 512)
-    fill(V("tb", 391, NT), 767)
-    fill(V("tb", SIB + NL, SIB + 256), 512)
-    fill(V("tb", HOLE, JUNK), 511)
-    fill(V("pos", 0, 200), 1408)
-    fill(V("pos", 200 + NL, 456), 1408)
-    ms(V("cnt", 0, 1), M0 + 0.5)
-    fill(V("ulo", 0, 8), int(M1))
-    fill(V("bt", NL, 256), 0)
-    fill(V("bt", 448, 512), 0)
-    fill(V("ft", 0, 200), 0)
-    fill(V("ft", 391, 456), 0)
-    fill(V("fz", 0, SIB + 256), 512)
-    fill(V("fz", SIB + 256, HOLE), 512 + NT)
-    fill(V("f0", 384, 512), 0)
-    fill(V("f1", NL, 512), 0)
-    fill(V("h0", 0, 4), 0)
-    fill(V("h1", 0, 4), 0)
-    ms(V("zero", 0, 512), 0.0)
-    quant("gq", "gs", 48, 176, V("zero", 0, 512))
+    for name, a, b, c in (("fa", NL - 1, NL, 0), ("ft0", 0, NB, 0), ("ft0", NI, NI + NB, 0), ("ft1", 0, NB, 0), ("ft1", NI - 1, NI + NB, 0),
+                          ("ix", NL, SB, 2 * NT - 1), ("pos", NL, SB, 0), ("sz", 0, NB - 1, 0), ("sz", NT, NT + NB - 1, 0),
+                          ("si", 0, 16, 0), ("ch", 0, NB, 0), ("ch", NI, NB + SB, 0), ("ch", NI + SB, 976, NB - 1),
+                          ("asz", 0, NB, 0), ("bt", 0, NB, 0), ("bt", NI, NB + SB, 0), ("bt", NI + SB, 512, 0),
+                          ("f0", NN, 512, 0), ("f1", NL, 512, 0), ("zero", 0, NN, 0)):
+        fill(V(name, a, b), c)
+    iota(V("id4", 0, NL), [[4, NL]], 3)
+    iota(V("rm", 0, 2 * NT), [[0, 2], [-1, NT]], 0)
+    ramp(V("kf", 0, 96), 0.25, -1 / 512.0)
+    iota(V("ta", 0, NT), [[1, NT // 4], [0, 4]], 0)
+    iota(V("par", 0, NL), [[0, NL // 2], [-1, 2]], 1)
+    iota(V("alt", 0, 768), [[0, 384], [1, 2]], 0)
+    act(V("cj", 0, 96), V("c16", 0, 96))
+    tt(V("cj", 15, 96, 16), V("c16", 15, 96, 16), V("rp", 0, 96, 16), A.add)
     ms(V("z", 0, 520), 0.0)
     ms(V("one", 0, 128), 1.0)
     add("g", lambda q: q.affine_select(T.z[:, 4:516:4], T.one[:], [[-1, 128]], A.is_equal, 0.0, 0, 1),
@@ -308,99 +297,102 @@ def build(T, topo, core, rank):
     for b in range(4):
         quant("eq", "es", 128 * b, 128 * b + 128, V("z", 4 - b, 516 - b))
 
+    kw = V("kw", 0, 24)
+    oc = new("off", 24)
+    plus(oc, kw, float(NB))
+    m_, t_, y_, oz = new("sm", 24), new("sm", 24), new("sm", 24), new("off", 24)
+    ts(m_, kw, float(NL), A.is_ge, float(SB + NL), A.mult)
+    tt(t_, kw, m_, A.add)
+    tt(y_, t_, own, A.max)
+    plus(sub(oz, 12, 24), sub(y_, 12, 24), -float(NL + SB))
+    plus(sub(oz, 0, 12), sub(y_, 0, 12), -float(NL))
+    cp((V("tb", 0, NT - 1), oc), V("slot", 0, NN))
+    act(V("zz", 0, NL), (V("zz", SB, 640), sub(oz, 12, 24)))
+    act(V("w", 320, 512), (V("zz", 0, 640), sub(oz, 0, 12)))
+    osl = new("off", 24)
+    oin, olf = sub(osl, 0, 12), sub(osl, 12, 24)
+    plus(oin, deal(V("tb", NI, NT)), K + NL)
+    act(V("w", 128, 320), (V("zz", 0, 448), oin))
+    plus(olf, deal(V("tb", NB, NI)), K + NL)
+    for h in range(2):
+        get(ON["ch"][h], V("ch", NB + SB * h, NI + SB * h), (V("rp", 0, NT), sub(oc, 12 * h, 12 * h + 12)))
+
     quant("uq", "us", 0, 128, V("uin", 0, 512))
     add("v", lambda q: q.tensor_copy(T.uq2[:].bitcast(dt.uint32), T.uq[:].bitcast(dt.uint32).indirect(ap(ou))),
         [V("uq2", 0, 128)], [V("uq", 0, 128), ou], 50 + 200 * CY)
     add("s", lambda q: q.activation(T.us2[:], T.us[:].indirect(ap(ou)), AF.Copy),
         [V("us2", 0, 128)], [V("us", 0, 128), ou], 65 + 200 * CY)
-    quant("vq", "vs", 0, 128, V("vin", 0, 512))
-
-    def unpack(q, s, dst, scale, b0=0):
-        for b in range(4):
-            o = mm(b0 + b, "eq", "es", 128 * b, q, s, 0, NN)
-            act(V(dst, b, 1536, 4), o, scale)
-
     quant("q0", "s0", NL, NN, V("xin", 768, 1536))
     p0 = mm(4, "uq2", "us2", 0, "q0", "s0", NL, NN)
     quant("q0", "s0", 0, NL, V("xin", 0, 768))
-    sx = [send(peer[0], V("lq", 0, NN), V("q0", 0, NN), "ax"), send(peer[0], V("ls", 0, NN), V("s0", 0, NN), "ax")]
-    arrive("ax", [V("lq", 0, NN), V("ls", 0, NN)], sx, 9000)
-    unpack("q0", "s0", "xa", 1.0)
-    ka, kb = V("kw", 0, 12), V("kw", 12, 24)
-    d, gz, d2, ca, cb = [new("sm", 12) for _ in range(5)]
-    tt(d, kb, ka, A.subtract)
-    ts(gz, kb, 0.0, A.is_ge, 2.0, A.mult)
-    tt(d2, d, gz, A.mult)
-    tt(ca, ka, d2, A.subtract)
-    tt(cb, kb, d2, A.add)
-    ts(V("fr", 0, NL), p0, 0.0, A.is_gt, 2.0, A.add)
-    fw = deal(V("fr", 0, NL))
-    t, kn = new("sm", 12), new("sm", 24)
-    tt(t, fw, d2, A.mult)
-    tt(sub(kn, 12, 24), cb, t, A.subtract)
-    tt(sub(kn, 0, 12), ca, t, A.add)
-    oc = new("off", 24)
-    ts(oc, kn, 8.0, A.add)
-    ocl, ocr = sub(oc, 0, 12), sub(oc, 12, 24)
-    tt(V("val", 0, NL), (V("hv", 0, NT), ocr), V("val", NL, NN), A.max)
-    tt(V("pre", 0, NL), (V("hn", 0, NT), ocl), V("val", 0, NL), A.min)
-    act(V("w", WOFF[0] + NL, WOFF[0] + NN), V("pre", 0, NL), fn=AF.Abs)
-    cp((V("w", 0, WOFF[0] + NL - 1), oc), V("val", 0, NN))
-    for h in range(4):
-        cp((V("tb", 0, 391), sub(oc, 6 * h, 6 * h + 6)), V("slot", 96 * h, 96 * h + 96))
-    act(V("tb", SIB, SIB + NL), (IT(0, NT), ocr))
-    act(V("tb", SIB + 256, SIB + 256 + NL), (IT(0, NT), ocl))
-    act(V("sop", 0, NL), V("tb", 200, NT), 1.0 / 4096, -0.125)
-    act(V("sop", NL, NN), V("tb", 200, NT), 1.0 / 4096)
-    tt(V("paye", 0, NL), (V("leaf", 0, NT), ocl), V("sop", 0, NL), A.add)
-    tt(V("paye", NL, NN), (V("leaf", 0, NT), ocr), V("sop", NL, NN), A.add)
-    act(V("pays", 0, NL), V("tb", 8, 200), 256.0, -512.0)
-    tt(V("pay0", 0, NL), V("pays", 0, NL), IT(8, 200), A.add)
-    oev = new("off", 12)
-    lin(oev, deal(V("tb", 8, 200)), 2.0, -312.0)
+    lq, ls = V("lq", 48, 48 + NN), V("ls", 48, 48 + NN)
+    arrive("ax", [lq, ls], [send(peer[0], lq, V("q0", 0, NN), "ax"), send(peer[0], ls, V("s0", 0, NN), "ax")], 9000)
+    quant("vq", "vs", 0, 128, V("vin", 0, 512))
+
+    def unpack(q, s, a, b0, *outs):
+        for b in range(4):
+            o = mm(b0 + b, "eq", "es", 128 * b, q, s, a, a + NN)
+            for dst, scale in outs:
+                act(V(dst, b, 1536, 4), o, scale)
+
+    unpack("q0", "s0", 0, 0, ("xa", 1.0))
+    ts(V("fa", 0, NL - 1), sub(p0, 0, NL - 1), 0.0, A.is_gt, float(NT), A.mult)
+    unpack("lq", "ls", 48, 4, ("th", 0.5))
+    get(ON["fb"], V("fb", 0, NL), V("fa", 0, NL), -1.0, float(NT))
+    tt(V("ix", SB, SB + NL), (V("rp", 0, NT), sub(oc, 0, 12)), V("fa", 0, NL), A.add)
+    tt(V("ix", 0, NL), (V("rp", 0, NT), sub(oc, 12, 24)), V("fb", 0, NL), A.add)
+    act(V("ft0", NB, NI), V("fa", 0, NL), fn=AF.Sign)
+    osx = new("off", 24)
+    for h in range(2):
+        get(ON["sx"], V("sx", NL * h, NL * h + NL), (V("ix", 0, 448), sub(osl, 12 * h, 12 * h + 12)))
+        plus(sub(osx, 12 * h, 12 * h + 12), deal(V("sx", NL * h, NL * h + NL)), K)
+    szw = V("sz", 0, 2 * NT)
+    get(ON["sz"][0], V("sz", NT + NB - 1, 2 * NT), V("tb", NB - 1, NT), 1 / 1024.0, NI / 1024.0 - 3)
+    get(ON["sz"][1], V("sz", NB - 1, NI), V("tb", NB - 1, NI), 1 / 1024.0, (NI + 512) / 1024.0 - 1)
+    get(ON["sz"][2], V("sz", NI, NT), V("tb", NI, NT), 1 / 1024.0, (NI + 512) / 1024.0)
+    tt(V("pay0", 0, NL), (szw, sub(osx, 12, 24)), V("id4", 0, NL), A.add)
+
     op = None
-    for k in range(9):
-        win = V("w", WOFF[k], WOFF[k] + NN + min(128, max(8, 2 ** k)))
-        if k < 8:
-            op = new("off", 24)
-            for h in (1, 0) if k == 0 else (0, 1):
-                lin(sub(op, 12 * h, 12 * h + 12), deal(V("w", WOFF[k] + NL * h, WOFF[k] + NL * h + NL)), 2.0, float(-PB))
-        for h in (0, 1):
-            if k < 8:
-                o = V("w", WOFF[k + 1] + NL * h, WOFF[k + 1] + NL * h + NL)
-            else:
-                o = V("pos", 456 - 256 * h, 456 - 256 * h + NL)
-            src = (win, sub(op, 12 * h, 12 * h + 12))
-            if k >= 8 and h == 1:
-                cp(o, src)
-            else:
-                act(o, src)
-    pw = V("pos", 0, 648)
+    for k in range(8):
+        win = V("w", 512 * k, 512 * k + 512)
+        op = new("off", 24)
+        nv = ON["jv"][k] if k < 7 else 12
+        cuts = [0, nv, (24 + nv) // 4 * 2, 24] if 0 < nv < 12 else [0, 12, 24]
+        parts = list(zip(cuts, cuts[1:]))[::-1]
+        for a, b in parts:
+            plus(sub(op, a, b), deal(V("w", 512 * k + 128 + 16 * a, 512 * k + 128 + 16 * b)), K + 256)
+        for a, b in parts:
+            get("v" if b == nv else "s", V("w", 512 * k + 640 + 16 * a, 512 * k + 640 + 16 * b), (win, sub(op, a, b)))
+    win = V("w", 512 * 8, 512 * 9)
+    oex, oen = sub(op, 0, 12), sub(op, 12, 24)
+    tt(V("een", 0, NL), (win, oen), V("sz", NI, NT), A.subtract)
+    tt(V("sz", NI, NT), (win, oex), V("een", 0, NL), A.subtract)
+    act(V("pos", 0, NL), (win, oen))
+    act(V("pos", SB, SB + NL), (win, oex), 1.0, -1.0)
     opos = new("off", 24)
-    lin(sub(opos, 0, 12), deal(V("pos", 200, NT)), 2.0, -1408.0)
-    dpost = deal(V("pos", 456, 648))
-    lin(sub(opos, 12, 24), dpost, 2.0, -1408.0)
-    ohi = new("off", 12)
-    lin(ohi, dpost, 2.0, -1407.0)
-    act(V("lqr", 0, NL), (pw, oev))
+    den, dex = deal(V("pos", 0, NL)), deal(V("pos", SB, SB + NL))
+    plus(sub(opos, 0, 12), den, K + 256)
+    plus(sub(opos, 12, 24), dex, K + 257)
+    get(ON["pay"][0], V("pay", 0, NL), (szw, sub(osx, 0, 12)), 0.5, 1.5)
+    get(ON["pay"][1], V("pay", NL, NN), (szw, sub(osx, 0, 12)), -0.5, -1.5)
+    cp((V("sc", 0, NN), opos), V("pay", 0, NN))
+    act(V("ol", 0, NL), (szw, sub(osx, 12, 24)), 0.5, 1 - M)
+    act(V("lqr", 0, NL), (V("pos", 0, 448), olf))
     olq = new("off", 12)
-    lin(olq, deal(V("lqr", 0, NL)), 2.0, -1408.0)
-    cp((V("scat", 0, NN), opos), V("paye", 0, NN))
-    scan(V("cnt", 1, 385), V("scat", 0, NN), V("m2", 0, NN), M0 + 0.5, A.add, A.add)
-    cw = V("cnt", 0, 385)
-    act(V("num", 0, NL), (cw, olq))
+    plus(olq, deal(V("lqr", 0, NL)), K + 256)
+    scan(V("ss", 0, NN), V("sc", 0, NN), V("c16", 0, NN), M, A.add, A.max)
+    tt(V("num", 0, NL), (V("ss", 0, NN), olq), V("ol", 0, NL), A.add)
     onum = new("off", 12)
-    lin(onum, deal(V("num", 0, NL)), 2.0, -(M0 + 0.5))
+    plus(onum, deal(V("num", 0, NL)), K)
     cp((V("sort0", 0, NL), onum), V("pay0", 0, NL))
-    unpack("lq", "ls", "th", 0.5, 4)
 
     def fold_lists(sort, m, lst):
         e = m // 8
         i4, l4, q4 = new("si", e), new("si", e), new("si", e)
-        lin(i4, deal(V(sort, 1, m, 2), 4), 2.0, -131072.0)
-        ts(q4, i4, 8, A.logical_shift_right, 255, A.bitwise_and)
-        ts(l4, i4, 255, A.bitwise_and)
-        lin(sub(lst, e, 2 * e), q4, 4.0, pt768)
+        whole(i4, deal(V(sort, 1, m, 2), 4), 1024)
+        bits(q4, i4, 0, 255)
+        bits(l4, i4, 12, 255)
+        lin(sub(lst, e, 2 * e), q4, 4.0, ptp)
         lin(sub(lst, 0, e), l4, 4.0, pt)
 
     def fold(win, lst, e, tmp, out):
@@ -412,160 +404,232 @@ def build(T, topo, core, rank):
     def rake(r, sort, m, x):
         n, c, e = m // 2, m // 32, m // 8
         c2 = c + c % 2
-        ab = "ab%d" % r
-        i16, s16, par = new("si", c), new("si", c), new("si", c)
-        lin(i16, deal(V(sort, 1, m, 2)), 2.0, -131072.0)
-        ts(par, i16, 8, A.logical_shift_right, 255, A.bitwise_and)
-        ts(s16, i16, 8, A.logical_shift_right)
-        opar, osib = new("off", c), new("off", c)
-        ts(opar, par, 200.0, A.add)
-        ts(osib, s16, float(SIB), A.add)
-        act(V(ab, 0, n), (V("tb", 0, NT), opar))
-        tt(V(ab, n, 2 * n), (V("tb", 0, HOLE), osib), V("kf", 0, n), A.add)
-        act(V(ab, 2 * n, 3 * n), (V("fz", 0, HOLE), osib))
-        cp((V("sk", 0, NT), opar), V(ab, n, 2 * n))
-        oa = deal(V(ab, 0, 3 * n))
-        ia, gp, t1, t2 = new("si", 3 * c), new("si", c), new("sm", c), new("sm", c)
-        lin(ia, oa, 2.0, -512.0)
-        ts(gp, sub(ia, 0, c), 255, A.bitwise_and)
-        sib, zz = sub(ia, c, 2 * c), sub(ia, 2 * c, 3 * c)
-        tt(t1, gp, zz, A.add)
-        tt(t2, sib, zz, A.subtract)
-        og, ob = new("off", 2 * c), new("off", 2 * c)
-        ts(sub(og, 0, c), t1, 200.0, A.add)
-        ts(sub(og, c, 2 * c), t2, 8.0 + NT, A.add)
-        act(V(ab, 5 * n, 7 * n), (V("sk", 0, 2 * NT), og))
-        o = deal(V(ab, 5 * n, 7 * n), 4)
-        os_, opre, otg = new("off", e), new("off", e), new("off", e)
-        lin(os_, sub(o, e, 2 * e), 8.0, ptm)
-        act(V("ts%d" % r, 0, 4 * n), (V(x, 0, 1536), os_))
-        ii, jj, cc, tg = new("si", 2 * e), new("si", 2 * e), new("sm", e), new("sm", e)
-        ts(ii, o, 2048.0, A.mult)
-        ts(jj, ii, 1023, A.bitwise_and)
-        lin(opre, sub(jj, e, 2 * e), 4.0, pt)
-        ts(cc, sub(jj, 0, e), 0.0, A.is_gt, float(NL), A.mult)
-        tt(tg, sub(o, e, 2 * e), cc, A.add)
-        lin(otg, tg, 8.0, ptm)
+        n2, ab, ih = 16 * c2, "ab%d" % r, "ih%d" % r
+        part = [V(ab, n2 * i, n2 * i + n2) for i in range(13)]
+        col = lambda v, i, k=1: sub(v, c2 * i, c2 * (i + k))
+        i0, o0 = V("si", 0, 16) if r else new("si", 4 * c2), new("off", 2 * c2)
+        whole(sub(i0, 0, c), deal(V(sort, 1, m, 2)), 1024)
+        bits(col(i0, 1), col(i0, 0), 0, 255)
+        bits(col(i0, 2), col(i0, 0), 0, 511)
+        bits(col(i0, 3), col(i0, 0), 9, 1)
+        cp(o0, col(i0, 1, 2))
+        opar, osib = col(o0, 0), col(o0, 1)
+        act(part[0], (V("tb", NL, NT), opar), 1.0, float(NL))
+        act(part[1], (V("ch", 0, 480), osib), 1.0, -float(NB))
+        tt(part[12], (V("ch", 0, 480), osib), V("kf", 0, n2), A.add)
+        cp((V("rm", NL, NT), sub(opar, 0, c)), sub(part[12], 0, n))
+        i1, o1, ra = new("si", 6 * c2), new("off", 5 * c2), new("sm", 2 * c2)
         if r == 0:
-            ts(sub(ob, 0, c), gp, 200.0, A.add)
-            ts(sub(ob, c, 2 * c), sib, 8.0, A.add)
-            act(V(ab, 3 * n, 5 * n), (V("sk", 0, NT), ob))
+            plus(col(i1, 0, 2), deal(V(ab, 0, 2 * n2)), K)
+            right = col(i0, 3)
         else:
-            ts(sub(ob, 0, c), sib, 8.0, A.add)
-            act(V(ab, 4 * n, 5 * n), (V("sk", 0, NT), sub(ob, 0, c)))
-        dc = "dc%d" % r
-        act(V(dc, n, 2 * n), V(ab, 4 * n, 5 * n), 1.0, M1)
-        act(V(dc, 0, n), V(dc, n, 2 * n), 1.0, -M1)
-        i2, i3, oct_ = new("si", c2), new("si", c2), new("off", c2)
-        lin(sub(i2, 0, c), sub(oa, 0, c), 2.0, -256.0)
-        ts(sub(i3, 0, c), sub(i2, 0, c), 511, A.bitwise_and)
-        ts(sub(oct_, 0, c), sub(i3, 0, c), float(SIB), A.add)
-        cp((V("tb", 0, HOLE), sub(oct_, 0, c)), V(dc, 0, n))
+            act(part[2], (V("ft0", 0, NI + NB), opar))
+            act(part[3], (V("ft1", 0, NI + NB), opar))
+            d1, r1, right = deal(V(ab, 0, 4 * n2)), new("sm", c2), new("sm", c2)
+            plus(col(i1, 0, 3), col(d1, 0, 3), K)
+            tt(r1, col(d1, 2), col(d1, 3), A.not_equal)
+            tt(right, r1, col(i0, 3), A.not_equal)
+        get("s" if r else "v", col(ra, 0), right, float(NT), float(NL))
+        get("s" if r else "v", col(ra, 1), right, -float(NT), float(NT))
+        g0 = 2 if r == 0 else 5
+        bits(col(i1, g0), col(i1, 0), 0, 255)
+        tt(col(i1, 3), col(i1, g0), col(ra, 0), A.add)
+        tt(col(i1, 4), col(i1, 1), col(ra, 1), A.add)
+        plus(o1, col(i1, 0, 5), float(NB))
+        ots = new("off", e)
+        lin(ots, deal(sub(part[1], 0, n), 4), 4.0, ptk)
+        act(V(ih, 0, 8 * n, 2), (V(x, 0, 1536), ots))
+        act(V(ab, 4 * n2, 6 * n2), (V("rm", 0, 2 * NT), col(o1, 3, 2)))
+        act(part[10], part[5], 1.0, M)
+        act(part[11], (V("rm", 0, NT), col(o1, 1)), 1.0, M)
+        act(part[6], part[10], 1.0, -M, AF.Abs)
+        act(part[9], part[11], 1.0, -M, AF.Abs)
+
+        def mark(out, src, shift):
+            act(part[3], src, fn=AF.Sign)
+            act(out, part[3], shift / 2, shift / 2)
+
+        mark(part[7], part[4], NN)
+        d = deal(V(ab, 6 * n2, 8 * n2), 4)
+        tg, otg = new("sm", e), new("off", e)
+        tt(tg, sub(d, 0, e), sub(d, 4 * c2, 4 * c2 + e), A.add)
+        lin(otg, tg, 4.0, ptj)
+        j0, j1, f_, g_, ob = new("si", e), new("si", e), new("sm", e), new("sm", e), new("off", e)
+        whole(j0, deal(sub(part[5], 0, n), 4), 512)
+        bits(j1, j0, 0, 511)
+        lin(f_, j1, -8.0, pb)
+        tt(g_, f_, sub(tsp, 0, e), A.min)
+        cp(ob, g_)
+        cp((V("ch", 0, 480), sub(o1, 0, c)), sub(part[9], 0, n))
         if r == 0:
-            rb, ee, nt, st, ost = new("si", 2 * c), new("sm", c), new("sm", c), new("sm", c), new("off", c)
-            lin(rb, deal(V(ab, 3 * n, 5 * n)), 2.0, -512.0)
-            tt(ee, sub(rb, 0, c), gp, A.subtract)
-            ts(nt, ee, float(NL), A.not_equal, float(JUNK), A.mult)
-            tt(st, sub(rb, c, 2 * c), nt, A.add)
-            ts(ost, st, 8.0, A.add)
-            cp((V("tb", 0, 1248), ost), V(ab, 0, n))
-        return opre, otg
+            mark(part[8], (V("rm", NL, NT), col(o1, 2)), NT)
+            d = deal(V(ab, 8 * n2, 10 * n2))
+            st, ost = new("sm", c), new("off", c)
+            tt(st, sub(d, c, 2 * c), sub(d, 0, c), A.add)
+            plus(ost, st, 2 * K)
+            act(part[2], part[0], 1.0, -float(NL))
+            cp((V("tb", 0, 2 * NT), ost), part[2])
+        return ob, otg
 
     def layer(r, gq, gs, n, lists, x):
-        h = "h%d" % r
+        ih, vb = "ih%d" % r, V("vb%d" % r, 0, 4 * n)
         for b in range(4):
             o = mm(4 + b, "wq", "wsc", 128 * b, gq, gs, 0, 128)
-            o, dst = V("ps", o[1], o[1] + n), V(h, 4 + b, 4 + 4 * n, 4)
-            if b == 3:
+            o, dst = V("ps", o[1], o[1] + n), V(ih, 2 * b + 1, 8 * n, 8)
+            if ON["relu"][b] == "v":
                 ts(dst, o, 0.0, A.max, 0.03125, A.mult)
             else:
                 act(dst, o, 0.03125, fn=AF.Relu)
-        va, vb = V("va%d" % r, 0, 4 * n), V("vb%d" % r, 0, 4 * n)
-        tt(va, (V(h, 0, 4 + 4 * n), lists[0]), V("ts%d" % r, 0, 4 * n), A.add)
-        tt(vb, va, V(h, 4, 4 + 4 * n), A.add)
+        scan(V(ih, 8 * n, 16 * n), V("alt", 0, 8 * n), V(ih, 0, 8 * n), 0.0, A.mult, A.add)
+        tt(vb, (V(ih, 8 * n, 16 * n), lists[0]), V(ih, 1, 8 * n, 2), A.add)
         cp((V(x, 0, 3072), lists[1]), vb)
 
-    lst0 = V("lst0", 0, 48)
+    lst0, ll = V("lst0", 0, 48), V("ll", 0, 48)
     fold_lists("sort0", NL, lst0)
-    arrive("al", [V("ll", 0, 48)], [send(peer[0], V("ll", 0, 48), lst0, "al")], 2200)
+    arrive("al", [ll], [send(peer[0], ll, lst0, "al")], 2000)
     lists0 = rake(0, "sort0", NL, "xa")
-    ub = M1 - M0 / 2
-    act(V("ulo", 8, 200), V("num", 0, NL), 0.5, ub)
-    act(V("ulo", 200, NT), (cw, sub(opos, 0, 12)), 0.5, ub)
-    act(V("uh", 0, NL), (cw, ohi), 0.5, ub)
-    act(V("um", 0, NL), (V("ulo", 0, NT), ocr))
-    tt(V("bt", 0, NL), V("uh", 0, NL), V("um", 0, NL), A.subtract)
-    tt(V("bt", 256, 448), V("ulo", 200, NT), V("um", 0, NL), A.subtract)
-    act(V("bt", 512, 960), V("bt", 0, 448), -1.0)
-    isl, cs, cpar = new("si", 24), new("si", 30), new("si", 30)
-    ts(isl, deal(V("scat", 0, NN)), 8192.0, A.mult)
-    ts(sub(cs, 0, 24), isl, 1023, A.bitwise_and)
-    ie, lf = new("si", 6), new("si", 6)
-    lin(ie, deal(V("sort0", 0, NL, 2)), 2.0, -131072.0)
-    ts(sub(cs, 24, 30), ie, 8, A.logical_shift_right)
-    ts(cpar, cs, 255, A.bitwise_and)
-    ts(lf, ie, 255, A.bitwise_and)
-    osl, opl, olf, olp = new("off", 30), new("off", 30), new("off", 6), new("off", 6)
-    cp(osl, cs)
-    ts(opl, cpar, 200.0, A.add)
-    ts(olf, lf, 8.0, A.add)
-    act(V("b1", 0, 480), (V("bt", 0, 960), osl))
-    act(V("lpr", 0, 96), (pw, sub(opl, 24, 30)))
-    lin(olp, deal(V("lpr", 0, 96)), 2.0, -1408.0)
-    act(V("pay1s", 0, 96), (V("tb", 0, NT), olf), 256.0, -512.0)
-    tt(V("pay1", 0, 96), (IT(0, NT), olf), V("pay1s", 0, 96), A.add)
-    fold(V("th", 0, 1536), V("ll", 0, 48), 24, "fp0", "f0")
+    act(V("lo", 0, NL), (V("ss", 0, NN), sub(opos, 0, 12)), 1.0, -M)
+    l2, l3, dd, yy, oa = new("si", 12), new("si", 12), new("sm", 12), new("sm", 12), new("off", 12)
+    whole(l2, deal(V("lo", 0, NL)), 2)
+    bits(l3, l2, 0, 2)
+    tt(dd, dex, den, A.subtract)
+    tt(yy, dd, l3, A.subtract)
+    plus(oa, yy, 6.0)
+    act(V("asz", NI, NT), (V("ta", 0, NT), oa))
+    act(V("asz", NB, NI), (V("par", 0, NL), onum))
+    for h in range(2):
+        act(V("bt", NB + SB * h, NI + SB * h), (V("asz", 0, NT), sub(oc, 12 * h, 12 * h + 12)))
+    act(V("bt", 512, 1024), V("bt", 0, 512), -1.0)
+    dt_ = deal(V("sc", 0, NN))
+    aa, sg, it, ib, ofb = new("sm", 24), new("sm", 24), new("si", 30), new("si", 66), new("off", 66)
+    act(aa, dt_, 2048.0, 2048.0 * K, AF.Abs)
+    ts(sg, dt_, -K, A.is_lt, 512.0, A.mult)
+    tt(sub(it, 0, 24), aa, sg, A.add)
+    whole(sub(it, 24, 30), deal(V("sort0", 0, NL, 2)), 1024)
+    bits(sub(ib, 0, 30), it, 0, 1023)
+    bits(sub(ib, 30, 60), it, 0, 255)
+    bits(sub(ib, 60, 66), sub(it, 24, 30), 12, 255)
+    cp(ofb, ib)
+    oal, olp = sub(ofb, 60, 66), new("off", 6)
+    act(V("b1", 0, 480), (V("bt", 0, 1024), sub(ofb, 0, 30)))
+    act(V("lp1", 0, 96), (V("lqr", 0, NL), oal))
+    plus(olp, deal(V("lp1", 0, 96)), K + 256)
+    act(V("p1s", 0, 96), (V("tb", NB, NI), oal), 1 / 1024.0, (NI + SB) / 1024.0)
+    tt(V("pay1", 0, 96), (V("id4", 0, NL), oal), V("p1s", 0, 96), A.add)
+    fold(V("th", 0, 1536), ll, 24, "fp0", "f0")
     quant("fq0", "fs0", 0, 128, V("f0", 0, 512))
     layer(0, "fq0", "fs0", 96, lists0, "xa")
 
     quant("q1", "s1", NL, NN, V("xa", 768, 1536))
     p1 = mm(4, "uq2", "us2", 0, "q1", "s1", NL, NN)
     quant("q1", "s1", 0, NL, V("xa", 0, 768))
-    unpack("q1", "s1", "xb", 1.0)
-    ts(V("ft", 200, 391), V("ps", p1[1], p1[1] + NL - 1), 0.0, A.is_gt)
-    tt(V("g1", 0, 480), (V("ft", 0, 456), opl), V("b1", 0, 480), A.mult)
-    scan(V("ss", 0, NN), V("g1", 0, NN), V("m2", 0, NN), 512.0, A.add, A.max)
-    tt(V("num1", 0, 96), (V("ss", 0, NN), olp), V("g1", NN, 480), A.add)
-    nh, on1 = new("sm", 6), new("off", 6)
-    tt(nh, deal(V("num1", 0, 96)), kwh, A.add)
-    ts(on1, nh, 2.0, A.mult)
+    unpack("q1", "s1", 0, 0, *[("xh", 0.5), ("xb", 1.0)][1 - ON["xh"]:])
+    ts(V("ft1", NB, NI - 1), sub(p1, 0, NL - 1), 0.0, A.is_gt)
+    tt(V("g1", 0, 480), (V("ft1", 0, NI + NB), sub(ofb, 30, 60)), V("b1", 0, 480), A.mult)
+    scan(V("ss1", 0, NN), V("g1", 0, NN), V("zero", 0, NN), 0.0, A.add, A.add)
+    tt(V("num1", 0, 96), (V("ss1", 0, NN), olp), V("g1", NN, 480), A.add)
+    on1 = new("off", 6)
+    plus(on1, deal(V("num1", 0, 96), 16, V("cj", 0, 96)), pk)
     cp((V("sort1", 0, 96), on1), V("pay1", 0, 96))
     lst1 = new("off", 24)
     fold_lists("sort1", 96, lst1)
-    fold(V("xb", 0, 1536), lst1, 12, "fp1", "fsum")
-    ts(V("f1", 0, NL), V("fsum", 0, NL), 0.5, A.mult)
+    if ON["xh"]:
+        fold(V("xh", 0, 1536), lst1, 12, "fp1", "f1")
+    else:
+        fold(V("xb", 0, 1536), lst1, 12, "fp1", "fsum")
+        ts(V("f1", 0, NL), V("fsum", 0, NL), 0.5, A.mult)
     quant("fq1", "fs1", 0, 128, V("f1", 0, 512))
-    sg = [send(peer[1], V("gq", 0, 48), V("fq1", 0, 48), "ag"), send(peer[1], V("gs", 0, 48), V("fs1", 0, 48), "ag")]
-    arrive("ag", [V("gq", 0, 48), V("gs", 0, 48)], sg, 2500)
-    act(V("fz", SIB, SIB + NL), V("ft", 200, NT), float(NT), 512.0)
-    act(V("fz", SIB + 256, HOLE), V("ft", 200, NT), float(-NT), 512.0 + NT)
+    gq, gs = V("lq", 0, 48), V("ls", 0, 48)
+    arrive("ag", [gq, gs], [send(peer[1], gq, V("fq1", 0, 48), "ag"), send(peer[1], gs, V("fs1", 0, 48), "ag")], 2300)
     lists1 = rake(1, "sort1", 96, "xb")
-    act(V("fb", 0, NL), V("ft", 200, NT), 256.0, 512.0)
-    fh, dead, dz, ik, ik2, ok = deal(V("fb", 0, NL)), new("sm", 12), new("sm", 12), new("sm", 24), new("sm", 24), new("off", 24)
-    tt(sub(ik, 0, 12), awl, fh, A.subtract)
-    tt(sub(ik, 12, 24), awr, fh, A.add)
-    tt(dead, deal(V("sk", 200, NT)), nodeh, A.not_equal)
-    ts(dz, dead, HOLE / 2.0, A.mult)
-    tt(sub(ik2, 0, 12), sub(ik, 0, 12), dz, A.max)
-    tt(sub(ik2, 12, 24), sub(ik, 12, 24), dz, A.max)
-    ts(ok, ik2, 2.0, A.mult)
-    act(V("kido", 0, NN), (V("tb", 0, JUNK), ok), 1.0, -512.0)
-    dma("y", T.kid[:], T.kido[0:128:16, :], [], [V("kido", 0, NN)], 12288)
-    layer(1, "gq", "gs", 48, lists1, "xb")
+    fxd, i1, i2, i3, ok = new("sm", 12), new("sm", 12), new("sm", 12), new("sm", 24), new("off", 24)
+    tt(fxd, deal(V("ft1", NB, NI)), deal(V("ft0", NB, NI)), A.not_equal)
+    act(i1, fxd, float(SB))
+    act(V("fb", 0, NL), V("rm", NI, NT), fn=AF.Sign)
+    act(V("gone", 0, NL), V("fb", 0, NL), float(SB), float(SB))
+    tt(i2, deal(V("gone", 0, NL)), kidc, A.add)
+    tt(sub(i3, 0, 12), i2, i1, A.add)
+    tt(sub(i3, 12, 24), i2, i1, A.subtract)
+    plus(sub(ok, 0, 12), sub(i3, 0, 12), K)
+    plus(sub(ok, 12, 24), sub(i3, 12, 24), K + SB)
+    act(V("kido", 0, NN), (V("ch", 0, 976), ok), 1.0, -float(NB))
+    dma("y", T.kid[:], T.kido[0:128:16, :], [], [V("kido", 0, NN)], 1600)
+    layer(1, "lq", "ls", 48, lists1, "xb")
 
     for h in range(2):
         a, b = NL * h, NL * h + NL
         quant("q2", "s2", a, b, V("xb", 4 * a, 4 * b))
         o = mm(h, "vq", "vs", 0, "q2", "s2", a, b)
-        if h:
-            cp(V("yo", a, b), o)
-        else:
-            act(V("yo", a, b), o)
-        dma("y" if h else "s", T.y[:, a:b], T.yo[:, a:b], [], [V("yo", a, b)], 98304)
-        dma("y", T.oc[:, 4 * a:4 * b], T.q2[:, a:b].bitcast(dt.uint8), [], [V("q2", a, b)], 98304)
+        get(ON["y"][h], V("yo", a, b), o)
+        dma("y" if h else "s", T.y[:, a:b], T.yo[:, a:b], [], [V("yo", a, b)], 2400)
+        dma("y", T.oc[:, 4 * a:4 * b], T.q2[:, a:b].bitcast(dt.uint8), [], [V("q2", a, b)], 2400)
     for k in range(4):
-        dma("s" if k % 2 else "y", T.osc[4 * k:4 * k + 4, :], T.s2[32 * k:32 * k + 4, :], [], [V("s2", 0, NN)], 1536)
+        dma("s" if k % 2 else "y", T.osc[4 * k:4 * k + 4, :], T.s2[32 * k:32 * k + 4, :], [], [V("s2", 0, NN)], 1600)
     return ops, count
+
+
+def pack(ops, before, after, key, turned):
+    n = len(ops)
+    left = [len(b) for b in before]
+    ready = sorted((key[i], -i) for i in range(n) if not left[i])
+    start, done, busy = [0.0] * n, [0.0] * n, {}
+    while ready:
+        i = -ready.pop()[1]
+        c, lat = ops[i]["c"], ops[i]["l"]
+        t = max([done[j] + WAKE for j in before[i]] + [0.0]) + (lat if turned else 0.0)
+        gaps = busy.setdefault(ops[i]["e"], [])
+        k = len(gaps)
+        while k and gaps[k - 1][1] > t:
+            k -= 1
+        while k < len(gaps) and t + c > gaps[k][0]:
+            t = max(t, gaps[k][1])
+            k += 1
+        gaps.insert(k, (t, t + c))
+        start[i], done[i] = t, t + c + (0.0 if turned else lat)
+        for j in after[i]:
+            left[j] -= 1
+            if not left[j]:
+                ready.append((key[j], -j))
+        ready.sort()
+    return start, done
+
+
+_ORDER = []
+
+
+def arrange(ops):
+    if _ORDER:
+        return _ORDER
+    n = len(ops)
+    before, after = [sorted(o["d"]) for o in ops], [[] for o in ops]
+    tail = [0.0] * n
+    for i in reversed(range(n)):
+        tail[i] += ops[i]["c"] + ops[i]["l"] + WAKE
+        for j in before[i]:
+            tail[j] = max(tail[j], tail[i])
+            after[j].append(i)
+
+    def settle(key):
+        key = pack(ops, after, before, pack(ops, before, after, key, False)[1], True)[1]
+        start, done = pack(ops, before, after, key, False)
+        return max(done), start, key
+
+    seed = [1]
+
+    def draw():
+        seed[0] = seed[0] * 48271 % 2147483647
+        return seed[0] / 2147483647.0
+
+    best = now = settle(tail)
+    for _ in range(TRIES):
+        mid, wide, far = draw() * max(now[2]), 1500 * 2 ** int(3 * draw()), 2000 * draw()
+        got = settle([k + far * (draw() - 0.5) if abs(k - mid) < wide else k for k in now[2]])
+        if got[0] <= now[0] + 30:
+            now = got
+        if got[0] < best[0]:
+            best = got
+    _ORDER.extend(sorted(range(n), key=lambda k: (best[1][k], k)))
+    return _ORDER
 
 
 def rank_program(g, core, T, topo):
@@ -573,9 +637,9 @@ def rank_program(g, core, T, topo):
     if rank is None:
         return
     ops, count = build(T, topo, core, rank)
-    order = ORDER
+    order = arrange(ops)
     place = {i: k for k, i in enumerate(order)}
-    assert len(place) == len(ops) and all(place[j] < place[i] for i, o in enumerate(ops) for j in o["d"])
+    assert all(place[j] < place[i] for i, o in enumerate(ops) for j in o["d"])
     queue = {"v": g.vector, "s": g.scalar, "t": g.tensor, "y": g.sync, "g": g}
     known = {e: set() for e in queue}
     saw, waits, needed = {}, {}, set()

@@ -9,9 +9,10 @@ NI = NL + NB
 SB = 256
 K = 1024.0
 M = 8388864.0
-CY, WAKE = 1.04, 100
-TRIES = 6000
-ON = {"sx": "s", "sz": "vss", "ch": "ss", "pay": "sv", "y": "ss", "relu": "ssss", "jv": [0] * 7, "gw": 2, "xh": 0, "fb": "s"}
+CY, GA, SC, WAKE, FIX = 0.955, 1.67, 3.63, 140, 40
+TRIES = 9000
+ON = {"sx": "ss", "sz": "ss", "ch": "ss", "fb": "s", "pv": 10, "y": "sv", "relu": "svsv", "jv": [6] * 7, "gw": 2, "pc": "v", "cc": "ss",
+      "mk": "vv", "bt": "s", "c0": [0, 8, 16, 24], "c1": [0, 4, 12], "cut": 240, "lh": [1, 1]}
 
 
 def _sb(n, d=F32):
@@ -28,17 +29,17 @@ SCRATCH = {
     "fq0": _sb(128, C4X), "fs0": _sb(128, U8), "fq1": _sb(128, C4X), "fs1": _sb(128, U8),
     "z": _sb(520, BF), "one": _sb(128, BF), "zero": _sb(NN, BF),
     "th": _sb(1536, BF), "xa": _sb(3072, BF), "xb": _sb(3072, BF), "xh": _sb(1536, BF),
-    "f0": _sb(512, BF), "f1": _sb(512, BF), "fp0": _sb(384, BF), "fp1": _sb(192, BF), "fsum": _sb(192, BF),
+    "f0": _sb(512, BF), "f1": _sb(512, BF), "fp0": _sb(384, BF), "fp1": _sb(192, BF),
     "ih0": _sb(1536, BF), "ih1": _sb(768, BF), "vb0": _sb(384, BF), "vb1": _sb(192, BF), "alt": _sb(768, BF),
     "c16": _sb(NN, BF), "c4": _sb(NL, BF), "cj": _sb(96, BF), "cst": _sb(192), "csi": _sb(32, I32),
-    "rp": _sb(448), "id4": _sb(NL), "slot": _sb(NN, BF), "zz": _sb(640, BF), "w": _sb(9 * 512, BF), "pos": _sb(448, BF),
-    "tb": _sb(2 * NT, BF), "ch": _sb(976), "ix": _sb(448), "sx": _sb(NN), "sz": _sb(2 * NT), "een": _sb(NL),
+    "rp": _sb(448), "id4": _sb(NL), "slot": _sb(NN), "zz": _sb(640, BF), "w": _sb(9 * 512, BF), "pos": _sb(448, BF),
+    "ch": _sb(976), "ix": _sb(448), "sx": _sb(NN), "sz": _sb(3 * NT), "sp": _sb(96), "een": _sb(NL),
     "pay": _sb(NN), "sc": _sb(NN), "ss": _sb(NN), "ol": _sb(NL), "lqr": _sb(NL, BF), "num": _sb(NL, BF), "pay0": _sb(NL),
-    "sort0": _sb(NL), "sort1": _sb(96), "rm": _sb(2 * NT), "kf": _sb(96), "fa": _sb(NL, BF), "fb": _sb(NL, BF),
+    "sort0": _sb(NL), "sort1": _sb(96), "rm": _sb(4 * NT, BF), "af0": _sb(192), "af1": _sb(128), "fa": _sb(NL, BF), "fb": _sb(NL, BF),
     "ft0": _sb(NI + NB, BF), "ft1": _sb(NI + NB, BF), "gone": _sb(NL, BF), "lo": _sb(NL, BF), "ta": _sb(NT, BF),
     "par": _sb(NL, BF), "asz": _sb(NT, BF), "bt": _sb(1024, BF), "b1": _sb(480, BF), "g1": _sb(480, BF), "ss1": _sb(NN, BF),
-    "lp1": _sb(96, BF), "num1": _sb(96, BF), "p1s": _sb(96), "pay1": _sb(96), "ab0": _sb(1248), "ab1": _sb(832),
-    "so": _sb(4096), "sh": _sb(6144, F16), "sm": _sb(768), "si": _sb(768, I32), "off": _sb(1024, U16),
+    "lp1": _sb(96, BF), "num1": _sb(96, BF), "p1s": _sb(96), "pay1": _sb(96), "ab0": _sb(1056, BF), "ab1": _sb(704, BF),
+    "so": _sb(4096), "sh": _sb(8192, F16), "sm": _sb(768), "si": _sb(768, I32), "off": _sb(1024, U16),
     "kido": _sb(NN), "yo": _sb(NN),
     "ps": ("psum", [128, 4096], F32),
 }
@@ -114,9 +115,9 @@ def build(T, topo, core, rank):
 
     def vcost(out, in0, n, plain):
         if len(in0) == 2:
-            return 50 + 1.56 * CY * n
+            return 50 + GA * n
         if len(out) == 2:
-            return 50 + 3.8 * CY * n
+            return 50 + SC * n
         return max(64, plain) * CY
 
     def ts(out, in0, s1, o1, s2=None, o2=None):
@@ -155,7 +156,7 @@ def build(T, topo, core, rank):
 
     def act(out, in0, scale=1.0, bias=0.0, fn=AF.Identity):
         n = _len(out)
-        c = 65 + 1.56 * CY * n if len(in0) == 2 else max(64, n) * CY + 30
+        c = 65 + GA * n if len(in0) == 2 else max(64, n) * CY + FIX
         if fn == AF.Identity and scale == 1.0 and bias == 0.0:
             return add("s", lambda q: q.activation(ap(out), ap(in0), AF.Copy), [out], [in0], c)
         return add("s", lambda q: q.activation(ap(out), ap(in0), fn, bias=sc(bias), scale=scale), [out], [in0, bias], c)
@@ -180,9 +181,9 @@ def build(T, topo, core, rank):
 
     def iota(out, pat, base, ch=0):
         if SCRATCH[out[0]][2] == I32:
-            return add("g", lambda q: q.iota(ap(out), pat, base, ch), [out], [], 130 + 2 * CY * _len(out))
+            return add("g", lambda q: q.iota(ap(out), pat, base, ch), [out], [], 170 + 2.6 * _len(out))
         return add("g", lambda q: q.iota(ap(out), pat, base, ch, allow_small_or_imprecise_dtypes=True), [out], [],
-                   130 + 2 * CY * _len(out))
+                   170 + 2.6 * _len(out))
 
     def fill(out, c):
         return iota(out, [[0, _len(out)]], c)
@@ -214,7 +215,7 @@ def build(T, topo, core, rank):
         count[sem] = count.get(sem, 0) + n
         count["sent"] = count.get("sent", 0) + n
         return add("g", lambda e: e.remote_dma(u8(out), u8(in_), T.sem[sem], T.sem["sent"], pid, rid, topo.mask(core, dst)),
-                   [], [in_], 300, 0.0, "r")
+                   [], [in_], 300 if count["sent"] > n else 1600, 0.0, "r")
 
     def arrive(sem, outs, sends, lat):
         i = add("a", None, outs, [], 0.0, lat, "a", sends)
@@ -238,11 +239,9 @@ def build(T, topo, core, rank):
     bits(V("csi", 3, 4), pi, 2, 3)
     bits(V("csi", 4, 5), pi, 0, 3)
     cp(V("cst", 0, 3), V("csi", 2, 5))
-    p16, p4, pt, ptp, ptk, ptj, pb, p32 = [sub(pc, i, i + 1) for i in range(8)]
-    pk = V("cst", 176, 177)
-    for out, src, m, c in ((ptp, pt, 1, 4 * (NL - NB)), (ptk, pt, 1, 4 * K), (ptj, pt, 1, 8 * K - 4 * NB), (pb, pt, 2, 1025),
-                           (p32, p16, 2, 0), (pk, p16, 1, K)):
-        act(out, src, float(m), float(c))
+    p16, p4, pt, pk, ptk, ptj, pb, p32 = [sub(pc, i, i + 1) for i in range(8)]
+    for out, src, m, c in ((ptk, pt, 1, 4 * K + 4 * NL), (ptj, pt, 1, 8 * K + 4 * NL), (pb, pt, 2, 1), (p32, p16, 2, 0), (pk, p16, 1, K)):
+        get(ON["pc"], out, src, float(m), float(c))
     j16, j4 = V("cst", 8, 40), V("cst", 40, 72)
     iota(j16, [[1, 2], [1, 16]], 0)
     iota(j4, [[1, 2], [0, 4], [1, 4]], 0)
@@ -253,21 +252,21 @@ def build(T, topo, core, rank):
         n = 16
         while n < top:
             k = min(n, top - n)
-            act(V(c, n, n + k), V(c, 0, k))
+            get(ON["cc"][blk == 4], V(c, n, n + k), V(c, 0, k))
             n += k
     own, kidc, tsp = V("cst", 104, 128), V("cst", 128, 140), V("cst", 152, 176)
-    for out, pat, base, p in ((own, [[SB, 2], [16, 12]], NL, p16), (kidc, [[16, 12]], NB, p16), (tsp, [[32, 24]], 0, p32)):
+    for out, pat, base, p in ((own, [[SB, 2], [16, 12]], NL, p16), (kidc, [[16, 12]], NB, p16), (tsp, [[32, 24]], -int(K), p32)):
         iota(out, pat, base)
-        act(out, out, 1.0, p)
+        get(ON["pc"], out, out, 1.0, p)
     iota(V("rp", 0, 112), [[1, 112]], 0)
     for a in (112, 224):
         ramp(V("rp", a, 2 * a), a)
-    ramp(V("slot", 0, NL), -NL)
-    ramp(V("slot", NL, NN), SB - NL)
+    ramp(V("slot", 0, NL), NB / 1024.0 - 3, 1 / 1024.0)
+    ramp(V("slot", NL, NN), (SB + NB) / 1024.0 - 3, 1 / 1024.0)
     ramp(V("zz", NL + 1, 640), NL + 1 - NN)
     ms(V("zz", NL, NL + 1), -256.0)
-    ms(V("tb", 0, NB), 0.0)
-    ms(V("tb", NT - 1, NT), 0.0)
+    ms(V("sz", NT, NT + NB), 0.0)
+    ms(V("sz", 2 * NT - 1, 2 * NT), NI / 1024.0 - 3)
     for k in range(9):
         if k < ON["gw"]:
             ramp(V("w", 512 * k, 512 * k + 128), 2 ** k - 256)
@@ -276,15 +275,14 @@ def build(T, topo, core, rank):
     iota(V("csi", 8, 16), [[16, 8]], 0)
     ou = new("off", 8)
     cp(ou, V("csi", 8, 16))
-    for name, a, b, c in (("fa", NL - 1, NL, 0), ("ft0", 0, NB, 0), ("ft0", NI, NI + NB, 0), ("ft1", 0, NB, 0), ("ft1", NI - 1, NI + NB, 0),
-                          ("ix", NL, SB, 2 * NT - 1), ("pos", NL, SB, 0), ("sz", 0, NB - 1, 0), ("sz", NT, NT + NB - 1, 0),
-                          ("si", 0, 16, 0), ("ch", 0, NB, 0), ("ch", NI, NB + SB, 0), ("ch", NI + SB, 976, NB - 1),
-                          ("asz", 0, NB, 0), ("bt", 0, NB, 0), ("bt", NI, NB + SB, 0), ("bt", NI + SB, 512, 0),
-                          ("f0", NN, 512, 0), ("f1", NL, 512, 0), ("zero", 0, NN, 0)):
+    for name, a, b, c in (("fa", NL - 1, NL, 0), ("ft0", 0, NB, 0), ("ft0", NI, NI + NB, 0), ("ix", NL, SB, 2 * NT - 1), ("pos", NL, SB, 0),
+                          ("ch", 0, NB, 0), ("ch", NI, NB + SB, 0), ("ch", NI + SB, 480, NB - 1), ("asz", 0, NB, 0),
+                          ("bt", 0, NB, 0), ("bt", NI, NB + SB, 0), ("bt", NI + SB, 512, 0), ("f0", NN, 512, 0),
+                          ("rm", 2 * NT, 4 * NT, 127)):
         fill(V(name, a, b), c)
     iota(V("id4", 0, NL), [[4, NL]], 3)
-    iota(V("rm", 0, 2 * NT), [[0, 2], [-1, NT]], 0)
-    ramp(V("kf", 0, 96), 0.25, -1 / 512.0)
+    iota(V("rm", 0, 2 * NT), [[0, 2], [1, NT]], -NI)
+    iota(V("ab0", 192, 288), [[1, 96]], 0)
     iota(V("ta", 0, NT), [[1, NT // 4], [0, 4]], 0)
     iota(V("par", 0, NL), [[0, NL // 2], [-1, 2]], 1)
     iota(V("alt", 0, 768), [[0, 384], [1, 2]], 0)
@@ -293,7 +291,7 @@ def build(T, topo, core, rank):
     ms(V("z", 0, 520), 0.0)
     ms(V("one", 0, 128), 1.0)
     add("g", lambda q: q.affine_select(T.z[:, 4:516:4], T.one[:], [[-1, 128]], A.is_equal, 0.0, 0, 1),
-        [V("z", 4, 516, 4)], [V("one", 0, 128)], 170 + 256 * CY)
+        [V("z", 4, 516, 4)], [V("one", 0, 128)], 550)
     for b in range(4):
         quant("eq", "es", 128 * b, 128 * b + 128, V("z", 4 - b, 516 - b))
 
@@ -306,14 +304,14 @@ def build(T, topo, core, rank):
     tt(y_, t_, own, A.max)
     plus(sub(oz, 12, 24), sub(y_, 12, 24), -float(NL + SB))
     plus(sub(oz, 0, 12), sub(y_, 0, 12), -float(NL))
-    cp((V("tb", 0, NT - 1), oc), V("slot", 0, NN))
+    cp((V("sz", NT, 2 * NT - 1), oc), V("slot", 0, NN))
     act(V("zz", 0, NL), (V("zz", SB, 640), sub(oz, 12, 24)))
     act(V("w", 320, 512), (V("zz", 0, 640), sub(oz, 0, 12)))
     osl = new("off", 24)
     oin, olf = sub(osl, 0, 12), sub(osl, 12, 24)
-    plus(oin, deal(V("tb", NI, NT)), K + NL)
+    lin(oin, deal(V("sz", NT + NI, 2 * NT)), 1024.0, 1024 * (K + 3) - NB)
     act(V("w", 128, 320), (V("zz", 0, 448), oin))
-    plus(olf, deal(V("tb", NB, NI)), K + NL)
+    lin(olf, deal(V("sz", NT + NB, NT + NI)), 1024.0, 1024 * (K + 3) - NB)
     for h in range(2):
         get(ON["ch"][h], V("ch", NB + SB * h, NI + SB * h), (V("rp", 0, NT), sub(oc, 12 * h, 12 * h + 12)))
 
@@ -337,19 +335,18 @@ def build(T, topo, core, rank):
 
     unpack("q0", "s0", 0, 0, ("xa", 1.0))
     ts(V("fa", 0, NL - 1), sub(p0, 0, NL - 1), 0.0, A.is_gt, float(NT), A.mult)
-    unpack("lq", "ls", 48, 4, ("th", 0.5))
     get(ON["fb"], V("fb", 0, NL), V("fa", 0, NL), -1.0, float(NT))
     tt(V("ix", SB, SB + NL), (V("rp", 0, NT), sub(oc, 0, 12)), V("fa", 0, NL), A.add)
     tt(V("ix", 0, NL), (V("rp", 0, NT), sub(oc, 12, 24)), V("fb", 0, NL), A.add)
     act(V("ft0", NB, NI), V("fa", 0, NL), fn=AF.Sign)
+    unpack("lq", "ls", 48, 4, ("th", 0.5))
     osx = new("off", 24)
     for h in range(2):
-        get(ON["sx"], V("sx", NL * h, NL * h + NL), (V("ix", 0, 448), sub(osl, 12 * h, 12 * h + 12)))
+        get(ON["sx"][h], V("sx", NL * h, NL * h + NL), (V("ix", 0, 448), sub(osl, 12 * h, 12 * h + 12)))
         plus(sub(osx, 12 * h, 12 * h + 12), deal(V("sx", NL * h, NL * h + NL)), K)
     szw = V("sz", 0, 2 * NT)
-    get(ON["sz"][0], V("sz", NT + NB - 1, 2 * NT), V("tb", NB - 1, NT), 1 / 1024.0, NI / 1024.0 - 3)
-    get(ON["sz"][1], V("sz", NB - 1, NI), V("tb", NB - 1, NI), 1 / 1024.0, (NI + 512) / 1024.0 - 1)
-    get(ON["sz"][2], V("sz", NI, NT), V("tb", NI, NT), 1 / 1024.0, (NI + 512) / 1024.0)
+    get(ON["sz"][0], V("sz", 0, NI), V("sz", NT, NT + NI), 1.0, 2.5)
+    get(ON["sz"][1], V("sz", NI, NT), V("sz", NT + NI, 2 * NT), 1.0, 3.5)
     tt(V("pay0", 0, NL), (szw, sub(osx, 12, 24)), V("id4", 0, NL), A.add)
 
     op = None
@@ -373,8 +370,10 @@ def build(T, topo, core, rank):
     den, dex = deal(V("pos", 0, NL)), deal(V("pos", SB, SB + NL))
     plus(sub(opos, 0, 12), den, K + 256)
     plus(sub(opos, 12, 24), dex, K + 257)
-    get(ON["pay"][0], V("pay", 0, NL), (szw, sub(osx, 0, 12)), 0.5, 1.5)
-    get(ON["pay"][1], V("pay", NL, NN), (szw, sub(osx, 0, 12)), -0.5, -1.5)
+    act(V("pay", 0, NL), (szw, sub(osx, 0, 12)), 0.5, 1.5)
+    for e, a, b in (("v", 0, ON["pv"]), ("s", ON["pv"], 12)):
+        if a < b:
+            get(e, V("pay", NL + 16 * a, NL + 16 * b), (szw, sub(osx, a, b)), -0.5, -1.5)
     cp((V("sc", 0, NN), opos), V("pay", 0, NN))
     act(V("ol", 0, NL), (szw, sub(osx, 12, 24)), 0.5, 1 - M)
     act(V("lqr", 0, NL), (V("pos", 0, 448), olf))
@@ -388,87 +387,88 @@ def build(T, topo, core, rank):
 
     def fold_lists(sort, m, lst):
         e = m // 8
-        i4, l4, q4 = new("si", e), new("si", e), new("si", e)
+        i4, lp = new("si", e), new("si", 2 * e)
         whole(i4, deal(V(sort, 1, m, 2), 4), 1024)
-        bits(q4, i4, 0, 255)
-        bits(l4, i4, 12, 255)
-        lin(sub(lst, e, 2 * e), q4, 4.0, ptp)
-        lin(sub(lst, 0, e), l4, 4.0, pt)
+        bits(sub(lp, e, 2 * e), i4, 0, 255)
+        bits(sub(lp, 0, e), i4, 12, 255)
+        lin(lst, lp, 4.0, pt)
 
-    def fold(win, lst, e, tmp, out):
-        h = e // 2
-        for i in range(2):
-            act(V(tmp, 16 * h * i, 16 * h * (i + 1)), (win, sub(lst, e + h * i, e + h * (i + 1))))
-            tt(V(out, 16 * h * i, 16 * h * (i + 1)), (win, sub(lst, h * i, h * (i + 1))), V(tmp, 16 * h * i, 16 * h * (i + 1)), A.add)
+    def fold(x, lst, e, tmp, out, cuts):
+        for a, b in zip(cuts, cuts[1:]):
+            act(V(tmp, 16 * a, 16 * b), (V(x, 4 * (NL - NB), 1536), sub(lst, e + a, e + b)))
+            tt(V(out, 16 * a, 16 * b), (V(x, 0, 768), sub(lst, a, b)), V(tmp, 16 * a, 16 * b), A.add)
 
     def rake(r, sort, m, x):
         n, c, e = m // 2, m // 32, m // 8
         c2 = c + c % 2
         n2, ab, ih = 16 * c2, "ab%d" % r, "ih%d" % r
-        part = [V(ab, n2 * i, n2 * i + n2) for i in range(13)]
+        part = [V(ab, n2 * i, n2 * i + n2) for i in range(11)]
         col = lambda v, i, k=1: sub(v, c2 * i, c2 * (i + k))
-        i0, o0 = V("si", 0, 16) if r else new("si", 4 * c2), new("off", 2 * c2)
+        i0, o0 = V("si", 0, 16) if r else new("si", 4 * c2), new("off", 3 * c2)
         whole(sub(i0, 0, c), deal(V(sort, 1, m, 2)), 1024)
-        bits(col(i0, 1), col(i0, 0), 0, 255)
-        bits(col(i0, 2), col(i0, 0), 0, 511)
+        bits(col(i0, 1), col(i0, 0), 0, 511)
+        bits(col(i0, 2), col(i0, 0), 0, 255)
         bits(col(i0, 3), col(i0, 0), 9, 1)
-        cp(o0, col(i0, 1, 2))
-        opar, osib = col(o0, 0), col(o0, 1)
-        act(part[0], (V("tb", NL, NT), opar), 1.0, float(NL))
-        act(part[1], (V("ch", 0, 480), osib), 1.0, -float(NB))
-        tt(part[12], (V("ch", 0, 480), osib), V("kf", 0, n2), A.add)
-        cp((V("rm", NL, NT), sub(opar, 0, c)), sub(part[12], 0, n))
-        i1, o1, ra = new("si", 6 * c2), new("off", 5 * c2), new("sm", 2 * c2)
+        cp(col(o0, 0, 2), col(i0, 1, 2))
+        osib, opar = col(o0, 0), col(o0, 1)
+        act(part[0], (V("sz", NT + NL, 2 * NT), opar), 1024.0, 3072.0 - NI)
+        act(part[1], (V("ch", 0, 480), osib), 1.0, -float(NI))
         if r == 0:
-            plus(col(i1, 0, 2), deal(V(ab, 0, 2 * n2)), K)
+            plus(col(o0, 2), col(i0, 2), 2.0 * NT)
+            cp((V("rm", NL, 3 * NT), col(o0, 1, 2)), V(ab, n, 3 * n))
+        else:
+            for h in range(2):
+                cp((V("rm", NL + 2 * NT * h, NT + 2 * NT * h), sub(opar, 0, c)), sub(part[1 + h], 0, n))
+        i1, o1, ra = new("si", 5 * c2), new("off", 5 * c2), new("sm", 2 * c2)
+        plus(col(i1, 0, 2), deal(V(ab, 0, 2 * n2)), K + NL)
+        if r == 0:
             right = col(i0, 3)
         else:
-            act(part[2], (V("ft0", 0, NI + NB), opar))
-            act(part[3], (V("ft1", 0, NI + NB), opar))
-            d1, r1, right = deal(V(ab, 0, 4 * n2)), new("sm", c2), new("sm", c2)
-            plus(col(i1, 0, 3), col(d1, 0, 3), K)
-            tt(r1, col(d1, 2), col(d1, 3), A.not_equal)
+            act(part[3], (V("ft0", 0, NI + NB), opar))
+            act(part[4], (V("ft1", 0, NI + NB), opar))
+            d1, r1, right = deal(V(ab, 3 * n2, 5 * n2)), new("sm", c2), new("sm", c2)
+            tt(r1, col(d1, 0), col(d1, 1), A.not_equal)
             tt(right, r1, col(i0, 3), A.not_equal)
-        get("s" if r else "v", col(ra, 0), right, float(NT), float(NL))
-        get("s" if r else "v", col(ra, 1), right, -float(NT), float(NT))
-        g0 = 2 if r == 0 else 5
-        bits(col(i1, g0), col(i1, 0), 0, 255)
-        tt(col(i1, 3), col(i1, g0), col(ra, 0), A.add)
+        lin(col(ra, 0), right, float(NT), float(NL))
+        lin(col(ra, 1), right, -float(NT), float(NT))
+        bits(col(i1, 2), col(i1, 0), 0, 255)
+        tt(col(i1, 3), col(i1, 2), col(ra, 0), A.add)
         tt(col(i1, 4), col(i1, 1), col(ra, 1), A.add)
-        plus(o1, col(i1, 0, 5), float(NB))
+        plus(o1, i1, float(NB))
         ots = new("off", e)
         lin(ots, deal(sub(part[1], 0, n), 4), 4.0, ptk)
         act(V(ih, 0, 8 * n, 2), (V(x, 0, 1536), ots))
-        act(V(ab, 4 * n2, 6 * n2), (V("rm", 0, 2 * NT), col(o1, 3, 2)))
-        act(part[10], part[5], 1.0, M)
-        act(part[11], (V("rm", 0, NT), col(o1, 1)), 1.0, M)
-        act(part[6], part[10], 1.0, -M, AF.Abs)
-        act(part[9], part[11], 1.0, -M, AF.Abs)
+        who, num = V("rm", 0, 2 * NT), V("rm", 2 * NT, 4 * NT)
 
         def mark(out, src, shift):
-            act(part[3], src, fn=AF.Sign)
-            act(out, part[3], shift / 2, shift / 2)
+            if ON["mk"][r] == "s":
+                act(part[10], src, -1.0, 126.5, AF.Sign)
+                act(out, part[10], shift / 2, shift / 2)
+            else:
+                ts(out, src, 126.5, A.is_lt, float(shift), A.mult)
 
-        mark(part[7], part[4], NN)
+        af, g_, ob = V("af%d" % r, 0, n2), new("sm", e), new("off", e)
+        act(af, (num, col(o1, 4)), 8.0, pb)
+        tt(g_, deal(sub(af, 0, n), 4), sub(tsp, 0, e), A.min)
+        plus(ob, g_, K)
+        act(part[6], (who, col(o1, 4)))
+        mark(part[7], (num, col(o1, 3)), NN)
         d = deal(V(ab, 6 * n2, 8 * n2), 4)
         tg, otg = new("sm", e), new("off", e)
         tt(tg, sub(d, 0, e), sub(d, 4 * c2, 4 * c2 + e), A.add)
         lin(otg, tg, 4.0, ptj)
-        j0, j1, f_, g_, ob = new("si", e), new("si", e), new("sm", e), new("sm", e), new("off", e)
-        whole(j0, deal(sub(part[5], 0, n), 4), 512)
-        bits(j1, j0, 0, 511)
-        lin(f_, j1, -8.0, pb)
-        tt(g_, f_, sub(tsp, 0, e), A.min)
-        cp(ob, g_)
-        cp((V("ch", 0, 480), sub(o1, 0, c)), sub(part[9], 0, n))
+        sv = V("af%d" % r, n2, 2 * n2)
+        act(sv, (who, col(o1, 1)), 1.0, float(NI))
+        cp((V("ch", 0, 480), sub(o1, 0, c)), sub(sv, 0, n))
         if r == 0:
-            mark(part[8], (V("rm", NL, NT), col(o1, 2)), NT)
+            mark(part[8], (V("rm", 2 * NT + NL, 3 * NT), col(o1, 2)), NT)
+            act(part[9], sv, 1.0, -float(NI))
             d = deal(V(ab, 8 * n2, 10 * n2))
             st, ost = new("sm", c), new("off", c)
             tt(st, sub(d, c, 2 * c), sub(d, 0, c), A.add)
-            plus(ost, st, 2 * K)
-            act(part[2], part[0], 1.0, -float(NL))
-            cp((V("tb", 0, 2 * NT), ost), part[2])
+            plus(ost, st, 2 * K + NI)
+            act(V("sp", 0, n), part[0], 1 / 1024.0, NI / 1024.0 - 3)
+            cp((V("sz", NT, 3 * NT), ost), V("sp", 0, n))
         return ob, otg
 
     def layer(r, gq, gs, n, lists, x):
@@ -480,13 +480,21 @@ def build(T, topo, core, rank):
                 ts(dst, o, 0.0, A.max, 0.03125, A.mult)
             else:
                 act(dst, o, 0.03125, fn=AF.Relu)
-        scan(V(ih, 8 * n, 16 * n), V("alt", 0, 8 * n), V(ih, 0, 8 * n), 0.0, A.mult, A.add)
-        tt(vb, (V(ih, 8 * n, 16 * n), lists[0]), V(ih, 1, 8 * n, 2), A.add)
-        cp((V(x, 0, 3072), lists[1]), vb)
+        e = n // 4 // ON["lh"][r]
+        for a in range(0, n // 4, e):
+            b = a + e
+            scan(V(ih, 8 * n + 32 * a, 8 * n + 32 * b), V("alt", 0, 32 * e), V(ih, 32 * a, 32 * b), 0.0, A.mult, A.add)
+            tt(sub(vb, 16 * a, 16 * b), (V(ih, 8 * n, 8 * n + 32 * b), sub(lists[0], a, b)), V(ih, 32 * a + 1, 32 * b, 2), A.add)
+            cp((V(x, 0, 3072), sub(lists[1], a, b)), sub(vb, 16 * a, 16 * b))
 
     lst0, ll = V("lst0", 0, 48), V("ll", 0, 48)
     fold_lists("sort0", NL, lst0)
-    arrive("al", [ll], [send(peer[0], ll, lst0, "al")], 2000)
+    sl = send(peer[0], ll, lst0, "al")
+    arrive("al", [ll], [sl], 2000)
+    late = [fill(V(name, a, b), c) for name, a, b, c in (
+        ("zero", 0, NN, 0), ("ft1", 0, NB, 0), ("ft1", NI - 1, NI + NB, 0), ("si", 0, 16, 0), ("f1", NL, 512, 0), ("ch", 480, 976, NB - 1))]
+    for i in late + [iota(V("ab1", 128, 192), [[1, 64]], 0)]:
+        ops[i]["d"].add(sl)
     lists0 = rake(0, "sort0", NL, "xa")
     act(V("lo", 0, NL), (V("ss", 0, NN), sub(opos, 0, 12)), 1.0, -M)
     l2, l3, dd, yy, oa = new("si", 12), new("si", 12), new("sm", 12), new("sm", 12), new("off", 12)
@@ -499,7 +507,7 @@ def build(T, topo, core, rank):
     act(V("asz", NB, NI), (V("par", 0, NL), onum))
     for h in range(2):
         act(V("bt", NB + SB * h, NI + SB * h), (V("asz", 0, NT), sub(oc, 12 * h, 12 * h + 12)))
-    act(V("bt", 512, 1024), V("bt", 0, 512), -1.0)
+    get(ON["bt"], V("bt", 512, 1024), V("bt", 0, 512), -1.0)
     dt_ = deal(V("sc", 0, NN))
     aa, sg, it, ib, ofb = new("sm", 24), new("sm", 24), new("si", 30), new("si", 66), new("off", 66)
     act(aa, dt_, 2048.0, 2048.0 * K, AF.Abs)
@@ -514,18 +522,19 @@ def build(T, topo, core, rank):
     act(V("b1", 0, 480), (V("bt", 0, 1024), sub(ofb, 0, 30)))
     act(V("lp1", 0, 96), (V("lqr", 0, NL), oal))
     plus(olp, deal(V("lp1", 0, 96)), K + 256)
-    act(V("p1s", 0, 96), (V("tb", NB, NI), oal), 1 / 1024.0, (NI + SB) / 1024.0)
+    act(V("p1s", 0, 96), (V("sz", NT + NB, NT + NI), oal), 1.0, 3 + SB / 1024.0)
     tt(V("pay1", 0, 96), (V("id4", 0, NL), oal), V("p1s", 0, 96), A.add)
-    fold(V("th", 0, 1536), ll, 24, "fp0", "f0")
+    fold("th", ll, 24, "fp0", "f0", ON["c0"])
     quant("fq0", "fs0", 0, 128, V("f0", 0, 512))
     layer(0, "fq0", "fs0", 96, lists0, "xa")
 
     quant("q1", "s1", NL, NN, V("xa", 768, 1536))
     p1 = mm(4, "uq2", "us2", 0, "q1", "s1", NL, NN)
     quant("q1", "s1", 0, NL, V("xa", 0, 768))
-    unpack("q1", "s1", 0, 0, *[("xh", 0.5), ("xb", 1.0)][1 - ON["xh"]:])
+    unpack("q1", "s1", 0, 0, ("xh", 0.5), ("xb", 1.0))
     ts(V("ft1", NB, NI - 1), sub(p1, 0, NL - 1), 0.0, A.is_gt)
-    tt(V("g1", 0, 480), (V("ft1", 0, NI + NB), sub(ofb, 30, 60)), V("b1", 0, 480), A.mult)
+    for a, b in ((0, 24), (24, 30)):
+        tt(V("g1", 16 * a, 16 * b), (V("ft1", 0, NI + NB), sub(ofb, 30 + a, 30 + b)), V("b1", 16 * a, 16 * b), A.mult)
     scan(V("ss1", 0, NN), V("g1", 0, NN), V("zero", 0, NN), 0.0, A.add, A.add)
     tt(V("num1", 0, 96), (V("ss1", 0, NN), olp), V("g1", NN, 480), A.add)
     on1 = new("off", 6)
@@ -533,20 +542,15 @@ def build(T, topo, core, rank):
     cp((V("sort1", 0, 96), on1), V("pay1", 0, 96))
     lst1 = new("off", 24)
     fold_lists("sort1", 96, lst1)
-    if ON["xh"]:
-        fold(V("xh", 0, 1536), lst1, 12, "fp1", "f1")
-    else:
-        fold(V("xb", 0, 1536), lst1, 12, "fp1", "fsum")
-        ts(V("f1", 0, NL), V("fsum", 0, NL), 0.5, A.mult)
+    fold("xh", lst1, 12, "fp1", "f1", ON["c1"])
     quant("fq1", "fs1", 0, 128, V("f1", 0, 512))
     gq, gs = V("lq", 0, 48), V("ls", 0, 48)
-    arrive("ag", [gq, gs], [send(peer[1], gq, V("fq1", 0, 48), "ag"), send(peer[1], gs, V("fs1", 0, 48), "ag")], 2300)
+    arrive("ag", [gq, gs], [send(peer[1], gq, V("fq1", 0, 48), "ag"), send(peer[1], gs, V("fs1", 0, 48), "ag")], 2800)
     lists1 = rake(1, "sort1", 96, "xb")
     fxd, i1, i2, i3, ok = new("sm", 12), new("sm", 12), new("sm", 12), new("sm", 24), new("off", 24)
     tt(fxd, deal(V("ft1", NB, NI)), deal(V("ft0", NB, NI)), A.not_equal)
-    act(i1, fxd, float(SB))
-    act(V("fb", 0, NL), V("rm", NI, NT), fn=AF.Sign)
-    act(V("gone", 0, NL), V("fb", 0, NL), float(SB), float(SB))
+    ts(i1, fxd, float(SB), A.mult)
+    ts(V("gone", 0, NL), V("rm", 2 * NT + NI, 3 * NT), 126.5, A.is_lt, 2.0 * SB, A.mult)
     tt(i2, deal(V("gone", 0, NL)), kidc, A.add)
     tt(sub(i3, 0, 12), i2, i1, A.add)
     tt(sub(i3, 12, 24), i2, i1, A.subtract)
@@ -557,14 +561,13 @@ def build(T, topo, core, rank):
     layer(1, "lq", "ls", 48, lists1, "xb")
 
     for h in range(2):
-        a, b = NL * h, NL * h + NL
+        a, b = (0, ON["cut"], NN)[h:h + 2]
         quant("q2", "s2", a, b, V("xb", 4 * a, 4 * b))
-        o = mm(h, "vq", "vs", 0, "q2", "s2", a, b)
-        get(ON["y"][h], V("yo", a, b), o)
-        dma("y" if h else "s", T.y[:, a:b], T.yo[:, a:b], [], [V("yo", a, b)], 2400)
-        dma("y", T.oc[:, 4 * a:4 * b], T.q2[:, a:b].bitcast(dt.uint8), [], [V("q2", a, b)], 2400)
+        get(ON["y"][h], V("yo", a, b), mm(h, "vq", "vs", 0, "q2", "s2", a, b))
+    dma("y", T.oc[:], T.q2[:].bitcast(dt.uint8), [], [V("q2", 0, NN)], 2600)
     for k in range(4):
-        dma("s" if k % 2 else "y", T.osc[4 * k:4 * k + 4, :], T.s2[32 * k:32 * k + 4, :], [], [V("s2", 0, NN)], 1600)
+        dma("y", T.osc[4 * k:4 * k + 4, :], T.s2[32 * k:32 * k + 4, :], [], [V("s2", 0, NN)], 2300)
+    dma("s", T.y[:], T.yo[:], [], [V("yo", 0, NN)], 2400)
     return ops, count
 
 
@@ -601,13 +604,21 @@ def arrange(ops):
     if _ORDER:
         return _ORDER
     n = len(ops)
-    before, after = [sorted(o["d"]) for o in ops], [[] for o in ops]
+    before, after, behind = [], [[] for o in ops], []
+    for i, o in enumerate(ops):
+        seen, near = set(), []
+        for j in sorted(o["d"], reverse=True):
+            if j not in seen:
+                near.append(j)
+                after[j].append(i)
+                seen |= behind[j] | {j}
+        before.append(near)
+        behind.append(seen)
     tail = [0.0] * n
     for i in reversed(range(n)):
         tail[i] += ops[i]["c"] + ops[i]["l"] + WAKE
         for j in before[i]:
             tail[j] = max(tail[j], tail[i])
-            after[j].append(i)
 
     def settle(key):
         key = pack(ops, after, before, pack(ops, before, after, key, False)[1], True)[1]
@@ -622,8 +633,8 @@ def arrange(ops):
 
     best = now = settle(tail)
     for _ in range(TRIES):
-        mid, wide, far = draw() * max(now[2]), 1500 * 2 ** int(3 * draw()), 2000 * draw()
-        got = settle([k + far * (draw() - 0.5) if abs(k - mid) < wide else k for k in now[2]])
+        mid, wide = draw() * max(now[2]), 1500 * 2 ** int(3 * draw())
+        got = settle([k + 3500 * (draw() - 0.5) * draw() ** 2 if abs(k - mid) < wide else k for k in now[2]])
         if got[0] <= now[0] + 30:
             now = got
         if got[0] < best[0]:
@@ -637,7 +648,10 @@ def rank_program(g, core, T, topo):
     if rank is None:
         return
     ops, count = build(T, topo, core, rank)
-    order = arrange(ops)
+    order = list(arrange(ops))
+    spots = [k for k, i in enumerate(order) if ops[i]["k"] == "d" and ops[i]["e"] == "y" and not ops[i]["r"]]
+    for k, i in zip(spots, sorted(order[k] for k in spots)):
+        order[k] = i
     place = {i: k for k, i in enumerate(order)}
     assert all(place[j] < place[i] for i, o in enumerate(ops) for j in o["d"])
     queue = {"v": g.vector, "s": g.scalar, "t": g.tensor, "y": g.sync, "g": g}

@@ -1,3 +1,5 @@
+import math
+
 from concourse.mybir import dt, AluOpType as A, ActivationFunctionType as AF
 
 F32, BF, F16, I32, U16, C4X, U8 = "float32", "bfloat16", "float16", "int32", "uint16", "float8_e4m3fn_x4", "uint8"
@@ -9,10 +11,10 @@ NI = NL + NB
 SB = 256
 K = 1024.0
 M = 8388864.0
-CY, GA, SC, WAKE, FIX = 0.955, 1.67, 3.63, 140, 40
-TRIES = 9000
-ON = {"sx": "ss", "sz": "ss", "ch": "ss", "fb": "s", "pv": 10, "y": "sv", "relu": "svsv", "jv": [6] * 7, "gw": 2, "pc": "v", "cc": "ss",
-      "mk": "vv", "bt": "s", "c0": [0, 8, 16, 24], "c1": [0, 4, 12], "cut": 240, "lh": [1, 1]}
+CY, GA, SC, WAKE, FIX = 1.0, 1.7, 3.7, 160, 50
+TRIES, SEED = 28000, 3
+ON = {"pv": 12, "relu": "svsv", "mk": "sv", "jc": [0, 8, 16, 24], "x0": 6, "fv": 12, "c1": [0, 6, 12], "cut": 232, "sp": 6, "sx": "sv",
+      "sz": "ss", "y": "sv", "bt": "s"}
 
 
 def _sb(n, d=F32):
@@ -25,25 +27,26 @@ SCRATCH = {
     "uq": _sb(128, C4X), "us": _sb(128, U8), "uq2": _sb(128, C4X), "us2": _sb(128, U8),
     "vq": _sb(128, C4X), "vs": _sb(128, U8),
     "q0": _sb(NN, C4X), "s0": _sb(NN, U8), "q1": _sb(NN, C4X), "s1": _sb(NN, U8), "q2": _sb(NN, C4X), "s2": _sb(NN, U8),
-    "lq": _sb(NN + 48, C4X), "ls": _sb(NN + 48, U8), "ll": _sb(48, U16), "lst0": _sb(48, U16),
+    "lq": _sb(NN + 48, C4X), "ls": _sb(NN + 48, U8), "ll": _sb(24, U16), "lst0": _sb(24, U16), "lp": _sb(12, U16), "lpo": _sb(12, U16),
     "fq0": _sb(128, C4X), "fs0": _sb(128, U8), "fq1": _sb(128, C4X), "fs1": _sb(128, U8),
     "z": _sb(520, BF), "one": _sb(128, BF), "zero": _sb(NN, BF),
-    "th": _sb(1536, BF), "xa": _sb(3072, BF), "xb": _sb(3072, BF), "xh": _sb(1536, BF),
-    "f0": _sb(512, BF), "f1": _sb(512, BF), "fp0": _sb(384, BF), "fp1": _sb(192, BF),
-    "ih0": _sb(1536, BF), "ih1": _sb(768, BF), "vb0": _sb(384, BF), "vb1": _sb(192, BF), "alt": _sb(768, BF),
-    "c16": _sb(NN, BF), "c4": _sb(NL, BF), "cj": _sb(96, BF), "cst": _sb(192), "csi": _sb(32, I32),
-    "rp": _sb(448), "id4": _sb(NL), "slot": _sb(NN), "zz": _sb(640, BF), "w": _sb(9 * 512, BF), "pos": _sb(448, BF),
-    "ch": _sb(976), "ix": _sb(448), "sx": _sb(NN), "sz": _sb(3 * NT), "sp": _sb(96), "een": _sb(NL),
+    "th": _sb(768, BF), "fi": _sb(1536, BF), "fo": _sb(1552, BF), "xa": _sb(3072, BF), "xb": _sb(3072, BF), "xh": _sb(1536, BF),
+    "f0": _sb(512, BF), "f1": _sb(512, BF), "fp1": _sb(192, BF),
+    "ih0": _sb(1536, BF), "ih1": _sb(768, BF), "vb0": _sb(384, BF), "vb1": _sb(192, BF), "alt": _sb(NN, BF),
+    "c16": _sb(NN, BF), "c4": _sb(NL, BF), "cj": _sb(96, BF), "cst": _sb(192), "csi": _sb(48, I32),
+    "rp": _sb(2 * NT), "id4": _sb(NL), "slot": _sb(NN, BF), "tb": _sb(2 * NT, BF), "zz": _sb(640, BF), "w": _sb(9 * 512, BF), "pos": _sb(448, BF),
+    "ch": _sb(976), "ix": _sb(448), "sx": _sb(NN), "sz": _sb(2 * NT), "een": _sb(NL),
     "pay": _sb(NN), "sc": _sb(NN), "ss": _sb(NN), "ol": _sb(NL), "lqr": _sb(NL, BF), "num": _sb(NL, BF), "pay0": _sb(NL),
-    "sort0": _sb(NL), "sort1": _sb(96), "rm": _sb(4 * NT, BF), "af0": _sb(192), "af1": _sb(128), "fa": _sb(NL, BF), "fb": _sb(NL, BF),
-    "ft0": _sb(NI + NB, BF), "ft1": _sb(NI + NB, BF), "gone": _sb(NL, BF), "lo": _sb(NL, BF), "ta": _sb(NT, BF),
-    "par": _sb(NL, BF), "asz": _sb(NT, BF), "bt": _sb(1024, BF), "b1": _sb(480, BF), "g1": _sb(480, BF), "ss1": _sb(NN, BF),
-    "lp1": _sb(96, BF), "num1": _sb(96, BF), "p1s": _sb(96), "pay1": _sb(96), "ab0": _sb(1056, BF), "ab1": _sb(704, BF),
-    "so": _sb(4096), "sh": _sb(8192, F16), "sm": _sb(768), "si": _sb(768, I32), "off": _sb(1024, U16),
+    "sort0": _sb(NL), "sort1": _sb(96), "rm": _sb(4 * NT, BF), "af0": _sb(192), "af1": _sb(128),
+    "fa": _sb(NI + NB, BF), "ft1": _sb(NI + NB, BF), "gone": _sb(NL, BF), "lo": _sb(NL, BF), "ta": _sb(NT, BF),
+    "par": _sb(NL, BF), "asz": _sb(NT, BF), "bt": _sb(976, BF), "b1": _sb(480, BF), "g1": _sb(480, BF), "ss1": _sb(NN, BF),
+    "lp1": _sb(96, BF), "num1": _sb(96, BF), "s1n": _sb(96, BF), "p1s": _sb(96), "pay1": _sb(96), "pt1": _sb(512), "id1": _sb(NL),
+    "ab0": _sb(1056, BF), "ab1": _sb(704, BF),
+    "so": _sb(2048), "sh": _sb(6656, F16), "sm": _sb(512), "si": _sb(512, I32), "off": _sb(1024, U16),
     "kido": _sb(NN), "yo": _sb(NN),
     "ps": ("psum", [128, 4096], F32),
 }
-SEMAPHORES = ["e%d" % i for i in range(140)] + ["ax", "al", "ag", "sent"]
+SEMAPHORES = ["e%d" % i for i in range(140)] + ["ax", "ap", "al", "ag", "sent"]
 
 
 def V(n, a, b, s=1):
@@ -107,8 +110,11 @@ def build(T, topo, core, rank):
         for i, o in enumerate(ops):
             if any(_meet(x, y) for x in w for y in o["r"] + o["w"]) or any(_meet(x, y) for x in r for y in o["w"]):
                 deps.add(i)
-        ops.append({"e": eng, "f": fn, "r": r, "w": w, "c": cost, "l": lat, "k": kind, "d": deps})
+        ops.append({"e": eng, "f": fn, "r": r, "w": w, "c": cost, "l": lat, "k": kind, "d": deps, "o": set()})
         return len(ops) - 1
+
+    def behind(i, *others):
+        ops[i]["o"] |= set(others)
 
     def sc(x):
         return ap(x) if isinstance(x, tuple) else x
@@ -133,8 +139,8 @@ def build(T, topo, core, rank):
     def plus(out, in0, c):
         return ts(out, in0, c, A.add)
 
-    def whole(out, d, m):
-        return ts(out, d, K, A.add, float(m), A.mult)
+    def whole(out, d, m, c=0.0):
+        return ts(out, d, K + c, A.add, float(m), A.mult)
 
     def bits(out, in0, shift, mask):
         if shift:
@@ -168,10 +174,18 @@ def build(T, topo, core, rank):
             return cp(out, src)
         return lin(out, src, scale, bias)
 
+    def share(out, win, lst, nv, scale=1.0, bias=0.0):
+        for q, a, b in (("v", 0, nv), ("s", nv, _len(lst))):
+            if a < b:
+                get(q, sub(out, 16 * a, 16 * b), (win, sub(lst, a, b)), scale, bias)
+
     def scan(out, d0, d1, init, o0, o1):
         n = _len(out)
         return add("v", lambda q: q.tensor_tensor_scan(ap(out), ap(d0), ap(d1), init, o0, o1), [out], [d0, d1],
                    max(64, n / 2 if two(out, d0, d1) else n) * CY)
+
+    def pairs(out, src):
+        return scan(out, V("alt", 0, _len(src)), src, 0.0, A.mult, A.add)
 
     def deal(src, blk=16, pat=None):
         n = _len(src)
@@ -193,7 +207,7 @@ def build(T, topo, core, rank):
 
     def quant(q, s, a, b, src):
         o, p = V(q, a, b), V(s, a, b)
-        return add("v", lambda e: e.quantize_mx(ap(o), ap(p), ap(src)), [o, p], [src], 1.25 * (12 + 0.22 * 4 * (b - a)))
+        return add("v", lambda e: e.quantize_mx(ap(o), ap(p), ap(src)), [o, p], [src], 13 + (b - a))
 
     def mm(bank, lq, ls, la, rq, rs, a, b):
         o, i = V("ps", 512 * bank, 512 * bank + b - a), [V(lq, la, la + 128), V(ls, la, la + 128), V(rq, a, b), V(rs, a, b)]
@@ -225,7 +239,7 @@ def build(T, topo, core, rank):
     peer = [T.cores[rank ^ 1], T.cores[rank ^ 2]]
 
     dma("y", T.kw[:, 0:12], T.ka[:], [V("kw", 0, 12)], [], 1900)
-    dma("s", T.kw[:, 12:24], T.kb[:], [V("kw", 12, 24)], [], 2100)
+    dma("s", T.kw[:, 12:24], T.kb[:], [V("kw", 12, 24)], [], 1900)
     dma("y", T.uin[:], T.u[:], [V("uin", 0, 512)], [], 2700)
     dma("y", T.xin[:, 768:1536], T.x[:, 768:1536], [V("xin", 768, 1536)], [], 3400)
     xl = dma("y", T.xin[:, 0:768], T.x[:, 0:768], [V("xin", 0, 768)], [], 4100)
@@ -234,59 +248,67 @@ def build(T, topo, core, rank):
     dma("y", T.vin[:], T.v[:], [V("vin", 0, 512)], [], 3800, [xl])
 
     pi, pc = V("csi", 0, 1), V("cst", 0, 8)
-    iota(pi, [[1, 1]], 0, 1)
+    first = iota(V("rp", 0, 112), [[1, 112]], 0)
+    behind(iota(pi, [[1, 1]], 0, 1), first)
     bits(V("csi", 2, 3), pi, 0, 15)
     bits(V("csi", 3, 4), pi, 2, 3)
     bits(V("csi", 4, 5), pi, 0, 3)
     cp(V("cst", 0, 3), V("csi", 2, 5))
     p16, p4, pt, pk, ptk, ptj, pb, p32 = [sub(pc, i, i + 1) for i in range(8)]
-    for out, src, m, c in ((ptk, pt, 1, 4 * K + 4 * NL), (ptj, pt, 1, 8 * K + 4 * NL), (pb, pt, 2, 1), (p32, p16, 2, 0), (pk, p16, 1, K)):
-        get(ON["pc"], out, src, float(m), float(c))
-    j16, j4 = V("cst", 8, 40), V("cst", 40, 72)
-    iota(j16, [[1, 2], [1, 16]], 0)
+    ptf = V("cst", 176, 177)
+    for out, src, m, c in ((ptk, pt, 1, 4 * K + 4 * NL), (ptj, pt, 1, 8 * K + 4 * NL), (pb, pt, 2, 1), (p32, p16, 2, 0), (pk, p16, 1, K),
+                           (ptf, pt, -NN, 2 * M)):
+        lin(out, src, float(m), float(c))
+    jp, j16, j4 = V("csi", 16, 48), V("cst", 8, 40), V("cst", 40, 72)
+    iota(jp, [[1, 2], [1, 16]], 128, -1)
+    bits(jp, jp, 0, 15)
+    ts(j16, jp, 0.0, A.is_equal, K, A.mult)
+    tt(V("c16", 0, 15), sub(j16, 0, 15), sub(j16, 16, 31), A.subtract)
+    plus(V("c16", 15, 16), sub(j16, 15, 16), -2 * K)
     iota(j4, [[1, 2], [0, 4], [1, 4]], 0)
-    for c, j, p, blk, top in (("c16", j16, p16, 16, NN), ("c4", j4, p4, 4, NL)):
-        ts(j, j, p, A.is_equal, K, A.mult)
-        tt(V(c, 0, 16), sub(j, 0, 16), sub(j, 16, 32), A.subtract)
-        plus(V(c, blk - 1, 16, blk), V(c, blk - 1, 16, blk), -2 * K)
-        n = 16
-        while n < top:
-            k = min(n, top - n)
-            get(ON["cc"][blk == 4], V(c, n, n + k), V(c, 0, k))
-            n += k
+    ts(j4, j4, p4, A.is_equal, K, A.mult)
+    tt(V("c4", 0, 16), sub(j4, 0, 16), sub(j4, 16, 32), A.subtract)
+    plus(V("c4", 3, 16, 4), V("c4", 3, 16, 4), -2 * K)
+    for c in ("c16", "c4"):
+        for n, top in ((16, 64), (64, NL)):
+            for a in range(n, top, n):
+                cp(V(c, a, a + n), V(c, 0, n))
+    cp(V("c16", NL, NN), V("c16", 0, NL))
     own, kidc, tsp = V("cst", 104, 128), V("cst", 128, 140), V("cst", 152, 176)
     for out, pat, base, p in ((own, [[SB, 2], [16, 12]], NL, p16), (kidc, [[16, 12]], NB, p16), (tsp, [[32, 24]], -int(K), p32)):
         iota(out, pat, base)
-        get(ON["pc"], out, out, 1.0, p)
-    iota(V("rp", 0, 112), [[1, 112]], 0)
+        plus(out, out, p)
     for a in (112, 224):
         ramp(V("rp", a, 2 * a), a)
-    ramp(V("slot", 0, NL), NB / 1024.0 - 3, 1 / 1024.0)
-    ramp(V("slot", NL, NN), (SB + NB) / 1024.0 - 3, 1 / 1024.0)
+    ramp(V("slot", 0, NL), -NL)
+    ramp(V("slot", NL, NN), SB - NL)
     ramp(V("zz", NL + 1, 640), NL + 1 - NN)
     ms(V("zz", NL, NL + 1), -256.0)
-    ms(V("sz", NT, NT + NB), 0.0)
-    ms(V("sz", 2 * NT - 1, 2 * NT), NI / 1024.0 - 3)
+    ms(V("tb", 0, NB), 0.0)
+    ms(V("tb", NT - 1, NT), 0.0)
     for k in range(9):
-        if k < ON["gw"]:
+        if k == 8:
+            ramp(V("w", 512 * k, 512 * k + 128), 0.0, 0.5)
+        elif k < 2:
             ramp(V("w", 512 * k, 512 * k + 128), 2 ** k - 256)
         else:
             iota(V("w", 512 * k, 512 * k + 128), [[1, 128]], 2 ** k - 256)
     iota(V("csi", 8, 16), [[16, 8]], 0)
     ou = new("off", 8)
     cp(ou, V("csi", 8, 16))
-    for name, a, b, c in (("fa", NL - 1, NL, 0), ("ft0", 0, NB, 0), ("ft0", NI, NI + NB, 0), ("ix", NL, SB, 2 * NT - 1), ("pos", NL, SB, 0),
+    for name, a, b, c in (("fa", 0, NB, 0), ("fa", NI - 1, NI + NB, 0), ("ix", NL, SB, 2 * NT - 1), ("pos", NL, SB, 0),
                           ("ch", 0, NB, 0), ("ch", NI, NB + SB, 0), ("ch", NI + SB, 480, NB - 1), ("asz", 0, NB, 0),
-                          ("bt", 0, NB, 0), ("bt", NI, NB + SB, 0), ("bt", NI + SB, 512, 0), ("f0", NN, 512, 0),
+                          ("bt", 0, NB, 0), ("bt", NI, NB + SB, 0), ("bt", NI + SB, 512 + NB, 0), ("f0", NN, 512, 0),
                           ("rm", 2 * NT, 4 * NT, 127)):
         fill(V(name, a, b), c)
-    iota(V("id4", 0, NL), [[4, NL]], 3)
+    iota(V("id4", 0, NL), [[2, NL]], 0)
     iota(V("rm", 0, 2 * NT), [[0, 2], [1, NT]], -NI)
     iota(V("ab0", 192, 288), [[1, 96]], 0)
     iota(V("ta", 0, NT), [[1, NT // 4], [0, 4]], 0)
     iota(V("par", 0, NL), [[0, NL // 2], [-1, 2]], 1)
-    iota(V("alt", 0, 768), [[0, 384], [1, 2]], 0)
-    act(V("cj", 0, 96), V("c16", 0, 96))
+    iota(V("alt", 0, NN), [[0, NL], [1, 2]], 0)
+    ramp(V("id1", 0, NL), 0.0, 1 / 1024.0)
+    cp(V("cj", 0, 96), V("c16", 0, 96))
     tt(V("cj", 15, 96, 16), V("c16", 15, 96, 16), V("rp", 0, 96, 16), A.add)
     ms(V("z", 0, 520), 0.0)
     ms(V("one", 0, 128), 1.0)
@@ -302,80 +324,91 @@ def build(T, topo, core, rank):
     ts(m_, kw, float(NL), A.is_ge, float(SB + NL), A.mult)
     tt(t_, kw, m_, A.add)
     tt(y_, t_, own, A.max)
-    plus(sub(oz, 12, 24), sub(y_, 12, 24), -float(NL + SB))
-    plus(sub(oz, 0, 12), sub(y_, 0, 12), -float(NL))
-    cp((V("sz", NT, 2 * NT - 1), oc), V("slot", 0, NN))
+    first = [plus(sub(oz, 12, 24), sub(y_, 12, 24), -float(NL + SB)), plus(sub(oz, 0, 12), sub(y_, 0, 12), -float(NL))]
+    behind(cp((V("tb", 0, NT - 1), oc), V("slot", 0, NN)), first[0])
     act(V("zz", 0, NL), (V("zz", SB, 640), sub(oz, 12, 24)))
     act(V("w", 320, 512), (V("zz", 0, 640), sub(oz, 0, 12)))
     osl = new("off", 24)
     oin, olf = sub(osl, 0, 12), sub(osl, 12, 24)
-    lin(oin, deal(V("sz", NT + NI, 2 * NT)), 1024.0, 1024 * (K + 3) - NB)
-    act(V("w", 128, 320), (V("zz", 0, 448), oin))
-    lin(olf, deal(V("sz", NT + NB, NT + NI)), 1024.0, 1024 * (K + 3) - NB)
+    plus(oin, deal(V("tb", NI, NT)), K + NL)
+    share(V("w", 128, 320), V("zz", 0, 448), oin, ON["x0"])
+    dlf, ilf, plf = deal(V("tb", NB, NI)), new("si", 12), new("si", 12)
+    plus(olf, dlf, K + NL)
+    plus(ilf, dlf, K + NL)
+    bits(plf, ilf, 0, 255)
+    cp(V("lpo", 0, 12), plf)
     for h in range(2):
-        get(ON["ch"][h], V("ch", NB + SB * h, NI + SB * h), (V("rp", 0, NT), sub(oc, 12 * h, 12 * h + 12)))
+        act(V("ch", NB + SB * h, NI + SB * h), (V("rp", 0, NT), sub(oc, 12 * h, 12 * h + 12)))
 
     quant("uq", "us", 0, 128, V("uin", 0, 512))
     add("v", lambda q: q.tensor_copy(T.uq2[:].bitcast(dt.uint32), T.uq[:].bitcast(dt.uint32).indirect(ap(ou))),
-        [V("uq2", 0, 128)], [V("uq", 0, 128), ou], 50 + 200 * CY)
+        [V("uq2", 0, 128)], [V("uq", 0, 128), ou], 50 + 128 * GA)
     add("s", lambda q: q.activation(T.us2[:], T.us[:].indirect(ap(ou)), AF.Copy),
-        [V("us2", 0, 128)], [V("us", 0, 128), ou], 65 + 200 * CY)
+        [V("us2", 0, 128)], [V("us", 0, 128), ou], 65 + 128 * GA)
     quant("q0", "s0", NL, NN, V("xin", 768, 1536))
     p0 = mm(4, "uq2", "us2", 0, "q0", "s0", NL, NN)
     quant("q0", "s0", 0, NL, V("xin", 0, 768))
     lq, ls = V("lq", 48, 48 + NN), V("ls", 48, 48 + NN)
     arrive("ax", [lq, ls], [send(peer[0], lq, V("q0", 0, NN), "ax"), send(peer[0], ls, V("s0", 0, NN), "ax")], 9000)
+    arrive("ap", [V("lp", 0, 12)], [send(peer[0], V("lp", 0, 12), V("lpo", 0, 12), "ap")], 6000)
     quant("vq", "vs", 0, 128, V("vin", 0, 512))
 
-    def unpack(q, s, a, b0, *outs):
+    def unpack(q, s, *outs):
         for b in range(4):
-            o = mm(b0 + b, "eq", "es", 128 * b, q, s, a, a + NN)
+            o = mm(b, "eq", "es", 128 * b, q, s, 0, NN)
             for dst, scale in outs:
                 act(V(dst, b, 1536, 4), o, scale)
 
-    unpack("q0", "s0", 0, 0, ("xa", 1.0))
-    ts(V("fa", 0, NL - 1), sub(p0, 0, NL - 1), 0.0, A.is_gt, float(NT), A.mult)
-    get(ON["fb"], V("fb", 0, NL), V("fa", 0, NL), -1.0, float(NT))
-    tt(V("ix", SB, SB + NL), (V("rp", 0, NT), sub(oc, 0, 12)), V("fa", 0, NL), A.add)
-    tt(V("ix", 0, NL), (V("rp", 0, NT), sub(oc, 12, 24)), V("fb", 0, NL), A.add)
-    act(V("ft0", NB, NI), V("fa", 0, NL), fn=AF.Sign)
-    unpack("lq", "ls", 48, 4, ("th", 0.5))
+    unpack("q0", "s0", ("xa", 1.0))
+    ts(V("fa", NB, NI - 1), sub(p0, 0, NL - 1), 0.0, A.is_gt, float(NT), A.mult)
+    pieces = [(a, a + ON["sp"]) for a in range(0, 12, ON["sp"])]
+    dfa, ni, oi = deal(V("fa", NB, NI)), new("sm", 24), new("off", 24)
+    iota(V("rp", 448, 2 * NT), [[1, 2 * NT - 448]], 448)
+    tt(sub(ni, 0, 12), sub(kw, 0, 12), dfa, A.add)
+    tt(sub(ni, 12, 24), sub(kw, 12, 24), dfa, A.subtract)
+    plus(sub(oi, 0, 12), sub(ni, 0, 12), K + NB)
+    plus(sub(oi, 12, 24), sub(ni, 12, 24), NT + NB - K)
+    act(V("ix", SB, SB + NL), (V("rp", 0, 2 * NT), sub(oi, 0, 12)))
+    act(V("ix", 0, NL), (V("rp", 0, 2 * NT), sub(oi, 12, 24)))
     osx = new("off", 24)
     for h in range(2):
         get(ON["sx"][h], V("sx", NL * h, NL * h + NL), (V("ix", 0, 448), sub(osl, 12 * h, 12 * h + 12)))
         plus(sub(osx, 12 * h, 12 * h + 12), deal(V("sx", NL * h, NL * h + NL)), K)
     szw = V("sz", 0, 2 * NT)
-    get(ON["sz"][0], V("sz", 0, NI), V("sz", NT, NT + NI), 1.0, 2.5)
-    get(ON["sz"][1], V("sz", NI, NT), V("sz", NT + NI, 2 * NT), 1.0, 3.5)
-    tt(V("pay0", 0, NL), (szw, sub(osx, 12, 24)), V("id4", 0, NL), A.add)
+    act(V("sz", NT, 2 * NT), V("tb", 0, NT), 1 / 2048.0, NI / 2048.0 - 1)
+    get(ON["sz"][0], V("sz", 0, NI), V("tb", 0, NI), 1 / 2048.0, NI / 2048.0 + 0.25)
+    get(ON["sz"][1], V("sz", NI, NT), V("tb", NI, NT), 1 / 2048.0, NI / 2048.0 + 0.75)
+    for a, b in pieces:
+        ops[tt(V("pay0", 16 * a, 16 * b), (szw, sub(osx, 12 + a, 12 + b)), V("id4", 16 * a, 16 * b), A.add)]["l"] = 300
+    for b in range(4):
+        o, a = mm(4 + b, "eq", "es", 128 * b, "lq", "ls", 48, 48 + NN), NN * b
+        act(V("fi", a, a + NN, 2), sub(o, 0, NL), 0.5)
+        act(V("th", NL * b, NL * b + NL), sub(o, NL, NN), 0.5)
+        act(V("fi", a + 1, a + NN, 2), (V("th", NL * b, NL * b + NL), V("lp", 0, 12)))
+        pairs(V("fo", a + 15, a + 15 + NN), V("fi", a, a + NN))
 
     op = None
+    parts = list(zip(ON["jc"], ON["jc"][1:]))[::-1]
     for k in range(8):
-        win = V("w", 512 * k, 512 * k + 512)
-        op = new("off", 24)
-        nv = ON["jv"][k] if k < 7 else 12
-        cuts = [0, nv, (24 + nv) // 4 * 2, 24] if 0 < nv < 12 else [0, 12, 24]
-        parts = list(zip(cuts, cuts[1:]))[::-1]
+        win, op = V("w", 512 * k, 512 * k + 512), new("off", 24)
         for a, b in parts:
             plus(sub(op, a, b), deal(V("w", 512 * k + 128 + 16 * a, 512 * k + 128 + 16 * b)), K + 256)
         for a, b in parts:
-            get("v" if b == nv else "s", V("w", 512 * k + 640 + 16 * a, 512 * k + 640 + 16 * b), (win, sub(op, a, b)))
+            get("s" if a else "v", V("w", 512 * k + 640 + 16 * a, 512 * k + 640 + 16 * b), (win, sub(op, a, b)), 0.5 if k == 7 else 1.0)
     win = V("w", 512 * 8, 512 * 9)
     oex, oen = sub(op, 0, 12), sub(op, 12, 24)
     tt(V("een", 0, NL), (win, oen), V("sz", NI, NT), A.subtract)
     tt(V("sz", NI, NT), (win, oex), V("een", 0, NL), A.subtract)
-    act(V("pos", 0, NL), (win, oen))
-    act(V("pos", SB, SB + NL), (win, oex), 1.0, -1.0)
+    act(V("pos", 0, NL), (win, oen), 2.0)
+    act(V("pos", SB, SB + NL), (win, oex), 2.0, -1.0)
     opos = new("off", 24)
     den, dex = deal(V("pos", 0, NL)), deal(V("pos", SB, SB + NL))
     plus(sub(opos, 0, 12), den, K + 256)
     plus(sub(opos, 12, 24), dex, K + 257)
-    act(V("pay", 0, NL), (szw, sub(osx, 0, 12)), 0.5, 1.5)
-    for e, a, b in (("v", 0, ON["pv"]), ("s", ON["pv"], 12)):
-        if a < b:
-            get(e, V("pay", NL + 16 * a, NL + 16 * b), (szw, sub(osx, a, b)), -0.5, -1.5)
+    act(V("pay", 0, NL), (szw, sub(osx, 0, 12)), 1.0, 1.0)
+    share(V("pay", NL, NN), szw, sub(osx, 0, 12), ON["pv"], -1.0, -1.0)
     cp((V("sc", 0, NN), opos), V("pay", 0, NN))
-    act(V("ol", 0, NL), (szw, sub(osx, 12, 24)), 0.5, 1 - M)
+    act(V("ol", 0, NL), (szw, sub(osx, 12, 24)), 1.0, 1 - M)
     act(V("lqr", 0, NL), (V("pos", 0, 448), olf))
     olq = new("off", 12)
     plus(olq, deal(V("lqr", 0, NL)), K + 256)
@@ -385,18 +418,7 @@ def build(T, topo, core, rank):
     plus(onum, deal(V("num", 0, NL)), K)
     cp((V("sort0", 0, NL), onum), V("pay0", 0, NL))
 
-    def fold_lists(sort, m, lst):
-        e = m // 8
-        i4, lp = new("si", e), new("si", 2 * e)
-        whole(i4, deal(V(sort, 1, m, 2), 4), 1024)
-        bits(sub(lp, e, 2 * e), i4, 0, 255)
-        bits(sub(lp, 0, e), i4, 12, 255)
-        lin(lst, lp, 4.0, pt)
-
-    def fold(x, lst, e, tmp, out, cuts):
-        for a, b in zip(cuts, cuts[1:]):
-            act(V(tmp, 16 * a, 16 * b), (V(x, 4 * (NL - NB), 1536), sub(lst, e + a, e + b)))
-            tt(V(out, 16 * a, 16 * b), (V(x, 0, 768), sub(lst, a, b)), V(tmp, 16 * a, 16 * b), A.add)
+    step = {}
 
     def rake(r, sort, m, x):
         n, c, e = m // 2, m // 32, m // 8
@@ -405,13 +427,22 @@ def build(T, topo, core, rank):
         part = [V(ab, n2 * i, n2 * i + n2) for i in range(11)]
         col = lambda v, i, k=1: sub(v, c2 * i, c2 * (i + k))
         i0, o0 = V("si", 0, 16) if r else new("si", 4 * c2), new("off", 3 * c2)
-        whole(sub(i0, 0, c), deal(V(sort, 1, m, 2)), 1024)
-        bits(col(i0, 1), col(i0, 0), 0, 511)
-        bits(col(i0, 2), col(i0, 0), 0, 255)
-        bits(col(i0, 3), col(i0, 0), 9, 1)
+        if r == 0:
+            whole(col(i0, 0), deal(V(sort, 1, m, 2)), 2048, 1.0)
+            behind(len(ops) - 2, step["list"])
+            bits(col(i0, 1), col(i0, 0), 0, 511)
+            bits(col(i0, 2), col(i0, 0), 0, 255)
+            bits(col(i0, 3), col(i0, 0), 9, 1)
+        else:
+            other = new("sm", c2)
+            whole(sub(i0, 0, c), deal(V(sort, 1, m, 2)), 1024)
+            bits(col(i0, 2), col(i0, 0), 12, 255)
+            bits(col(i0, 3), col(i0, 0), 8, 1)
+            lin(other, col(i0, 3), -float(SB), float(SB))
+            tt(col(i0, 1), col(i0, 2), other, A.add)
         cp(col(o0, 0, 2), col(i0, 1, 2))
         osib, opar = col(o0, 0), col(o0, 1)
-        act(part[0], (V("sz", NT + NL, 2 * NT), opar), 1024.0, 3072.0 - NI)
+        act(part[0], (V("tb", NL, NT), opar))
         act(part[1], (V("ch", 0, 480), osib), 1.0, -float(NI))
         if r == 0:
             plus(col(o0, 2), col(i0, 2), 2.0 * NT)
@@ -424,7 +455,7 @@ def build(T, topo, core, rank):
         if r == 0:
             right = col(i0, 3)
         else:
-            act(part[3], (V("ft0", 0, NI + NB), opar))
+            act(part[3], (V("fa", 0, NI + NB), opar), fn=AF.Sign)
             act(part[4], (V("ft1", 0, NI + NB), opar))
             d1, r1, right = deal(V(ab, 3 * n2, 5 * n2)), new("sm", c2), new("sm", c2)
             tt(r1, col(d1, 0), col(d1, 1), A.not_equal)
@@ -467,8 +498,7 @@ def build(T, topo, core, rank):
             st, ost = new("sm", c), new("off", c)
             tt(st, sub(d, c, 2 * c), sub(d, 0, c), A.add)
             plus(ost, st, 2 * K + NI)
-            act(V("sp", 0, n), part[0], 1 / 1024.0, NI / 1024.0 - 3)
-            cp((V("sz", NT, 3 * NT), ost), V("sp", 0, n))
+            step["slots"] = cp((V("tb", 0, 2 * NT), ost), part[0])
         return ob, otg
 
     def layer(r, gq, gs, n, lists, x):
@@ -480,21 +510,20 @@ def build(T, topo, core, rank):
                 ts(dst, o, 0.0, A.max, 0.03125, A.mult)
             else:
                 act(dst, o, 0.03125, fn=AF.Relu)
-        e = n // 4 // ON["lh"][r]
-        for a in range(0, n // 4, e):
-            b = a + e
-            scan(V(ih, 8 * n + 32 * a, 8 * n + 32 * b), V("alt", 0, 32 * e), V(ih, 32 * a, 32 * b), 0.0, A.mult, A.add)
+        for a, b in ((0, n // 8), (n // 8, n // 4)):
+            pairs(V(ih, 8 * n + 32 * a, 8 * n + 32 * b), V(ih, 32 * a, 32 * b))
             tt(sub(vb, 16 * a, 16 * b), (V(ih, 8 * n, 8 * n + 32 * b), sub(lists[0], a, b)), V(ih, 32 * a + 1, 32 * b, 2), A.add)
-            cp((V(x, 0, 3072), sub(lists[1], a, b)), sub(vb, 16 * a, 16 * b))
+        cp((V(x, 0, 3072), lists[1]), vb)
 
-    lst0, ll = V("lst0", 0, 48), V("ll", 0, 48)
-    fold_lists("sort0", NL, lst0)
+    lst0, ll = V("lst0", 0, 24), V("ll", 0, 24)
+    step["list"] = ts(lst0, deal(V("sort0", 1, NL, 2), 4), 2 * M + K, A.add, ptf, A.subtract) - 1
     sl = send(peer[0], ll, lst0, "al")
     arrive("al", [ll], [sl], 2000)
-    late = [fill(V(name, a, b), c) for name, a, b, c in (
-        ("zero", 0, NN, 0), ("ft1", 0, NB, 0), ("ft1", NI - 1, NI + NB, 0), ("si", 0, 16, 0), ("f1", NL, 512, 0), ("ch", 480, 976, NB - 1))]
-    for i in late + [iota(V("ab1", 128, 192), [[1, 64]], 0)]:
-        ops[i]["d"].add(sl)
+    for name, a, b, c in (("zero", 0, NN, 0), ("ft1", 0, NB, 0), ("ft1", NI - 1, NI + NB, 0), ("si", 0, 16, 0), ("f1", NL, 512, 0),
+                          ("ch", 480, 976, NB - 1)):
+        behind(fill(V(name, a, b), c), sl)
+    behind(iota(V("ab1", 128, 192), [[1, 64]], 0), sl)
+    behind(iota(V("pt1", 0, 512), [[1, 2], [16, SB]], 16 * NB), sl)
     lists0 = rake(0, "sort0", NL, "xa")
     act(V("lo", 0, NL), (V("ss", 0, NN), sub(opos, 0, 12)), 1.0, -M)
     l2, l3, dd, yy, oa = new("si", 12), new("si", 12), new("sm", 12), new("sm", 12), new("off", 12)
@@ -507,32 +536,35 @@ def build(T, topo, core, rank):
     act(V("asz", NB, NI), (V("par", 0, NL), onum))
     for h in range(2):
         act(V("bt", NB + SB * h, NI + SB * h), (V("asz", 0, NT), sub(oc, 12 * h, 12 * h + 12)))
-    get(ON["bt"], V("bt", 512, 1024), V("bt", 0, 512), -1.0)
+    get(ON["bt"], V("bt", 512 + NB, 512 + NI + SB), V("bt", NB, NI + SB), -1.0)
     dt_ = deal(V("sc", 0, NN))
     aa, sg, it, ib, ofb = new("sm", 24), new("sm", 24), new("si", 30), new("si", 66), new("off", 66)
     act(aa, dt_, 2048.0, 2048.0 * K, AF.Abs)
     ts(sg, dt_, -K, A.is_lt, 512.0, A.mult)
     tt(sub(it, 0, 24), aa, sg, A.add)
-    whole(sub(it, 24, 30), deal(V("sort0", 0, NL, 2)), 1024)
+    whole(sub(it, 24, 30), deal(V("sort0", 0, NL, 2)), 2048, 1.0)
     bits(sub(ib, 0, 30), it, 0, 1023)
     bits(sub(ib, 30, 60), it, 0, 255)
     bits(sub(ib, 60, 66), sub(it, 24, 30), 12, 255)
     cp(ofb, ib)
-    oal, olp = sub(ofb, 60, 66), new("off", 6)
-    act(V("b1", 0, 480), (V("bt", 0, 1024), sub(ofb, 0, 30)))
+    oal, olp, osn = sub(ofb, 60, 66), new("off", 6), new("off", 6)
+    act(V("b1", 0, 480), (V("bt", 0, 512 + NI + SB), sub(ofb, 0, 30)))
     act(V("lp1", 0, 96), (V("lqr", 0, NL), oal))
     plus(olp, deal(V("lp1", 0, 96)), K + 256)
-    act(V("p1s", 0, 96), (V("sz", NT + NB, NT + NI), oal), 1.0, 3 + SB / 1024.0)
-    tt(V("pay1", 0, 96), (V("id4", 0, NL), oal), V("p1s", 0, 96), A.add)
-    fold("th", ll, 24, "fp0", "f0", ON["c0"])
+    act(V("s1n", 0, 96), (V("tb", NB, NI), oal))
+    plus(osn, deal(V("s1n", 0, 96)), K + NL)
+    act(V("p1s", 0, 96), (V("pt1", 0, 512), osn), 0.25, pt)
+    tt(V("pay1", 0, 96), (V("id1", 0, NL), oal), V("p1s", 0, 96), A.add)
+    share(V("f0", 0, NN), V("fo", 16, 1551), ll, ON["fv"])
     quant("fq0", "fs0", 0, 128, V("f0", 0, 512))
     layer(0, "fq0", "fs0", 96, lists0, "xa")
 
     quant("q1", "s1", NL, NN, V("xa", 768, 1536))
     p1 = mm(4, "uq2", "us2", 0, "q1", "s1", NL, NN)
-    quant("q1", "s1", 0, NL, V("xa", 0, 768))
-    unpack("q1", "s1", 0, 0, ("xh", 0.5), ("xb", 1.0))
-    ts(V("ft1", NB, NI - 1), sub(p1, 0, NL - 1), 0.0, A.is_gt)
+    turn = ts(V("ft1", NB, NI - 1), sub(p1, 0, NL - 1), 0.0, A.is_gt)
+    behind(quant("q1", "s1", 0, NL, V("xa", 0, 768)), turn)
+    behind(turn, step["slots"])
+    unpack("q1", "s1", ("xh", 0.5), ("xb", 1.0))
     for a, b in ((0, 24), (24, 30)):
         tt(V("g1", 16 * a, 16 * b), (V("ft1", 0, NI + NB), sub(ofb, 30 + a, 30 + b)), V("b1", 16 * a, 16 * b), A.mult)
     scan(V("ss1", 0, NN), V("g1", 0, NN), V("zero", 0, NN), 0.0, A.add, A.add)
@@ -540,15 +572,21 @@ def build(T, topo, core, rank):
     on1 = new("off", 6)
     plus(on1, deal(V("num1", 0, 96), 16, V("cj", 0, 96)), pk)
     cp((V("sort1", 0, 96), on1), V("pay1", 0, 96))
-    lst1 = new("off", 24)
-    fold_lists("sort1", 96, lst1)
-    fold("xh", lst1, 12, "fp1", "f1", ON["c1"])
+    d, i4, l4, lst1 = deal(V("sort1", 1, 96, 2), 4), new("si", 12), new("si", 12), new("off", 24)
+    ts(sub(lst1, 12, 24), d, M + K, A.add, M, A.subtract)
+    whole(i4, d, 1024)
+    bits(l4, i4, 0, 255)
+    lin(sub(lst1, 0, 12), l4, 4.0, pt)
+    for a, b in zip(ON["c1"], ON["c1"][1:]):
+        act(V("fp1", 16 * a, 16 * b), (V("xh", 4 * (NL - NB), 1536), sub(lst1, 12 + a, 12 + b)))
+        tt(V("f1", 16 * a, 16 * b), (V("xh", 0, 768), sub(lst1, a, b)), V("fp1", 16 * a, 16 * b), A.add)
     quant("fq1", "fs1", 0, 128, V("f1", 0, 512))
     gq, gs = V("lq", 0, 48), V("ls", 0, 48)
     arrive("ag", [gq, gs], [send(peer[1], gq, V("fq1", 0, 48), "ag"), send(peer[1], gs, V("fs1", 0, 48), "ag")], 2800)
     lists1 = rake(1, "sort1", 96, "xb")
-    fxd, i1, i2, i3, ok = new("sm", 12), new("sm", 12), new("sm", 12), new("sm", 24), new("off", 24)
-    tt(fxd, deal(V("ft1", NB, NI)), deal(V("ft0", NB, NI)), A.not_equal)
+    f0d, fxd, i1, i2, i3, ok = new("sm", 12), new("sm", 12), new("sm", 12), new("sm", 12), new("sm", 24), new("off", 24)
+    ts(f0d, dfa, 1 - K, A.min)
+    tt(fxd, deal(V("ft1", NB, NI)), f0d, A.not_equal)
     ts(i1, fxd, float(SB), A.mult)
     ts(V("gone", 0, NL), V("rm", 2 * NT + NI, 3 * NT), 126.5, A.is_lt, 2.0 * SB, A.mult)
     tt(i2, deal(V("gone", 0, NL)), kidc, A.add)
@@ -571,32 +609,6 @@ def build(T, topo, core, rank):
     return ops, count
 
 
-def pack(ops, before, after, key, turned):
-    n = len(ops)
-    left = [len(b) for b in before]
-    ready = sorted((key[i], -i) for i in range(n) if not left[i])
-    start, done, busy = [0.0] * n, [0.0] * n, {}
-    while ready:
-        i = -ready.pop()[1]
-        c, lat = ops[i]["c"], ops[i]["l"]
-        t = max([done[j] + WAKE for j in before[i]] + [0.0]) + (lat if turned else 0.0)
-        gaps = busy.setdefault(ops[i]["e"], [])
-        k = len(gaps)
-        while k and gaps[k - 1][1] > t:
-            k -= 1
-        while k < len(gaps) and t + c > gaps[k][0]:
-            t = max(t, gaps[k][1])
-            k += 1
-        gaps.insert(k, (t, t + c))
-        start[i], done[i] = t, t + c + (0.0 if turned else lat)
-        for j in after[i]:
-            left[j] -= 1
-            if not left[j]:
-                ready.append((key[j], -j))
-        ready.sort()
-    return start, done
-
-
 _ORDER = []
 
 
@@ -604,42 +616,77 @@ def arrange(ops):
     if _ORDER:
         return _ORDER
     n = len(ops)
+    calls = range(n)
     before, after, behind = [], [[] for o in ops], []
     for i, o in enumerate(ops):
         seen, near = set(), []
-        for j in sorted(o["d"], reverse=True):
+        for j in sorted(o["d"] | o["o"], reverse=True):
             if j not in seen:
-                near.append(j)
-                after[j].append(i)
+                way = WAKE if j in o["d"] else 0.0
+                near.append((j, way))
+                after[j].append((i, way))
                 seen |= behind[j] | {j}
         before.append(near)
         behind.append(seen)
-    tail = [0.0] * n
-    for i in reversed(range(n)):
-        tail[i] += ops[i]["c"] + ops[i]["l"] + WAKE
-        for j in before[i]:
-            tail[j] = max(tail[j], tail[i])
+    queue, cost, lat, none = [o["e"] for o in ops], [o["c"] for o in ops], [o["l"] for o in ops], [0.0] * n
 
-    def settle(key):
-        key = pack(ops, after, before, pack(ops, before, after, key, False)[1], True)[1]
-        start, done = pack(ops, before, after, key, False)
+    queues = sorted(set(queue))
+
+    def pack(key, follows, first, then):
+        start, done, busy = [0.0] * n, [0.0] * n, {q: ([], []) for q in queues}
+        for t, i in sorted(zip(key, calls), reverse=True):
+            t = 0.0
+            for j, way in follows[i]:
+                if done[j] + way > t:
+                    t = done[j] + way
+            t += first[i]
+            (a, b), c = busy[queue[i]], cost[i]
+            k = m = len(a)
+            while k and b[k - 1] > t:
+                k -= 1
+            while k < m and t + c > a[k]:
+                if b[k] > t:
+                    t = b[k]
+                k += 1
+            a.insert(k, t)
+            b.insert(k, t + c)
+            start[i], done[i] = t, t + c + then[i] + 0.001
+        return start, done
+
+    def settle(key, both):
+        for i in calls:
+            for j, way in before[i]:
+                if key[i] >= key[j]:
+                    key[i] = key[j] - 0.01
+        start, done = pack(key, before, none, lat)
+        if both:
+            back = pack(done, after, lat, none)[1]
+            again, end = pack(back, before, none, lat)
+            if max(end) <= max(done):
+                return max(end), again, back
         return max(done), start, key
 
-    seed = [1]
+    seed = [SEED]
 
     def draw():
         seed[0] = seed[0] * 48271 % 2147483647
         return seed[0] / 2147483647.0
 
-    best = now = settle(tail)
-    for _ in range(TRIES):
-        mid, wide = draw() * max(now[2]), 1500 * 2 ** int(3 * draw())
-        got = settle([k + 3500 * (draw() - 0.5) * draw() ** 2 if abs(k - mid) < wide else k for k in now[2]])
-        if got[0] <= now[0] + 30:
+    tail = [0.0] * n
+    for i in reversed(calls):
+        tail[i] += cost[i] + lat[i] + WAKE
+        for j, way in before[i]:
+            tail[j] = max(tail[j], tail[i])
+    best = now = settle(tail, True)
+    for k in range(TRIES):
+        keys = now[2] if draw() < 0.5 else [now[0] - t for t in now[1]]
+        mid, wide, part = draw() * now[0], 800 * 2 ** int(4 * draw()), draw() ** 2
+        got = settle([t + 4000 * (draw() - 0.5) * draw() if abs(t - mid) < wide and draw() < part else t for t in keys], draw() < 0.6)
+        if got[0] <= now[0] - (35 - 30.0 * k / TRIES) * math.log(draw()):
             now = got
         if got[0] < best[0]:
             best = got
-    _ORDER.extend(sorted(range(n), key=lambda k: (best[1][k], k)))
+    _ORDER.extend(sorted(calls, key=lambda k: (best[1][k], k)))
     return _ORDER
 
 

import math

from concourse.mybir import dt, AluOpType as A, ActivationFunctionType as AF

F32, BF, F16, I32, U16, C4X, U8 = "float32", "bfloat16", "float16", "int32", "uint16", "float8_e4m3fn_x4", "uint8"
NL = 192
NN = 384
NB = 16
NT = NN + NB
NI = NL + NB
SB = 256
K = 1024.0
M = 8388864.0
CY, GA, SC, WAKE, FIX = 1.0, 1.7, 3.7, 160, 50
TRIES, SEED = 28000, 3
ON = {"pv": 12, "relu": "svsv", "mk": "sv", "jc": [0, 8, 16, 24], "x0": 6, "fv": 12, "c1": [0, 6, 12], "cut": 232, "sp": 6, "sx": "sv",
      "sz": "ss", "y": "sv", "bt": "s"}


def _sb(n, d=F32):
    return ("sbuf", [128, n], d)


SCRATCH = {
    "xin": _sb(1536, BF), "uin": _sb(512, BF), "vin": _sb(512, BF), "kw": _sb(24, I32),
    "wq": _sb(512, C4X), "wsc": _sb(512, U8), "eq": _sb(512, C4X), "es": _sb(512, U8),
    "uq": _sb(128, C4X), "us": _sb(128, U8), "uq2": _sb(128, C4X), "us2": _sb(128, U8),
    "vq": _sb(128, C4X), "vs": _sb(128, U8),
    "q0": _sb(NN, C4X), "s0": _sb(NN, U8), "q1": _sb(NN, C4X), "s1": _sb(NN, U8), "q2": _sb(NN, C4X), "s2": _sb(NN, U8),
    "lq": _sb(NN + 48, C4X), "ls": _sb(NN + 48, U8), "ll": _sb(24, U16), "lst0": _sb(24, U16), "lp": _sb(12, U16), "lpo": _sb(12, U16),
    "fq0": _sb(128, C4X), "fs0": _sb(128, U8), "fq1": _sb(128, C4X), "fs1": _sb(128, U8),
    "z": _sb(520, BF), "one": _sb(128, BF), "zero": _sb(NN, BF),
    "th": _sb(768, BF), "fi": _sb(1536, BF), "fo": _sb(1552, BF), "xa": _sb(3072, BF), "xb": _sb(3072, BF), "xh": _sb(1536, BF),
    "f0": _sb(512, BF), "f1": _sb(512, BF), "fp1": _sb(192, BF),
    "ih0": _sb(1536, BF), "ih1": _sb(768, BF), "vb0": _sb(384, BF), "vb1": _sb(192, BF), "alt": _sb(NN, BF),
    "c16": _sb(NN, BF), "c4": _sb(NL, BF), "cj": _sb(96, BF), "cst": _sb(192), "csi": _sb(48, I32),
    "rp": _sb(2 * NT), "id4": _sb(NL), "slot": _sb(NN, BF), "tb": _sb(2 * NT, BF), "zz": _sb(640, BF), "w": _sb(9 * 512, BF), "pos": _sb(448, BF),
    "ch": _sb(976), "ix": _sb(448), "sx": _sb(NN), "sz": _sb(2 * NT), "een": _sb(NL),
    "pay": _sb(NN), "sc": _sb(NN), "ss": _sb(NN), "ol": _sb(NL), "lqr": _sb(NL, BF), "num": _sb(NL, BF), "pay0": _sb(NL),
    "sort0": _sb(NL), "sort1": _sb(96), "rm": _sb(4 * NT, BF), "af0": _sb(192), "af1": _sb(128),
    "fa": _sb(NI + NB, BF), "ft1": _sb(NI + NB, BF), "gone": _sb(NL, BF), "lo": _sb(NL, BF), "ta": _sb(NT, BF),
    "par": _sb(NL, BF), "asz": _sb(NT, BF), "bt": _sb(976, BF), "b1": _sb(480, BF), "g1": _sb(480, BF), "ss1": _sb(NN, BF),
    "lp1": _sb(96, BF), "num1": _sb(96, BF), "s1n": _sb(96, BF), "p1s": _sb(96), "pay1": _sb(96), "pt1": _sb(512), "id1": _sb(NL),
    "ab0": _sb(1056, BF), "ab1": _sb(704, BF),
    "so": _sb(2048), "sh": _sb(6656, F16), "sm": _sb(512), "si": _sb(512, I32), "off": _sb(1024, U16),
    "kido": _sb(NN), "yo": _sb(NN),
    "ps": ("psum", [128, 4096], F32),
}
SEMAPHORES = ["e%d" % i for i in range(140)] + ["ax", "ap", "al", "ag", "sent"]


def V(n, a, b, s=1):
    return (n, a, b, s)


def _len(v):
    return (v[2] - v[1] + v[3] - 1) // v[3]


def _span(v):
    if v[0] == "ps":
        return ("ps", v[1] // 512 * 512, (v[2] + 511) // 512 * 512, 1)
    return v


def _meet(x, y):
    if x[0] != y[0] or x[2] <= y[1] or y[2] <= x[1]:
        return False
    return not (x[3] == y[3] and x[3] > 1 and (x[1] - y[1]) % x[3] != 0)


def build(T, topo, core, rank):
    ops = []
    used = {"sm": 0, "si": 16, "off": 0, "so": 0, "sh": 0}

    def new(n, k):
        a = used[n]
        used[n] = a + (k + 7) // 8 * 8
        assert used[n] <= SCRATCH[n][1][1]
        return V(n, a, a + k)

    def sub(v, a, b):
        return V(v[0], v[1] + a * v[3], min(v[2], v[1] + b * v[3]), v[3])

    def ap(v):
        if len(v) == 2:
            return ap(v[0]).indirect(ap(v[1]))
        if v[3] == 1:
            return T[v[0]][:, v[1]:v[2]]
        return T[v[0]][:, v[1]:v[2]:v[3]]

    def two(*vs):
        return all(SCRATCH[v[0]][2] in (BF, U16, F16) for v in vs)

    def add(eng, fn, outs, ins, cost, lat=0.0, kind="c", after=()):
        r, w = [], []
        for v in ins:
            if isinstance(v, tuple):
                r += list(v) if len(v) == 2 else [v]
        for v in outs:
            if len(v) == 2:
                w.append(v[0])
                r.append(v[1])
            else:
                w.append(v)
        w += [v for v in r if v[0] == "ps"]
        r = [_span(v) for v in r if v[0] != "ps"]
        w = [_span(v) for v in w]
        deps = set(after)
        for i, o in enumerate(ops):
            if any(_meet(x, y) for x in w for y in o["r"] + o["w"]) or any(_meet(x, y) for x in r for y in o["w"]):
                deps.add(i)
        ops.append({"e": eng, "f": fn, "r": r, "w": w, "c": cost, "l": lat, "k": kind, "d": deps, "o": set()})
        return len(ops) - 1

    def behind(i, *others):
        ops[i]["o"] |= set(others)

    def sc(x):
        return ap(x) if isinstance(x, tuple) else x

    def vcost(out, in0, n, plain):
        if len(in0) == 2:
            return 50 + GA * n
        if len(out) == 2:
            return 50 + SC * n
        return max(64, plain) * CY

    def ts(out, in0, s1, o1, s2=None, o2=None):
        n = _len(out)
        c = vcost(out, in0, n, n / 2 if len(in0) > 2 and two(out, in0) else n)
        if o2 is None:
            return add("v", lambda q: q.tensor_scalar(ap(out), ap(in0), sc(s1), None, o1), [out], [in0, s1], c)
        return add("v", lambda q: q.tensor_scalar(ap(out), ap(in0), sc(s1), sc(s2), o1, o2), [out], [in0, s1, s2], c)

    def lin(out, in0, m, c):
        return ts(out, in0, m, A.mult, c, A.add)

    def plus(out, in0, c):
        return ts(out, in0, c, A.add)

    def whole(out, d, m, c=0.0):
        return ts(out, d, K + c, A.add, float(m), A.mult)

    def bits(out, in0, shift, mask):
        if shift:
            return ts(out, in0, shift, A.logical_shift_right, mask, A.bitwise_and)
        return ts(out, in0, mask, A.bitwise_and)

    def tt(out, a, b, o):
        n = _len(out)
        return add("v", lambda q: q.tensor_tensor(ap(out), ap(a), ap(b), o), [out], [a, b], vcost(out, a, n, 2 * n))

    def cp(out, in0):
        n = _len(in0) if len(out) == 2 else _len(out)
        c = vcost(out, in0, n, n / 2 if len(in0) > 2 and len(out) > 2 and two(out, in0) else n)
        return add("v", lambda q: q.tensor_copy(ap(out), ap(in0)), [out], [in0], c)

    def ms(out, c):
        n = _len(out)
        return add("v", lambda q: q.memset(ap(out), c), [out], [], max(64, n / 2 if two(out) else n) * CY)

    def act(out, in0, scale=1.0, bias=0.0, fn=AF.Identity):
        n = _len(out)
        c = 65 + GA * n if len(in0) == 2 else max(64, n) * CY + FIX
        if fn == AF.Identity and scale == 1.0 and bias == 0.0:
            return add("s", lambda q: q.activation(ap(out), ap(in0), AF.Copy), [out], [in0], c)
        return add("s", lambda q: q.activation(ap(out), ap(in0), fn, bias=sc(bias), scale=scale), [out], [in0, bias], c)

    def get(eng, out, src, scale=1.0, bias=0.0):
        if eng == "s":
            return act(out, src, scale, bias)
        if scale == 1.0 and bias == 0.0:
            return cp(out, src)
        return lin(out, src, scale, bias)

    def share(out, win, lst, nv, scale=1.0, bias=0.0):
        for q, a, b in (("v", 0, nv), ("s", nv, _len(lst))):
            if a < b:
                get(q, sub(out, 16 * a, 16 * b), (win, sub(lst, a, b)), scale, bias)

    def scan(out, d0, d1, init, o0, o1):
        n = _len(out)
        return add("v", lambda q: q.tensor_tensor_scan(ap(out), ap(d0), ap(d1), init, o0, o1), [out], [d0, d1],
                   max(64, n / 2 if two(out, d0, d1) else n) * CY)

    def pairs(out, src):
        return scan(out, V("alt", 0, _len(src)), src, 0.0, A.mult, A.add)

    def deal(src, blk=16, pat=None):
        n = _len(src)
        o = new("sh" if two(src) else "so", n)
        scan(o, src, pat or V("c16" if blk == 16 else "c4", 0, n), -2 * K, A.max, A.add)
        return V(o[0], o[1] + blk - 1, o[2], blk)

    def iota(out, pat, base, ch=0):
        if SCRATCH[out[0]][2] == I32:
            return add("g", lambda q: q.iota(ap(out), pat, base, ch), [out], [], 170 + 2.6 * _len(out))
        return add("g", lambda q: q.iota(ap(out), pat, base, ch, allow_small_or_imprecise_dtypes=True), [out], [],
                   170 + 2.6 * _len(out))

    def fill(out, c):
        return iota(out, [[0, _len(out)]], c)

    def ramp(out, base, step=1.0):
        return act(out, V("rp", 0, _len(out)), float(step), float(base))

    def quant(q, s, a, b, src):
        o, p = V(q, a, b), V(s, a, b)
        return add("v", lambda e: e.quantize_mx(ap(o), ap(p), ap(src)), [o, p], [src], 13 + (b - a))

    def mm(bank, lq, ls, la, rq, rs, a, b):
        o, i = V("ps", 512 * bank, 512 * bank + b - a), [V(lq, la, la + 128), V(ls, la, la + 128), V(rq, a, b), V(rs, a, b)]
        add("t", lambda e: e.matmul_mx(ap(o), ap(i[0]), ap(i[1]), ap(i[2]), ap(i[3]), True, True), [o], i, (b - a + 16) * 0.6)
        return o

    def dma(eng, out, in_, outs, ins, lat, after=()):
        return add(eng, lambda e: e.dma_start(out, in_), outs, ins, 60, lat, "d", after)

    def u8(v):
        return ap(v).bitcast(dt.uint8) if SCRATCH[v[0]][2] == C4X else ap(v)

    count = {}

    def send(dst, out, in_, sem):
        assert topo.may_write(core, dst)
        rid, pid = topo.addr(dst)[:2]
        n = len(topo.engines(core, dst))
        count[sem] = count.get(sem, 0) + n
        count["sent"] = count.get("sent", 0) + n
        return add("g", lambda e: e.remote_dma(u8(out), u8(in_), T.sem[sem], T.sem["sent"], pid, rid, topo.mask(core, dst)),
                   [], [in_], 300 if count["sent"] > n else 1600, 0.0, "r")

    def arrive(sem, outs, sends, lat):
        i = add("a", None, outs, [], 0.0, lat, "a", sends)
        ops[i]["sem"] = (sem, count[sem])
        return i

    peer = [T.cores[rank ^ 1], T.cores[rank ^ 2]]

    dma("y", T.kw[:, 0:12], T.ka[:], [V("kw", 0, 12)], [], 1900)
    dma("s", T.kw[:, 12:24], T.kb[:], [V("kw", 12, 24)], [], 1900)
    dma("y", T.uin[:], T.u[:], [V("uin", 0, 512)], [], 2700)
    dma("y", T.xin[:, 768:1536], T.x[:, 768:1536], [V("xin", 768, 1536)], [], 3400)
    xl = dma("y", T.xin[:, 0:768], T.x[:, 0:768], [V("xin", 0, 768)], [], 4100)
    dma("y", T.wq[:].bitcast(dt.uint8), T.wc[:], [V("wq", 0, 512)], [], 3000, [xl])
    dma("y", T.wsc[:], T.ws[:], [V("wsc", 0, 512)], [], 3300, [xl])
    dma("y", T.vin[:], T.v[:], [V("vin", 0, 512)], [], 3800, [xl])

    pi, pc = V("csi", 0, 1), V("cst", 0, 8)
    first = iota(V("rp", 0, 112), [[1, 112]], 0)
    behind(iota(pi, [[1, 1]], 0, 1), first)
    bits(V("csi", 2, 3), pi, 0, 15)
    bits(V("csi", 3, 4), pi, 2, 3)
    bits(V("csi", 4, 5), pi, 0, 3)
    cp(V("cst", 0, 3), V("csi", 2, 5))
    p16, p4, pt, pk, ptk, ptj, pb, p32 = [sub(pc, i, i + 1) for i in range(8)]
    ptf = V("cst", 176, 177)
    for out, src, m, c in ((ptk, pt, 1, 4 * K + 4 * NL), (ptj, pt, 1, 8 * K + 4 * NL), (pb, pt, 2, 1), (p32, p16, 2, 0), (pk, p16, 1, K),
                           (ptf, pt, -NN, 2 * M)):
        lin(out, src, float(m), float(c))
    jp, j16, j4 = V("csi", 16, 48), V("cst", 8, 40), V("cst", 40, 72)
    iota(jp, [[1, 2], [1, 16]], 128, -1)
    bits(jp, jp, 0, 15)
    ts(j16, jp, 0.0, A.is_equal, K, A.mult)
    tt(V("c16", 0, 15), sub(j16, 0, 15), sub(j16, 16, 31), A.subtract)
    plus(V("c16", 15, 16), sub(j16, 15, 16), -2 * K)
    iota(j4, [[1, 2], [0, 4], [1, 4]], 0)
    ts(j4, j4, p4, A.is_equal, K, A.mult)
    tt(V("c4", 0, 16), sub(j4, 0, 16), sub(j4, 16, 32), A.subtract)
    plus(V("c4", 3, 16, 4), V("c4", 3, 16, 4), -2 * K)
    for c in ("c16", "c4"):
        for n, top in ((16, 64), (64, NL)):
            for a in range(n, top, n):
                cp(V(c, a, a + n), V(c, 0, n))
    cp(V("c16", NL, NN), V("c16", 0, NL))
    own, kidc, tsp = V("cst", 104, 128), V("cst", 128, 140), V("cst", 152, 176)
    for out, pat, base, p in ((own, [[SB, 2], [16, 12]], NL, p16), (kidc, [[16, 12]], NB, p16), (tsp, [[32, 24]], -int(K), p32)):
        iota(out, pat, base)
        plus(out, out, p)
    for a in (112, 224):
        ramp(V("rp", a, 2 * a), a)
    ramp(V("slot", 0, NL), -NL)
    ramp(V("slot", NL, NN), SB - NL)
    ramp(V("zz", NL + 1, 640), NL + 1 - NN)
    ms(V("zz", NL, NL + 1), -256.0)
    ms(V("tb", 0, NB), 0.0)
    ms(V("tb", NT - 1, NT), 0.0)
    for k in range(9):
        if k == 8:
            ramp(V("w", 512 * k, 512 * k + 128), 0.0, 0.5)
        elif k < 2:
            ramp(V("w", 512 * k, 512 * k + 128), 2 ** k - 256)
        else:
            iota(V("w", 512 * k, 512 * k + 128), [[1, 128]], 2 ** k - 256)
    iota(V("csi", 8, 16), [[16, 8]], 0)
    ou = new("off", 8)
    cp(ou, V("csi", 8, 16))
    for name, a, b, c in (("fa", 0, NB, 0), ("fa", NI - 1, NI + NB, 0), ("ix", NL, SB, 2 * NT - 1), ("pos", NL, SB, 0),
                          ("ch", 0, NB, 0), ("ch", NI, NB + SB, 0), ("ch", NI + SB, 480, NB - 1), ("asz", 0, NB, 0),
                          ("bt", 0, NB, 0), ("bt", NI, NB + SB, 0), ("bt", NI + SB, 512 + NB, 0), ("f0", NN, 512, 0),
                          ("rm", 2 * NT, 4 * NT, 127)):
        fill(V(name, a, b), c)
    iota(V("id4", 0, NL), [[2, NL]], 0)
    iota(V("rm", 0, 2 * NT), [[0, 2], [1, NT]], -NI)
    iota(V("ab0", 192, 288), [[1, 96]], 0)
    iota(V("ta", 0, NT), [[1, NT // 4], [0, 4]], 0)
    iota(V("par", 0, NL), [[0, NL // 2], [-1, 2]], 1)
    iota(V("alt", 0, NN), [[0, NL], [1, 2]], 0)
    ramp(V("id1", 0, NL), 0.0, 1 / 1024.0)
    cp(V("cj", 0, 96), V("c16", 0, 96))
    tt(V("cj", 15, 96, 16), V("c16", 15, 96, 16), V("rp", 0, 96, 16), A.add)
    ms(V("z", 0, 520), 0.0)
    ms(V("one", 0, 128), 1.0)
    add("g", lambda q: q.affine_select(T.z[:, 4:516:4], T.one[:], [[-1, 128]], A.is_equal, 0.0, 0, 1),
        [V("z", 4, 516, 4)], [V("one", 0, 128)], 550)
    for b in range(4):
        quant("eq", "es", 128 * b, 128 * b + 128, V("z", 4 - b, 516 - b))

    kw = V("kw", 0, 24)
    oc = new("off", 24)
    plus(oc, kw, float(NB))
    m_, t_, y_, oz = new("sm", 24), new("sm", 24), new("sm", 24), new("off", 24)
    ts(m_, kw, float(NL), A.is_ge, float(SB + NL), A.mult)
    tt(t_, kw, m_, A.add)
    tt(y_, t_, own, A.max)
    first = [plus(sub(oz, 12, 24), sub(y_, 12, 24), -float(NL + SB)), plus(sub(oz, 0, 12), sub(y_, 0, 12), -float(NL))]
    behind(cp((V("tb", 0, NT - 1), oc), V("slot", 0, NN)), first[0])
    act(V("zz", 0, NL), (V("zz", SB, 640), sub(oz, 12, 24)))
    act(V("w", 320, 512), (V("zz", 0, 640), sub(oz, 0, 12)))
    osl = new("off", 24)
    oin, olf = sub(osl, 0, 12), sub(osl, 12, 24)
    plus(oin, deal(V("tb", NI, NT)), K + NL)
    share(V("w", 128, 320), V("zz", 0, 448), oin, ON["x0"])
    dlf, ilf, plf = deal(V("tb", NB, NI)), new("si", 12), new("si", 12)
    plus(olf, dlf, K + NL)
    plus(ilf, dlf, K + NL)
    bits(plf, ilf, 0, 255)
    cp(V("lpo", 0, 12), plf)
    for h in range(2):
        act(V("ch", NB + SB * h, NI + SB * h), (V("rp", 0, NT), sub(oc, 12 * h, 12 * h + 12)))

    quant("uq", "us", 0, 128, V("uin", 0, 512))
    add("v", lambda q: q.tensor_copy(T.uq2[:].bitcast(dt.uint32), T.uq[:].bitcast(dt.uint32).indirect(ap(ou))),
        [V("uq2", 0, 128)], [V("uq", 0, 128), ou], 50 + 128 * GA)
    add("s", lambda q: q.activation(T.us2[:], T.us[:].indirect(ap(ou)), AF.Copy),
        [V("us2", 0, 128)], [V("us", 0, 128), ou], 65 + 128 * GA)
    quant("q0", "s0", NL, NN, V("xin", 768, 1536))
    p0 = mm(4, "uq2", "us2", 0, "q0", "s0", NL, NN)
    quant("q0", "s0", 0, NL, V("xin", 0, 768))
    lq, ls = V("lq", 48, 48 + NN), V("ls", 48, 48 + NN)
    arrive("ax", [lq, ls], [send(peer[0], lq, V("q0", 0, NN), "ax"), send(peer[0], ls, V("s0", 0, NN), "ax")], 9000)
    arrive("ap", [V("lp", 0, 12)], [send(peer[0], V("lp", 0, 12), V("lpo", 0, 12), "ap")], 6000)
    quant("vq", "vs", 0, 128, V("vin", 0, 512))

    def unpack(q, s, *outs):
        for b in range(4):
            o = mm(b, "eq", "es", 128 * b, q, s, 0, NN)
            for dst, scale in outs:
                act(V(dst, b, 1536, 4), o, scale)

    unpack("q0", "s0", ("xa", 1.0))
    ts(V("fa", NB, NI - 1), sub(p0, 0, NL - 1), 0.0, A.is_gt, float(NT), A.mult)
    pieces = [(a, a + ON["sp"]) for a in range(0, 12, ON["sp"])]
    dfa, ni, oi = deal(V("fa", NB, NI)), new("sm", 24), new("off", 24)
    iota(V("rp", 448, 2 * NT), [[1, 2 * NT - 448]], 448)
    tt(sub(ni, 0, 12), sub(kw, 0, 12), dfa, A.add)
    tt(sub(ni, 12, 24), sub(kw, 12, 24), dfa, A.subtract)
    plus(sub(oi, 0, 12), sub(ni, 0, 12), K + NB)
    plus(sub(oi, 12, 24), sub(ni, 12, 24), NT + NB - K)
    act(V("ix", SB, SB + NL), (V("rp", 0, 2 * NT), sub(oi, 0, 12)))
    act(V("ix", 0, NL), (V("rp", 0, 2 * NT), sub(oi, 12, 24)))
    osx = new("off", 24)
    for h in range(2):
        get(ON["sx"][h], V("sx", NL * h, NL * h + NL), (V("ix", 0, 448), sub(osl, 12 * h, 12 * h + 12)))
        plus(sub(osx, 12 * h, 12 * h + 12), deal(V("sx", NL * h, NL * h + NL)), K)
    szw = V("sz", 0, 2 * NT)
    act(V("sz", NT, 2 * NT), V("tb", 0, NT), 1 / 2048.0, NI / 2048.0 - 1)
    get(ON["sz"][0], V("sz", 0, NI), V("tb", 0, NI), 1 / 2048.0, NI / 2048.0 + 0.25)
    get(ON["sz"][1], V("sz", NI, NT), V("tb", NI, NT), 1 / 2048.0, NI / 2048.0 + 0.75)
    for a, b in pieces:
        ops[tt(V("pay0", 16 * a, 16 * b), (szw, sub(osx, 12 + a, 12 + b)), V("id4", 16 * a, 16 * b), A.add)]["l"] = 300
    for b in range(4):
        o, a = mm(4 + b, "eq", "es", 128 * b, "lq", "ls", 48, 48 + NN), NN * b
        act(V("fi", a, a + NN, 2), sub(o, 0, NL), 0.5)
        act(V("th", NL * b, NL * b + NL), sub(o, NL, NN), 0.5)
        act(V("fi", a + 1, a + NN, 2), (V("th", NL * b, NL * b + NL), V("lp", 0, 12)))
        pairs(V("fo", a + 15, a + 15 + NN), V("fi", a, a + NN))

    op = None
    parts = list(zip(ON["jc"], ON["jc"][1:]))[::-1]
    for k in range(8):
        win, op = V("w", 512 * k, 512 * k + 512), new("off", 24)
        for a, b in parts:
            plus(sub(op, a, b), deal(V("w", 512 * k + 128 + 16 * a, 512 * k + 128 + 16 * b)), K + 256)
        for a, b in parts:
            get("s" if a else "v", V("w", 512 * k + 640 + 16 * a, 512 * k + 640 + 16 * b), (win, sub(op, a, b)), 0.5 if k == 7 else 1.0)
    win = V("w", 512 * 8, 512 * 9)
    oex, oen = sub(op, 0, 12), sub(op, 12, 24)
    tt(V("een", 0, NL), (win, oen), V("sz", NI, NT), A.subtract)
    tt(V("sz", NI, NT), (win, oex), V("een", 0, NL), A.subtract)
    act(V("pos", 0, NL), (win, oen), 2.0)
    act(V("pos", SB, SB + NL), (win, oex), 2.0, -1.0)
    opos = new("off", 24)
    den, dex = deal(V("pos", 0, NL)), deal(V("pos", SB, SB + NL))
    plus(sub(opos, 0, 12), den, K + 256)
    plus(sub(opos, 12, 24), dex, K + 257)
    act(V("pay", 0, NL), (szw, sub(osx, 0, 12)), 1.0, 1.0)
    share(V("pay", NL, NN), szw, sub(osx, 0, 12), ON["pv"], -1.0, -1.0)
    cp((V("sc", 0, NN), opos), V("pay", 0, NN))
    act(V("ol", 0, NL), (szw, sub(osx, 12, 24)), 1.0, 1 - M)
    act(V("lqr", 0, NL), (V("pos", 0, 448), olf))
    olq = new("off", 12)
    plus(olq, deal(V("lqr", 0, NL)), K + 256)
    scan(V("ss", 0, NN), V("sc", 0, NN), V("c16", 0, NN), M, A.add, A.max)
    tt(V("num", 0, NL), (V("ss", 0, NN), olq), V("ol", 0, NL), A.add)
    onum = new("off", 12)
    plus(onum, deal(V("num", 0, NL)), K)
    cp((V("sort0", 0, NL), onum), V("pay0", 0, NL))

    step = {}

    def rake(r, sort, m, x):
        n, c, e = m // 2, m // 32, m // 8
        c2 = c + c % 2
        n2, ab, ih = 16 * c2, "ab%d" % r, "ih%d" % r
        part = [V(ab, n2 * i, n2 * i + n2) for i in range(11)]
        col = lambda v, i, k=1: sub(v, c2 * i, c2 * (i + k))
        i0, o0 = V("si", 0, 16) if r else new("si", 4 * c2), new("off", 3 * c2)
        if r == 0:
            whole(col(i0, 0), deal(V(sort, 1, m, 2)), 2048, 1.0)
            behind(len(ops) - 2, step["list"])
            bits(col(i0, 1), col(i0, 0), 0, 511)
            bits(col(i0, 2), col(i0, 0), 0, 255)
            bits(col(i0, 3), col(i0, 0), 9, 1)
        else:
            other = new("sm", c2)
            whole(sub(i0, 0, c), deal(V(sort, 1, m, 2)), 1024)
            bits(col(i0, 2), col(i0, 0), 12, 255)
            bits(col(i0, 3), col(i0, 0), 8, 1)
            lin(other, col(i0, 3), -float(SB), float(SB))
            tt(col(i0, 1), col(i0, 2), other, A.add)
        cp(col(o0, 0, 2), col(i0, 1, 2))
        osib, opar = col(o0, 0), col(o0, 1)
        act(part[0], (V("tb", NL, NT), opar))
        act(part[1], (V("ch", 0, 480), osib), 1.0, -float(NI))
        if r == 0:
            plus(col(o0, 2), col(i0, 2), 2.0 * NT)
            cp((V("rm", NL, 3 * NT), col(o0, 1, 2)), V(ab, n, 3 * n))
        else:
            for h in range(2):
                cp((V("rm", NL + 2 * NT * h, NT + 2 * NT * h), sub(opar, 0, c)), sub(part[1 + h], 0, n))
        i1, o1, ra = new("si", 5 * c2), new("off", 5 * c2), new("sm", 2 * c2)
        plus(col(i1, 0, 2), deal(V(ab, 0, 2 * n2)), K + NL)
        if r == 0:
            right = col(i0, 3)
        else:
            act(part[3], (V("fa", 0, NI + NB), opar), fn=AF.Sign)
            act(part[4], (V("ft1", 0, NI + NB), opar))
            d1, r1, right = deal(V(ab, 3 * n2, 5 * n2)), new("sm", c2), new("sm", c2)
            tt(r1, col(d1, 0), col(d1, 1), A.not_equal)
            tt(right, r1, col(i0, 3), A.not_equal)
        lin(col(ra, 0), right, float(NT), float(NL))
        lin(col(ra, 1), right, -float(NT), float(NT))
        bits(col(i1, 2), col(i1, 0), 0, 255)
        tt(col(i1, 3), col(i1, 2), col(ra, 0), A.add)
        tt(col(i1, 4), col(i1, 1), col(ra, 1), A.add)
        plus(o1, i1, float(NB))
        ots = new("off", e)
        lin(ots, deal(sub(part[1], 0, n), 4), 4.0, ptk)
        act(V(ih, 0, 8 * n, 2), (V(x, 0, 1536), ots))
        who, num = V("rm", 0, 2 * NT), V("rm", 2 * NT, 4 * NT)

        def mark(out, src, shift):
            if ON["mk"][r] == "s":
                act(part[10], src, -1.0, 126.5, AF.Sign)
                act(out, part[10], shift / 2, shift / 2)
            else:
                ts(out, src, 126.5, A.is_lt, float(shift), A.mult)

        af, g_, ob = V("af%d" % r, 0, n2), new("sm", e), new("off", e)
        act(af, (num, col(o1, 4)), 8.0, pb)
        tt(g_, deal(sub(af, 0, n), 4), sub(tsp, 0, e), A.min)
        plus(ob, g_, K)
        act(part[6], (who, col(o1, 4)))
        mark(part[7], (num, col(o1, 3)), NN)
        d = deal(V(ab, 6 * n2, 8 * n2), 4)
        tg, otg = new("sm", e), new("off", e)
        tt(tg, sub(d, 0, e), sub(d, 4 * c2, 4 * c2 + e), A.add)
        lin(otg, tg, 4.0, ptj)
        sv = V("af%d" % r, n2, 2 * n2)
        act(sv, (who, col(o1, 1)), 1.0, float(NI))
        cp((V("ch", 0, 480), sub(o1, 0, c)), sub(sv, 0, n))
        if r == 0:
            mark(part[8], (V("rm", 2 * NT + NL, 3 * NT), col(o1, 2)), NT)
            act(part[9], sv, 1.0, -float(NI))
            d = deal(V(ab, 8 * n2, 10 * n2))
            st, ost = new("sm", c), new("off", c)
            tt(st, sub(d, c, 2 * c), sub(d, 0, c), A.add)
            plus(ost, st, 2 * K + NI)
            step["slots"] = cp((V("tb", 0, 2 * NT), ost), part[0])
        return ob, otg

    def layer(r, gq, gs, n, lists, x):
        ih, vb = "ih%d" % r, V("vb%d" % r, 0, 4 * n)
        for b in range(4):
            o = mm(4 + b, "wq", "wsc", 128 * b, gq, gs, 0, 128)
            o, dst = V("ps", o[1], o[1] + n), V(ih, 2 * b + 1, 8 * n, 8)
            if ON["relu"][b] == "v":
                ts(dst, o, 0.0, A.max, 0.03125, A.mult)
            else:
                act(dst, o, 0.03125, fn=AF.Relu)
        for a, b in ((0, n // 8), (n // 8, n // 4)):
            pairs(V(ih, 8 * n + 32 * a, 8 * n + 32 * b), V(ih, 32 * a, 32 * b))
            tt(sub(vb, 16 * a, 16 * b), (V(ih, 8 * n, 8 * n + 32 * b), sub(lists[0], a, b)), V(ih, 32 * a + 1, 32 * b, 2), A.add)
        cp((V(x, 0, 3072), lists[1]), vb)

    lst0, ll = V("lst0", 0, 24), V("ll", 0, 24)
    step["list"] = ts(lst0, deal(V("sort0", 1, NL, 2), 4), 2 * M + K, A.add, ptf, A.subtract) - 1
    sl = send(peer[0], ll, lst0, "al")
    arrive("al", [ll], [sl], 2000)
    for name, a, b, c in (("zero", 0, NN, 0), ("ft1", 0, NB, 0), ("ft1", NI - 1, NI + NB, 0), ("si", 0, 16, 0), ("f1", NL, 512, 0),
                          ("ch", 480, 976, NB - 1)):
        behind(fill(V(name, a, b), c), sl)
    behind(iota(V("ab1", 128, 192), [[1, 64]], 0), sl)
    behind(iota(V("pt1", 0, 512), [[1, 2], [16, SB]], 16 * NB), sl)
    lists0 = rake(0, "sort0", NL, "xa")
    act(V("lo", 0, NL), (V("ss", 0, NN), sub(opos, 0, 12)), 1.0, -M)
    l2, l3, dd, yy, oa = new("si", 12), new("si", 12), new("sm", 12), new("sm", 12), new("off", 12)
    whole(l2, deal(V("lo", 0, NL)), 2)
    bits(l3, l2, 0, 2)
    tt(dd, dex, den, A.subtract)
    tt(yy, dd, l3, A.subtract)
    plus(oa, yy, 6.0)
    act(V("asz", NI, NT), (V("ta", 0, NT), oa))
    act(V("asz", NB, NI), (V("par", 0, NL), onum))
    for h in range(2):
        act(V("bt", NB + SB * h, NI + SB * h), (V("asz", 0, NT), sub(oc, 12 * h, 12 * h + 12)))
    get(ON["bt"], V("bt", 512 + NB, 512 + NI + SB), V("bt", NB, NI + SB), -1.0)
    dt_ = deal(V("sc", 0, NN))
    aa, sg, it, ib, ofb = new("sm", 24), new("sm", 24), new("si", 30), new("si", 66), new("off", 66)
    act(aa, dt_, 2048.0, 2048.0 * K, AF.Abs)
    ts(sg, dt_, -K, A.is_lt, 512.0, A.mult)
    tt(sub(it, 0, 24), aa, sg, A.add)
    whole(sub(it, 24, 30), deal(V("sort0", 0, NL, 2)), 2048, 1.0)
    bits(sub(ib, 0, 30), it, 0, 1023)
    bits(sub(ib, 30, 60), it, 0, 255)
    bits(sub(ib, 60, 66), sub(it, 24, 30), 12, 255)
    cp(ofb, ib)
    oal, olp, osn = sub(ofb, 60, 66), new("off", 6), new("off", 6)
    act(V("b1", 0, 480), (V("bt", 0, 512 + NI + SB), sub(ofb, 0, 30)))
    act(V("lp1", 0, 96), (V("lqr", 0, NL), oal))
    plus(olp, deal(V("lp1", 0, 96)), K + 256)
    act(V("s1n", 0, 96), (V("tb", NB, NI), oal))
    plus(osn, deal(V("s1n", 0, 96)), K + NL)
    act(V("p1s", 0, 96), (V("pt1", 0, 512), osn), 0.25, pt)
    tt(V("pay1", 0, 96), (V("id1", 0, NL), oal), V("p1s", 0, 96), A.add)
    share(V("f0", 0, NN), V("fo", 16, 1551), ll, ON["fv"])
    quant("fq0", "fs0", 0, 128, V("f0", 0, 512))
    layer(0, "fq0", "fs0", 96, lists0, "xa")

    quant("q1", "s1", NL, NN, V("xa", 768, 1536))
    p1 = mm(4, "uq2", "us2", 0, "q1", "s1", NL, NN)
    turn = ts(V("ft1", NB, NI - 1), sub(p1, 0, NL - 1), 0.0, A.is_gt)
    behind(quant("q1", "s1", 0, NL, V("xa", 0, 768)), turn)
    behind(turn, step["slots"])
    unpack("q1", "s1", ("xh", 0.5), ("xb", 1.0))
    for a, b in ((0, 24), (24, 30)):
        tt(V("g1", 16 * a, 16 * b), (V("ft1", 0, NI + NB), sub(ofb, 30 + a, 30 + b)), V("b1", 16 * a, 16 * b), A.mult)
    scan(V("ss1", 0, NN), V("g1", 0, NN), V("zero", 0, NN), 0.0, A.add, A.add)
    tt(V("num1", 0, 96), (V("ss1", 0, NN), olp), V("g1", NN, 480), A.add)
    on1 = new("off", 6)
    plus(on1, deal(V("num1", 0, 96), 16, V("cj", 0, 96)), pk)
    cp((V("sort1", 0, 96), on1), V("pay1", 0, 96))
    d, i4, l4, lst1 = deal(V("sort1", 1, 96, 2), 4), new("si", 12), new("si", 12), new("off", 24)
    ts(sub(lst1, 12, 24), d, M + K, A.add, M, A.subtract)
    whole(i4, d, 1024)
    bits(l4, i4, 0, 255)
    lin(sub(lst1, 0, 12), l4, 4.0, pt)
    for a, b in zip(ON["c1"], ON["c1"][1:]):
        act(V("fp1", 16 * a, 16 * b), (V("xh", 4 * (NL - NB), 1536), sub(lst1, 12 + a, 12 + b)))
        tt(V("f1", 16 * a, 16 * b), (V("xh", 0, 768), sub(lst1, a, b)), V("fp1", 16 * a, 16 * b), A.add)
    quant("fq1", "fs1", 0, 128, V("f1", 0, 512))
    gq, gs = V("lq", 0, 48), V("ls", 0, 48)
    arrive("ag", [gq, gs], [send(peer[1], gq, V("fq1", 0, 48), "ag"), send(peer[1], gs, V("fs1", 0, 48), "ag")], 2800)
    lists1 = rake(1, "sort1", 96, "xb")
    f0d, fxd, i1, i2, i3, ok = new("sm", 12), new("sm", 12), new("sm", 12), new("sm", 12), new("sm", 24), new("off", 24)
    ts(f0d, dfa, 1 - K, A.min)
    tt(fxd, deal(V("ft1", NB, NI)), f0d, A.not_equal)
    ts(i1, fxd, float(SB), A.mult)
    ts(V("gone", 0, NL), V("rm", 2 * NT + NI, 3 * NT), 126.5, A.is_lt, 2.0 * SB, A.mult)
    tt(i2, deal(V("gone", 0, NL)), kidc, A.add)
    tt(sub(i3, 0, 12), i2, i1, A.add)
    tt(sub(i3, 12, 24), i2, i1, A.subtract)
    plus(sub(ok, 0, 12), sub(i3, 0, 12), K)
    plus(sub(ok, 12, 24), sub(i3, 12, 24), K + SB)
    act(V("kido", 0, NN), (V("ch", 0, 976), ok), 1.0, -float(NB))
    dma("y", T.kid[:], T.kido[0:128:16, :], [], [V("kido", 0, NN)], 1600)
    layer(1, "lq", "ls", 48, lists1, "xb")

    for h in range(2):
        a, b = (0, ON["cut"], NN)[h:h + 2]
        quant("q2", "s2", a, b, V("xb", 4 * a, 4 * b))
        get(ON["y"][h], V("yo", a, b), mm(h, "vq", "vs", 0, "q2", "s2", a, b))
    dma("y", T.oc[:], T.q2[:].bitcast(dt.uint8), [], [V("q2", 0, NN)], 2600)
    for k in range(4):
        dma("y", T.osc[4 * k:4 * k + 4, :], T.s2[32 * k:32 * k + 4, :], [], [V("s2", 0, NN)], 2300)
    dma("s", T.y[:], T.yo[:], [], [V("yo", 0, NN)], 2400)
    return ops, count


_ORDER = []


def arrange(ops):
    if _ORDER:
        return _ORDER
    n = len(ops)
    calls = range(n)
    before, after, behind = [], [[] for o in ops], []
    for i, o in enumerate(ops):
        seen, near = set(), []
        for j in sorted(o["d"] | o["o"], reverse=True):
            if j not in seen:
                way = WAKE if j in o["d"] else 0.0
                near.append((j, way))
                after[j].append((i, way))
                seen |= behind[j] | {j}
        before.append(near)
        behind.append(seen)
    queue, cost, lat, none = [o["e"] for o in ops], [o["c"] for o in ops], [o["l"] for o in ops], [0.0] * n

    queues = sorted(set(queue))

    def pack(key, follows, first, then):
        start, done, busy = [0.0] * n, [0.0] * n, {q: ([], []) for q in queues}
        for t, i in sorted(zip(key, calls), reverse=True):
            t = 0.0
            for j, way in follows[i]:
                if done[j] + way > t:
                    t = done[j] + way
            t += first[i]
            (a, b), c = busy[queue[i]], cost[i]
            k = m = len(a)
            while k and b[k - 1] > t:
                k -= 1
            while k < m and t + c > a[k]:
                if b[k] > t:
                    t = b[k]
                k += 1
            a.insert(k, t)
            b.insert(k, t + c)
            start[i], done[i] = t, t + c + then[i] + 0.001
        return start, done

    def settle(key, both):
        for i in calls:
            for j, way in before[i]:
                if key[i] >= key[j]:
                    key[i] = key[j] - 0.01
        start, done = pack(key, before, none, lat)
        if both:
            back = pack(done, after, lat, none)[1]
            again, end = pack(back, before, none, lat)
            if max(end) <= max(done):
                return max(end), again, back
        return max(done), start, key

    seed = [SEED]

    def draw():
        seed[0] = seed[0] * 48271 % 2147483647
        return seed[0] / 2147483647.0

    tail = [0.0] * n
    for i in reversed(calls):
        tail[i] += cost[i] + lat[i] + WAKE
        for j, way in before[i]:
            tail[j] = max(tail[j], tail[i])
    best = now = settle(tail, True)
    for k in range(TRIES):
        keys = now[2] if draw() < 0.5 else [now[0] - t for t in now[1]]
        mid, wide, part = draw() * now[0], 800 * 2 ** int(4 * draw()), draw() ** 2
        got = settle([t + 4000 * (draw() - 0.5) * draw() if abs(t - mid) < wide and draw() < part else t for t in keys], draw() < 0.6)
        if got[0] <= now[0] - (35 - 30.0 * k / TRIES) * math.log(draw()):
            now = got
        if got[0] < best[0]:
            best = got
    _ORDER.extend(sorted(calls, key=lambda k: (best[1][k], k)))
    return _ORDER


def rank_program(g, core, T, topo):
    rank = T.rank_of(core)
    if rank is None:
        return
    ops, count = build(T, topo, core, rank)
    order = list(arrange(ops))
    spots = [k for k, i in enumerate(order) if ops[i]["k"] == "d" and ops[i]["e"] == "y" and not ops[i]["r"]]
    for k, i in zip(spots, sorted(order[k] for k in spots)):
        order[k] = i
    place = {i: k for k, i in enumerate(order)}
    assert all(place[j] < place[i] for i, o in enumerate(ops) for j in o["d"])
    queue = {"v": g.vector, "s": g.scalar, "t": g.tensor, "y": g.sync, "g": g}
    known = {e: set() for e in queue}
    saw, waits, needed = {}, {}, set()
    for i in order:
        o = ops[i]
        if o["k"] == "a":
            saw[i] = set()
            continue
        k, ws = known[o["e"]], []
        for j in sorted(o["d"], key=lambda q: -place[q]):
            if j not in k and ops[j]["k"] != "r":
                ws.append(j)
                k.add(j)
                k |= saw[j]
        waits[i] = ws
        needed |= set(ws)
        saw[i] = set(k)
    tail = [i for i in order if ops[i]["k"] == "d" and i not in needed]
    needed |= set(tail)
    last, total, sem = [], [], {}
    for i in order:
        o = ops[i]
        if o["k"] == "a":
            sem[i] = o["sem"]
            continue
        q = queue[o["e"]]
        for j in waits[i]:
            q.wait_ge(T.sem[sem[j][0]], sem[j][1])
        call = o["f"](q)
        if i in needed:
            step = 16 if o["k"] == "d" else 1
            free = [s for s in range(len(last)) if step == 1 and last[s] in saw[i] and ops[last[s]]["e"] == o["e"] and ops[last[s]]["k"] == "c"]
            if free:
                s = free[0]
            else:
                s = len(last)
                last.append(i)
                total.append(0)
            last[s] = i
            total[s] += step
            sem[i] = ("e%d" % s, total[s])
            call.then_inc(T.sem[sem[i][0]], step)
    for i in tail:
        g.wait_ge(T.sem[sem[i][0]], sem[i][1])
    g.wait_ge(T.sem["sent"], count["sent"])
